import numpy as np, ml_dtypes
CORES = [2,7,18,23,34]
N = 5
BF = ml_dtypes.bfloat16
def gentries(a):
    return np.ascontiguousarray(a.reshape(8, 16, -1).transpose(0, 2, 1)).reshape(8, -1)
def gtable(e):
    e = np.asarray(e); return np.ascontiguousarray(e.reshape(8, -1, 16).transpose(0, 2, 1)).reshape(128, -1).astype(np.int32)
C, K, A, V, S = 4096, 512, 2, 3, 3
L = V * S
E = (V - 1) * S
def rock(rng, big=False):
    Q = C // 4; o = np.argsort(rng.random((N, 8, C)), axis=-1)
    a = np.where(rng.random((N, 8, 16, Q)) < 0.25, rng.integers(1, 3, (N, 8, 16, Q)), 0); a[:, :, 0] = rng.integers(0, 3, (N, 8, Q)); a[..., :Q // 16] = 0
    lv = [a]; pp = [rng.integers(0, Q // 16, (N, 8, Q))]
    for i in range(1, 4):
        j = rng.integers(0, Q, (N, 8, Q)); up = np.where(rng.random((N, 8, 16, Q)) < 0.15, rng.integers(1, 3, (N, 8, 16, Q)), 0); up[:, :, 0] = rng.integers(0, 3, (N, 8, Q))
        if big: up = up * rng.choice(np.array([1, 1, 2, 4]), (N, 8, 1, Q))
        lv.append(np.minimum(7, np.take_along_axis(lv[-1], j[:, :, None, :], 3) + up)); pp.append(j + (i - 1) * Q)
    fp = np.concatenate(lv, axis=3); pp = np.concatenate(pp, axis=2); inv = np.argsort(o, axis=-1)
    fm = np.ascontiguousarray(np.take_along_axis(fp, inv[:, :, None, :], 3)); nx = rng.integers(0, C, (N, 8, 16, C))
    nx[:, :, 0] = np.take_along_axis(o, np.take_along_axis(pp, inv, 2), 2)
    return fm, nx
def melts(rng):
    b = np.where(rng.random((N, 8, 16, K)) < 0.1, rng.integers(0, 4, (N, 8, 16, K)), rng.integers(4, 44, (N, 8, 16, K))); b[:, :, 0] = rng.integers(0, 16, (N, 8, K))
    w = np.where(rng.random((N, 8, 16, A * K)) < 0.5, rng.integers(0, 9, (N, 8, 16, A * K)), 0); w[:, :, 0] = rng.integers(0, 9, (N, 8, A * K))
    return b, w, rng.integers(0, C, (N, 8, K))
def link(fm, nx, g, a, form, row, after, partner):
    fm[:, g, :, a] = form; nx[:, g, row, a] = after; nx[:, g, 0, a] = partner
def mend(fm, nx, zs):
    low = np.take_along_axis(fm, nx[:, :, :1], 3)
    nx[:, :, 0] = np.where(np.any(low > fm, axis=2), np.array(zs).reshape(1, 8, 1), nx[:, :, 0])
def pack(fm, nx, w, b, m):
    return {"fm": np.ascontiguousarray(fm.reshape(N, 128, C)).astype(BF), "nx": np.ascontiguousarray(nx.reshape(N, 128, C)).astype(np.int32), "wl": np.ascontiguousarray(w.reshape(N, 128, A * K)).astype(BF),
            "b0": np.ascontiguousarray(b.reshape(N, 128, K)).astype(BF), "m0": np.stack([gtable(a) for a in m])}
def setup_inputs(rng):
    fm, nx = rock(rng); b, w, m = melts(rng)
    return pack(fm, nx, w, b, m)
def setup_inputs_spread(rng):
    fm, nx = rock(rng, True); b, w, m = melts(rng)
    b = np.minimum(255, (np.exp2(8 * rng.random((N, 8, 1, K))) * rng.random((N, 8, 16, K))).astype(np.int64))
    b[:, :, 0] = np.minimum(255, (np.exp2(8 * rng.random((N, 8, K)) * rng.random((N, 8, K))) - 1).astype(np.int64))
    w = np.minimum(255, (np.exp2(8 * rng.random((N, 8, 1, A * K))) * rng.random((N, 8, 16, A * K)) * rng.random((N, 8, 16, A * K))).astype(np.int64)) * (rng.random((N, 8, 1, A * K)) > 0.125)
    return pack(fm, nx, w, b, m)
def setup_inputs_ends(rng):
    full = rng.random((N, 8, 1, C)) < 0.3
    fm = 7 * (full | (rng.random((N, 8, 16, C)) < 0.3)).astype(np.int64)
    nx = np.where(rng.random((N, 8, 16, C)) < 0.75, (C - 1) * rng.integers(0, 2, (N, 8, 16, C)), rng.integers(0, C, (N, 8, 16, C))); nx[:, :, 0] = (C - 1) * rng.integers(0, 2, (N, 8, C))
    style = rng.integers(0, 4, (N, 8, 1, K)); rich = (np.arange(16) > 0).astype(np.int64).reshape(1, 1, 16, 1)
    b = 255 * np.where(style == 0, 0, np.where(style == 1, 1, np.where(style == 2, rng.integers(0, 2, (N, 8, 16, K)), rich)))
    w = 255 * rng.integers(0, 2, (N, 8, 16, A * K))
    m = np.where(rng.random((N, 8, K)) < 0.7, (C - 1) * rng.integers(0, 2, (N, 8, K)), rng.integers(0, C, (N, 8, K)))
    form = 7 * rich.reshape(16); zs = []
    for g in range(8):
        ch = [C - 1 - 2 * i for i in range(E - 1)] + [C - 2, 1]; z = 0; h = 1; half = 2
        idle = [3 + i for i in range((V - 3) * S)]
        if g % 2 == 1:
            ch = [C - 1 - a for a in ch]; z = C - 1; h = C - 2; half = C - 3; idle = [C - 1 - a for a in idle]
        for i in range(E): link(fm, nx, g, ch[i], form, 15, ch[i + 1], z)
        link(fm, nx, g, z, np.zeros(16, np.int64), 15, rng.integers(0, C, N), z)
        link(fm, nx, g, h, np.full(16, 7), 15, z, z)
        link(fm, nx, g, half, 7 * (np.arange(16) > 7), 15, ch[0], z)
        nx[:, g, 0, ch[E - 1]] = half; zs.append(z)
        way = idle + [ch[E - S]]
        for i in range(len(idle)): link(fm, nx, g, way[i], np.full(16, 7), 15, z, way[i + 1])
        pk = rng.permutation(K)
        ks = np.unique(np.concatenate([np.array([0, K // 2, K - 1]), pk[:K // 4]]))
        kc = np.setdiff1d(pk[K // 4:K // 4 + K // 16], ks); ka = np.concatenate([ks, kc])
        b[:, g, 0, ka] = 0; b[:, g, 1:, ka] = 255; m[:, g, ks] = ch[0]; m[:, g, kc] = way[0]
        for j in range(A):
            w[:, g, 0, j * K + ka] = 0; w[:, g, 1:, j * K + ka] = 255
    mend(fm, nx, zs)
    return pack(fm, nx, w, b, m)
def setup_inputs_corners(rng):
    fm, nx = rock(rng); b, w, m = melts(rng)
    u = rng.random(nx.shape); nx = np.where(u < 0.04, np.arange(C), np.where(u < 0.08, 0, np.where(u < 0.12, C - 1, nx)))
    kind = rng.integers(0, 3, (N, 8, 1, A * K)); w = np.where(kind == 0, 0, np.where(kind == 1, 255, rng.integers(0, 256, (N, 8, 16, A * K)))); w[:, :, 0] = rng.integers(0, 2, (N, 8, A * K))
    cls = rng.integers(0, 6, (N, 8, K)); cls[:, 7] = 4; cls[:, 7, 0] = 5; cls[:, 6] = 0; cls[:, 5] = 1; cls[:, :, K - 1] = np.arange(8) % 6
    rich = (np.arange(16) > 0).astype(np.int64).reshape(1, 1, 16, 1); c4 = cls[:, :, None, :]
    b = np.where(c4 == 0, 255, np.where(c4 == 1, 0, np.where(c4 == 2, b, 255 * rich)))
    m[:, 4] = rng.integers(0, C, (N, 1)); m[:, 5] = rng.integers(0, C, (N, 1)); m[:, 3, ::2] = 0; m[:, 3, 1::2] = C - 1; zs = []
    for g in range(8):
        nm = [int(a) for a in rng.permutation(C)[:L + 1]]; z = nm[L]; h = nm[L - 1]
        for i in range(L - 1): link(fm, nx, g, nm[i], rich.reshape(16), 15, nm[i + 1], z)
        link(fm, nx, g, h, 7 * (np.arange(16) == 0), 15, nm[0], z)
        link(fm, nx, g, z, np.zeros(16, np.int64), 15, rng.integers(0, C, N), z)
        zs.append(z); m[:, g] = np.where(cls[:, g] == 4, nm[0], np.where(cls[:, g] == 5, nm[1], m[:, g]))
    mend(fm, nx, zs)
    return pack(fm, nx, w, b, m)
def setup_inputs_calm(rng):
    fm, nx = rock(rng); b, w, m = melts(rng); w[:, :, 0] = rng.integers(0, 2, (N, 8, A * K)); zs = []
    part = rng.random((N, 8, K)); part[:, :, 0] = 0.0; part[:, :, K - 1] = 0.0
    still = rng.integers(20, 61, (N, 8, 16, K)); still[:, :, 0] = 0; still[:, :, 5] = 0
    b = np.where((part < 0.8)[:, :, None, :], still, b); r16 = np.arange(16)
    for g in range(8):
        j = g % 4; nm = [int(a) for a in rng.permutation(C)[:E + 3]]; h, q, z = nm[E], nm[E + 1], nm[E + 2]
        for i in range(E):
            if i < E - j: link(fm, nx, g, nm[i], 3 * (r16 == 5), 5, nm[i + 1], z)
            else: link(fm, nx, g, nm[i], ((r16 != 0) & (r16 != 5)).astype(np.int64), 15, nm[i + 1], z)
        link(fm, nx, g, h, 7 * (r16 == 0), 15, nm[0], q)
        link(fm, nx, g, q, 3 * (r16 == 0), 15, nm[0], z)
        link(fm, nx, g, z, np.zeros(16, np.int64), 15, rng.integers(0, C, N), z)
        zs.append(z); any_ = np.array(nm)[rng.integers(0, E + 1, (N, K))]
        m[:, g] = np.where(part[:, g] < 0.6, nm[0], np.where(part[:, g] < 0.8, any_, m[:, g]))
    mend(fm, nx, zs)
    return pack(fm, nx, w, b, m)
def check_inputs(d):
    bad = []
    for k, lo, hi in (("fm", 0, 7), ("nx", 0, C - 1), ("wl", 0, 255), ("b0", 0, 255), ("m0", 0, C - 1)):
        v = np.asarray(d[k]).astype(np.float64)
        if not (np.min(v) >= lo and np.max(v) <= hi): bad.append("range of " + k)
        if np.any(v != np.floor(v)): bad.append("whole numbers of " + k)
    fm = np.asarray(d["fm"]).astype(np.float32).reshape(N, 8, 16, C); p0 = np.clip(np.asarray(d["nx"]).astype(np.int64).reshape(N, 8, 16, C)[:, :, :1], 0, C - 1)
    if np.any(np.take_along_axis(fm, p0, 3) > fm): bad.append("partners in nx that are richer than their minerals in fm")
    return bad
def at(a, ix):
    return np.take_along_axis(a, ix[:, :, None, :], 3)
def one(a, ix):
    return np.take_along_axis(a, ix[:, :, None, :], 2)[:, :, 0]
def reference(fm, nx, wl, b0, m0):
    F = fm.astype(np.int64).reshape(N, 8, 16, C); X = nx.astype(np.int64).reshape(N, 8, 16, C); wall = wl.astype(np.int64).reshape(N, 8, 16, A * K)
    B = b0.astype(np.int64).reshape(N, 8, 16, K); m = np.stack([gentries(a) for a in m0]).astype(np.int64)
    lg = np.full((N, 8, L, K), -1, np.int64); n = np.zeros((N, 8, K), np.int64); c = np.full((N, 8, K), -1, np.int64)
    for v in range(V):
        if v > 0:
            B, m, lg, n, c = [np.roll(a, 1, axis=0) for a in (B, m, lg, n, c)]
            has = c >= 0; col = (one(lg, np.maximum(c, 0)) & (A - 1)) * K + np.arange(K)
            B = np.minimum(255, B + np.where(has[:, :, None, :], at(wall, col), 0))
            if v < V - 1:
                keep = np.ones((N, 8, A * K), np.int64); np.put_along_axis(keep, col, np.where(has, 0, 1), 2)
                wall = wall * keep[:, :, None, :]
        for s in range(S):
            f = at(F, m); short = B < f
            ok = ~np.any(short, axis=2); back = short[:, :, 0] & ~np.any(short[:, :, 1:], axis=2) & (c >= 0)
            B = B - np.where(ok[:, :, None, :], f, 0)
            low = B < f; p = np.where(np.any(low, axis=2), np.argmax(low, axis=2), 15)
            after = one(at(X, m), p)
            t = np.where(back, one(lg, np.maximum(c, 0)), m); pi = np.take_along_axis(X[:, :, 0], t, 2)
            B = B + np.where(back[:, :, None, :], at(F, t) - at(F, pi), 0)
            slot = np.where(ok, n, np.maximum(c, 0)); new = np.where(ok, m, np.where(back, pi, one(lg, slot)))
            np.put_along_axis(lg, slot[:, :, None, :], new[:, :, None, :], 2)
            c = np.where(ok, n, np.where(back, c - 1, c)); n = n + ok; m = np.where(back, m, after)
    return {"yb": B.reshape(N, 128, K).astype(np.float32), "yl": np.stack([gtable(a.reshape(8, L * K)) for a in lg]).astype(np.float32),
            "ym": np.stack([gtable(a) for a in m]).astype(np.float32), "yc": np.stack([gtable(a) for a in c]).astype(np.float32)}

@@ -1,0 +1,464 @@
+from concourse.mybir import AluOpType as A, ActivationFunctionType as AF
+
+C, K, V_, S_ = 4096, 512, 3, 3
+O = 16
+NH = 2
+OFF = 2064.0
+XCH = [0, 1280, 2560, 3584, 4096]
+
+SCRATCH = {
+    "G": ("sbuf", [128, C + O], "bfloat16"), "U": ("sbuf", [128, C + O], "bfloat16"),
+    "XI": ("sbuf", [128, C + O], "int32"), "XF": ("sbuf", [128, C + O], "float32"),
+    "WT": ("sbuf", [128, 2 * K + O], "bfloat16"), "B0": ("sbuf", [128, K], "bfloat16"),
+    "M0": ("sbuf", [128, 32], "int32"), "PL": ("sbuf", [128, 256], "int32"),
+    "PA": ("sbuf", [128, 256], "int32"), "PC": ("sbuf", [128, 256], "int32"),
+    "HI": ("sbuf", [128, 256], "bfloat16"), "LO": ("sbuf", [128, 256], "bfloat16"),
+    "J": ("sbuf", [128, 144], "float32"), "QI": ("sbuf", [128, 8], "int32"), "COL": ("sbuf", [128, 16], "float32"),
+    "TA": ("sbuf", [128, 128], "bfloat16"), "TC": ("sbuf", [128, 128], "bfloat16"),
+    "TD": ("sbuf", [128, 128], "bfloat16"), "TE": ("sbuf", [128, 128], "bfloat16"), "TF": ("sbuf", [128, 128], "bfloat16"),
+    "ZS": ("sbuf", [128, 128], "bfloat16"), "ZD": ("sbuf", [128, 128], "bfloat16"),
+    "ID": ("sbuf", [128, 128], "bfloat16"), "NI": ("sbuf", [128, 128], "bfloat16"),
+    "KO": ("sbuf", [128, 128], "bfloat16"), "PQ": ("sbuf", [128, 256], "float16"),
+    "WB": ("sbuf", [128, 144], "bfloat16"), "KC": ("sbuf", [128, 32], "float16"),
+    "SL": ("sbuf", [128, 288], "bfloat16"), "BI": ("sbuf", [128, 18], "int32"), "BL": ("sbuf", [128, 18], "uint16"),
+    "KI": ("sbuf", [128, 32], "int32"), "KK": ("sbuf", [128, 32], "float32"),
+    "F": ("sbuf", [128, K], "bfloat16"), "F2": ("sbuf", [128, K], "bfloat16"), "X": ("sbuf", [128, K], "float32"),
+    "R1": ("sbuf", [128, 2 * K], "bfloat16"), "D": ("sbuf", [128, K], "bfloat16"), "Y": ("sbuf", [128, K], "float16"),
+    "GA": ("sbuf", [128, 3 * K], "bfloat16"), "GB": ("sbuf", [128, 3 * K], "bfloat16"),
+    "BW": ("sbuf", [128, K], "bfloat16"), "EX": ("sbuf", [128, K], "bfloat16"),
+    "MT": ("sbuf", [128, 64], "int32"), "LS": ("sbuf", [128, 64], "uint16"),
+    "J1": ("sbuf", [128, 32], "uint16"), "J2": ("sbuf", [128, 32], "uint16"), "WL": ("sbuf", [128, 32], "uint16"),
+    "N": ("sbuf", [128, 32 * 16], "float32"), "CN": ("sbuf", [128, 96], "bfloat16"), "NI32": ("sbuf", [128, 96], "int32"),
+    "H": ("sbuf", [128, 288], "bfloat16"), "P": ("sbuf", [128, 288], "float32"), "PR": ("sbuf", [128, 288], "float32"),
+    "SB0": ("sbuf", [128, K], "bfloat16"), "SB1": ("sbuf", [128, K], "bfloat16"),
+    "RB0": ("sbuf", [128, K], "bfloat16"), "RB1": ("sbuf", [128, K], "bfloat16"),
+    "SA0": ("sbuf", [128, 256], "float16"), "SA1": ("sbuf", [128, 160], "float16"),
+    "RA0": ("sbuf", [128, 256], "float16"), "RA1": ("sbuf", [128, 160], "float16"),
+    "SL0": ("sbuf", [128, 64], "float16"), "RL0": ("sbuf", [128, 64], "float16"),
+    "SL1": ("sbuf", [128, 192], "float16"), "RL1": ("sbuf", [128, 192], "float16"),
+    "OB": ("sbuf", [128, K], "float32"), "OL": ("sbuf", [128, 288], "float32"), "OM": ("sbuf", [128, 32], "float32"),
+    "OC": ("sbuf", [128, 32], "float32"),
+}
+PSUM = ["PB0", "PB1", "Z0", "Z1", "T1", "TU", "T2", "LG"]
+for _n in PSUM:
+    SCRATCH[_n] = ("psum", [128, 512], "float32")
+SEMAPHORES = ["eV", "eS", "eP", "eG", "sent", "a0", "a1", "b0", "b1", "l0", "l1"] + ["d%d" % i for i in range(24)]
+
+
+def rank_program(g, core, T, topo):
+    rank = T.rank_of(core)
+    if rank is None:
+        return
+    n_ranks = len(T.cores)
+    nxt, prv = T.cores[(rank + 1) % n_ranks], T.cores[(rank - 1) % n_ranks]
+    rid, pid = topo.addr(nxt)[0], topo.addr(nxt)[1]
+    mask_out = topo.mask(core, nxt)
+    n_out, n_in = len(topo.engines(core, nxt)), len(topo.engines(prv, core))
+    Q = {"V": g.vector, "S": g.scalar, "P": g.tensor, "G": g, "Y": g.sync}
+    cnt = {"eV": 0, "eS": 0, "eP": 0, "eG": 0, "sent": 0}
+    known = {e: {} for e in list(Q) + ["dma"]}
+    acc = {}
+    ndma = [0]
+    ends = []
+
+    def ap(r):
+        if r[0] == "ind":
+            return ap(r[1]).indirect(ap(r[2]))
+        if len(r) == 4:
+            return T[r[0]][:, r[1]:r[2]:r[3]]
+        return T[r[0]][:, r[1]:r[2]]
+
+    def spans(rs):
+        out = []
+        for r in rs:
+            if not isinstance(r, tuple):
+                continue
+            if r[0] == "ind":
+                out += [r[1], r[2]]
+            else:
+                out.append(r)
+        return out
+
+    def order(e, reads, writes):
+        need = {}
+        for rs, w in ((reads, False), (writes, True)):
+            for r in spans(rs):
+                for lo, hi, pw, pe, tok, clock in acc.get(r[0], []):
+                    if r[0] in PSUM:
+                        hit = pe != e or (e != "P" and (w or pw) and lo < r[2] and r[1] < hi)
+                    else:
+                        hit = (w or pw) and lo < r[2] and r[1] < hi
+                    if hit and need.get(tok[0], (0, None))[0] < tok[1]:
+                        need[tok[0]] = (tok[1], clock)
+        items = sorted(need.items())
+        for s, (v, clock) in items:
+            if known[e].get(s, 0) >= v:
+                continue
+            if any(s2 != s and c2.get(s, 0) >= v for s2, (v2, c2) in items):
+                continue
+            Q[e].wait_ge(T.sem[s], v)
+        for s, (v, clock) in items:
+            for s2, v2 in list(clock.items()) + [(s, v)]:
+                if known[e].get(s2, 0) < v2:
+                    known[e][s2] = v2
+
+    def note(e, reads, writes, tok):
+        clock = dict(known[e])
+        for rs, w in ((reads, False), (writes, True)):
+            for r in spans(rs):
+                lst = acc.setdefault(r[0], [])
+                if w:
+                    lst[:] = [a for a in lst if not (r[1] <= a[0] and a[1] <= r[2] and len(r) == 3)]
+                lst.append([r[1], r[2], w, e, tok, clock])
+
+    def op(e, fn, out, ins):
+        order(e, ins, [out])
+        cnt["e" + e] += 1
+        fn().then_inc(T.sem["e" + e], 1)
+        note(e, ins, [out], ("e" + e, cnt["e" + e]))
+
+    def sc(x):
+        return ap(x) if isinstance(x, tuple) else x
+
+    def tt(out, a, b, o):
+        op("V", lambda: g.vector.tensor_tensor(ap(out), ap(a), ap(b), o), out, [a, b])
+
+    def ts(out, a, s1, o0, s2=None, o1=None):
+        if o1 is None:
+            op("V", lambda: g.vector.tensor_scalar(ap(out), ap(a), sc(s1), None, o0), out, [a, s1])
+        else:
+            op("V", lambda: g.vector.tensor_scalar(ap(out), ap(a), sc(s1), sc(s2), o0, o1), out, [a, s1, s2])
+
+    def cp(out, a):
+        op("V", lambda: g.vector.tensor_copy(ap(out), ap(a)), out, [a])
+
+    def ms(out, v):
+        op("V", lambda: g.vector.memset(ap(out), v), out, [])
+
+    def act(out, a, func=AF.Copy, bias=None, scale=1.0):
+        if bias is None:
+            op("S", lambda: g.scalar.activation(ap(out), ap(a), func, scale=scale), out, [a])
+        else:
+            op("S", lambda: g.scalar.activation(ap(out), ap(a), func, bias=ap(bias), scale=scale), out, [a, bias])
+
+    def mm(out, w, x, start, stop):
+        op("P", lambda: g.tensor.matmul(ap(out), ap(w), ap(x), start, stop), out, [w, x])
+
+    def iota(out, pat, base, ch, small):
+        if small:
+            op("G", lambda: g.iota(ap(out), pat, base, ch, allow_small_or_imprecise_dtypes=True), out, [])
+        else:
+            op("G", lambda: g.iota(ap(out), pat, base, ch), out, [])
+
+    def dma(e, out_ap, in_ap, reads, writes):
+        order(e, reads, writes)
+        s = "d%d" % ndma[0]
+        ndma[0] += 1
+        Q[e].dma_start(out_ap, in_ap).then_inc(T.sem[s], 16)
+        note("dma", reads, writes, (s, 16))
+        ends.append((s, 16))
+
+    def send(dst, src, sem):
+        order("G", [src], [])
+        g.remote_dma(ap(dst), ap(src), T.sem[sem], T.sem["sent"], pid, rid, mask_out)
+        cnt["sent"] += n_out
+        acc.setdefault(dst[0], []).append([dst[1], dst[2], True, "rem", (sem, n_in), {}])
+        ends.append((sem, n_in))
+
+    def ind(win, off):
+        return ("ind", win, off)
+
+    def nn(i):
+        return ("N", 32 * i, 32 * i + 32)
+
+    def col(i):
+        return ("COL", i, i + 1)
+
+    def M(n):
+        return (n, 0, 128)
+
+    W = K // NH
+    hs = [(h, h * W, (h + 1) * W) for h in range(NH)]
+    GW, UW, XW, XIW = ("G", 0, C + O), ("U", 0, C + O), ("XF", 0, C + O), ("XI", 0, C + O)
+    MU, TAU = ("MT", 0, 32), ("MT", 32, 64)
+    C1, NN, SLOT = ("CN", 0, 32), ("CN", 32, 64), ("CN", 64, 96)
+    E0, E1, J2F, J1F, P1, NB, BK, BM, QQ, RR, VA, VB, HK, WX, P0 = [nn(i) for i in range(15)]
+    CNT, UP, TP, VP = ("T1", 0, 32), ("TU", 0, 32), ("TU", 32, 64), ("T2", 0, 32)
+
+    dma("Y", ap(("G", O, C + O)), T.fm[:, :], [], [("G", O, C + O)])
+    dma("S", T.M0[:, :], T.m0[:, :], [], [("M0", 0, 32)])
+    dma("S", T.B0[:, :], T.b0[:, :], [], [("B0", 0, K)])
+    dma("S", T.PL[:, :], T.nx[0:128:16, :], [], [("PL", 0, 256)])
+    for a, b in zip(XCH[:-1], XCH[1:]):
+        dma("Y", ap(("XI", O + a, O + b)), T.nx[:, a:b], [], [("XI", O + a, O + b)])
+    dma("Y", ap(("WT", O, O + 2 * K)), T.wl[:, :], [], [("WT", O, O + 2 * K)])
+
+    iota(("QI", 0, 1), [[0, 1]], 0, 1, False)
+    iota(("J", 0, 144), [[1, 144]], 0, 0, True)
+    iota(("BI", 0, 18), [[0, 9], [16, 2]], 0, 0, False)
+    iota(("KI", 0, 32), [[16, 32]], O, 0, False)
+    iota(("SL", 0, 288), [[1, 9], [0, 32]], 1, 0, True)
+    ms(("U", 0, C + O), 0.0)
+    ms(("G", 0, O), 0.0)
+    ms(("XI", 0, O), 0)
+    ms(("XF", 0, O), 0.0)
+    ms(("WT", 0, O), 0.0)
+    ms(("LG", 0, 96), -OFF)
+    ms(col(9), -255.0)
+    ms(col(10), 255.0)
+    ts(("QI", 1, 2), ("QI", 0, 1), 15, A.bitwise_and)
+    cp(col(0), ("QI", 1, 2))
+    tt(col(1), ("QI", 0, 1), ("QI", 1, 2), A.subtract)
+    ts(col(3), col(0), 0.0, A.is_gt, 64.0, A.mult)
+    ts(col(4), col(0), 0.0, A.is_equal, 1.0 / 128, A.mult)
+    ts(col(6), col(0), 15.0, A.is_equal, 0.5, A.mult)
+    ts(col(2), col(1), 15.0, A.add)
+    ts(col(3), col(3), 64.0, A.add)
+    ts(col(4), col(4), 1.0 / 128, A.add)
+    ts(col(7), col(6), 2048.0, A.mult, 255.0, A.add)
+    ts(col(5), col(4), -2048.0, A.mult)
+    ts(M("TA"), M("J"), col(1), A.subtract)
+    ts(("WB", 0, 144), ("J", 0, 144), col(2), A.is_equal, col(3), A.mult)
+    ts(M("ID"), M("TA"), col(0), A.is_equal)
+    ts(M("TC"), M("TA"), col(0), A.is_gt)
+    ts(M("TD"), M("TA"), 0.0, A.is_ge, 64.0, A.mult)
+    ts(M("TE"), M("TA"), 0.0, A.is_equal, 64.0, A.mult)
+    ts(M("TF"), M("TA"), 15.0, A.is_le)
+    tt(M("TD"), M("TD"), M("TE"), A.add)
+    ts(M("NI"), M("ID"), -1.0, A.mult)
+    ts(M("KO"), M("ID"), OFF, A.mult)
+    tt(M("TD"), M("TD"), M("TF"), A.mult)
+    ts(M("TE"), M("ID"), 16.0, A.mult, -1.0, A.add)
+    ts(M("TF"), M("TC"), -14.0, A.mult)
+    tt(M("TC"), M("ID"), M("TC"), A.subtract)
+    tt(M("TE"), M("TE"), M("TF"), A.add)
+    ts(M("TC"), M("TC"), col(6), A.subtract)
+    tt(M("ZS"), M("TE"), M("TD"), A.mult)
+    tt(M("ZD"), M("TC"), M("TD"), A.mult)
+    ts(("KC", 0, 32), ("J", 0, 32), 0.0, A.mult, 6160.0, A.add)
+    ts(("BL", 0, 18), ("BI", 0, 18), col(0), A.add)
+    ts(("KK", 0, 32), ("KI", 0, 32), col(0), A.add)
+    ts(("LS", 0, 32), ("M0", 0, 32), float(O), A.add)
+    ts(MU, ("M0", 0, 32), float(O), A.add)
+    ts(("EX", 0, K), ("B0", 0, K), -1.0, A.mult, 255.0, A.add)
+    ts(("PA", 0, 256), ("PL", 0, 256), float(O), A.add)
+    ts(("PC", 0, 256), ("PA", 0, 256), 6, A.arith_shift_right)
+    ts(("PA", 0, 256), ("PA", 0, 256), 63, A.bitwise_and)
+    cp(("HI", 0, 256), ("PC", 0, 256))
+    ts(("LO", 0, 256), ("PA", 0, 256), 1.0 / 128, A.mult)
+    dma("Y", T.U[0:128:16, O:C + O], T.HI[:, :], [("HI", 0, 256), UW], [("U0", 0, 1)])
+    dma("Y", T.U[1:128:16, O:C + O], T.LO[:, :], [("LO", 0, 256), UW], [("U1", 0, 1)])
+
+    def xconv(j):
+        a, b = XCH[j], XCH[j + 1]
+        ts(("XF", O + a, O + b), ("XI", O + a, O + b), col(4), A.mult, col(5), A.add)
+
+    def tolist(out, buf, lo, hi, first):
+        for r in range(16):
+            mm(out, ("WB", 15 - r, 143 - r), (buf, lo + r, hi, 16), first and r == 0, r == 15)
+
+    def bc(win, n):
+        return win if n == 1 else ind(win, ("BL", 0, 2 * n))
+
+    def lst(name, lo, hi):
+        return (name, lo // 16, hi // 16)
+
+    bank = 0
+    later = []
+    for v in range(V_):
+        if v > 0:
+            RB, RA = "RB%d" % (v - 1), "RA%d" % (v - 1)
+            if v == 1:
+                ms(("LG", 64, 192), -OFF)
+                cp(("LG", 0, 64), ("RL0", 0, 64))
+            else:
+                ms(("LG", 192, 288), -OFF)
+            ts(("LS", 0, 64), (RA, 0, 64), OFF, A.add)
+            if v == 1:
+                cp(("WL", 0, 32), (RA, 64, 96))
+            else:
+                tt(WX, (RA, 64, 96), ("RA0", 64, 96), A.not_equal)
+                tt(WX, WX, (RA, 64, 96), A.mult)
+                cp(("WL", 0, 32), WX)
+            cp(("BW", 0, K), ind(("WT", 0, O + 2 * K), ("WL", 0, 32)))
+            mm(("PB%d" % bank, 0, K), M("ID"), ("BW", 0, K), True, False)
+            mm(("PB%d" % bank, 0, K), M("NI"), (RB, 0, K), False, True)
+            ts(("MT", 0, 64), (RA, 0, 64), OFF, A.add)
+            if v == 1:
+                cp(("CN", 0, 96), (RA, 96, 192))
+                tt(VB, (RA, 224, 256), (RA, 192, 224), A.subtract)
+                tt(("H", 0, 96), bc(SLOT, 3), ("SL", 0, 96), A.is_equal)
+                tt(("P", 0, 96), bc(VB, 3), ("H", 0, 96), A.mult)
+                later.append(lambda: tt(("LG", 0, 96), ("P", 0, 96), ("LG", 0, 96), A.add))
+            else:
+                cp(("CN", 0, 64), (RA, 96, 160))
+                later.append(lambda: cp(("LG", 0, 192), ("RL1", 0, 192)))
+        else:
+            mm(("PB%d" % bank, 0, K), M("NI"), ("EX", 0, K), True, True)
+        terms = [("NI", ("EX", 0, K))]
+
+        for st in range(S_):
+            i = S_ * v + st + 1
+            last, fin = st == S_ - 1, i == S_ * V_
+            PB, PN = "PB%d" % bank, ("PB%d" % (1 - bank), 0, K)
+            bank = 1 - bank
+            GA, GB = ("GA", K * st, K * st + K), ("GB", K * st, K * st + K)
+            fresh = st == 0 and v > 0
+            if not fresh:
+                for j, (w, x) in enumerate(terms):
+                    mm(PN, M(w), x, j == 0, False)
+            for h, lo, hi in hs:
+                act(("F", lo, hi), ind(GW, lst("LS", lo, hi)), AF.Identity, col(9))
+            if i > 1:
+                if i == 2:
+                    order("S", [("U0", 0, 1), ("U1", 0, 1)], [])
+                act(("R1", K, 2 * K), ind(UW, ("LS", 32, 64)))
+                act(("X", 0, K), ind(XW, ("LS", 0, 32)))
+            for h, lo, hi in hs:
+                tt(("R1", lo, hi), ("F", lo, hi), (PB, lo, hi), A.is_gt)
+            for h, lo, hi in hs:
+                ts(("F2", lo, hi), ("F", lo, hi), 2.0, A.mult, col(7), A.add)
+                tt(("D", lo, hi), ("F2", lo, hi), (PB, lo, hi), A.is_gt)
+            if fresh:
+                act(("EX", 0, K), (PB, 0, K), AF.Relu, None, -1.0)
+            tolist(CNT, "R1", 0, K, True)
+            for h, lo, hi in hs:
+                mm(("Z%d" % h, 0, W), M("ZS"), ("R1", lo, hi), True, False)
+                mm(("Z%d" % h, 0, W), M("ZD"), ("D", lo, hi), False, True)
+            if i > 1:
+                tolist(UP, "R1", K, 2 * K, True)
+            mm(VP, M("ID"), ("KC", 0, 32), True, False)
+
+            def ycall():
+                for h, lo, hi in hs:
+                    tt(("Y", lo, hi), ("X", lo, hi), ("Z%d" % h, 0, W), A.min)
+                tolist(VP, "Y", 0, K, False)
+
+            if i == 1:
+                xconv(0)
+                ts(E0, CNT, 0.0, A.is_equal)
+                tt(P0, E0, MU, A.mult)
+                cp(C1, E0)
+                cp(("J1", 0, 32), P0)
+                cp(("LS", 32, 64), P0)
+                act(GA, ind(GW, ("J1", 0, 32)))
+                mm(PN, M("NI"), GA, False, True)
+                terms.append(("NI", GA))
+                cp(TAU, P0)
+                cp(NN, E0)
+                ts(("LG", 0, 32), P0, -OFF, A.add)
+                for j in range(1, len(XCH) - 2):
+                    xconv(j)
+                for h, lo, hi in hs:
+                    ts(("X", lo, hi), ind(XIW, lst("LS", lo, hi)), col(4), A.mult, col(5), A.add)
+                ycall()
+                xconv(len(XCH) - 2)
+                cp(("NI32", 0, 32), VP)
+                ts(MU, ("NI32", 0, 32), 8191, A.bitwise_and)
+                cp(("LS", 0, 32), MU)
+                continue
+
+            n0, n1 = 32 * (i - 1), 32 * i
+            ts(E1, CNT, 64.0, A.is_equal)
+            ts(E0, CNT, 0.0, A.is_equal)
+            tt(J2F, E1, TAU, A.mult)
+            tt(P0, E0, MU, A.mult)
+            cp(("J2", 0, 32), J2F)
+            act(GB, ind(GW, ("J2", 0, 32)))
+            ycall()
+            tt(P1, E1, UP, A.mult)
+            tt(NN, NN, E0, A.add)
+            tt(J1F, P0, P1, A.add)
+            tt(QQ, NN, E0, A.mult)
+            cp(("J1", 0, 32), J1F)
+            act(GA, ind(GW, ("J1", 0, 32)))
+            if fresh:
+                mm(PN, M("NI"), ("EX", 0, K), True, False)
+            mm(PN, M("ID"), GB, False, False)
+            tt(SLOT, QQ, C1, A.max)
+            ts(NB, J2F, 0.0, A.is_equal)
+            tt(RR, C1, E1, A.subtract)
+            terms += [("ID", GB), ("NI", GA)]
+            if i != S_:
+                tt(VB, J1F, J2F, A.subtract)
+            for f in later:
+                f()
+            del later[:]
+            tt(("H", 0, n1), bc(SLOT, i), ("SL", 0, n1), A.is_equal)
+            if fin:
+                mm(PN, M("NI"), GA, False, True)
+                tt(("P", 0, n1), bc(VB, i), ("H", 0, n1), A.mult)
+                tt(BM, VP, MU, A.subtract)
+                tt(("PR", 0, n1), ("P", 0, n1), ("LG", 0, n1), A.add)
+                tt(BM, BM, NB, A.mult)
+                ts(("OL", 0, 288), ("PR", 0, 288), OFF - O, A.add, -1.0, A.max)
+                dma("Y", T.yl[:, :], T.OL[:, :], [("OL", 0, 288)], [])
+                tt(("NI32", 0, 32), BM, MU, A.add)
+                tt(C1, QQ, RR, A.max)
+                ts(MU, ("NI32", 0, 32), 8191, A.bitwise_and)
+                ts(("OC", 0, 32), C1, -1.0, A.add)
+                ts(("OM", 0, 32), MU, -float(O), A.add)
+                dma("Y", T.yc[:, :], T.OC[:, :], [("OC", 0, 32)], [])
+                dma("Y", T.ym[:, :], T.OM[:, :], [("OM", 0, 32)], [])
+                act(("OB", 0, K), PN, AF.Identity, col(10))
+                dma("S", T.yb[:, :], T.OB[:, :], [("OB", 0, K)], [])
+                continue
+            if i > 2:
+                tt(("PQ", 0, n0 - 32), ("H", 32, n0), ("LG", 0, n0 - 32), A.mult)
+                for j in range(i - 2):
+                    mm(TP, M("KO"), ("H", 32 * j + 32, 32 * j + 64), j == 0, False)
+                for j in range(i - 2):
+                    mm(TP, M("ID"), ("PQ", 32 * j, 32 * j + 32), False, j == i - 3)
+            mm(PN, M("NI"), GA, False, True)
+            if last:
+                act(("SB%d" % v, 0, K), PN, AF.Relu, None, -1.0)
+            tt(BM, VP, MU, A.subtract)
+            ts(BK, CNT, 128.0, A.is_ge)
+            tt(BM, BM, NB, A.mult)
+            tt(C1, QQ, RR, A.max)
+            tt(("NI32", 0, 32), BM, MU, A.add)
+            tt(BK, BK, TAU, A.mult)
+            ts(MU, ("NI32", 0, 32), 8191, A.bitwise_and)
+            tt(BK, BK, P0, A.add)
+            if not last:
+                cp(("LS", 0, 32), MU)
+            elif v == 0:
+                cp(("SA0", 96, 192), ("CN", 0, 96))
+                ts(("SA0", 192, 256), ("N", 64, 128), -OFF, A.add)
+            else:
+                cp(("SA1", 96, 160), ("CN", 0, 64))
+            if i == 2:
+                cp(("LS", 32, 64), BK)
+                cp(TAU, BK)
+            else:
+                tt(VA, E1, TP, A.mult)
+                if last:
+                    ts(HK, C1, 0.0, A.is_gt)
+                tt(TAU, VA, BK, A.add)
+            if not last:
+                if i > 2:
+                    cp(("LS", 32, 64), TAU)
+                tt(("P", 0, n1), bc(VB, i), ("H", 0, n1), A.mult)
+                tt(("LG", 0, n1), ("P", 0, n1), ("LG", 0, n1), A.add)
+                if i == 2:
+                    cp(("SL0", 0, 64), ("LG", 0, 64))
+                    send(("RL0", 0, 64), ("SL0", 0, 64), "l0")
+            else:
+                SA = "SA%d" % v
+                tt(HK, HK, ("KK", 0, 32), A.mult)
+                ts(("NI32", 64, 96), TAU, 1, A.bitwise_and)
+                ts((SA, 0, 64), ("MT", 0, 64), -OFF, A.add)
+                ts(WX, ("NI32", 64, 96), 512.0, A.mult)
+                tt((SA, 64, 96), WX, HK, A.add)
+                na = 256 if v == 0 else 160
+                send(("RA%d" % v, 0, na), (SA, 0, na), "a%d" % v)
+                send(("RB%d" % v, 0, K), ("SB%d" % v, 0, K), "b%d" % v)
+                if v == 1:
+                    tt(("P", 0, n1), bc(VB, i), ("H", 0, n1), A.mult)
+                    tt(("SL1", 0, n1), ("P", 0, n1), ("LG", 0, n1), A.add)
+                    send(("RL1", 0, n1), ("SL1", 0, n1), "l1")
+
+    for s in ("eV", "eS", "eP", "eG", "sent"):
+        g.wait_ge(T.sem[s], cnt[s])
+    for s, val in ends:
+        g.wait_ge(T.sem[s], val)

@@ -2,13 +2,17 @@ from concourse.mybir import AluOpType as A, ActivationFunctionType as AF
 
 C, K, V_, S_ = 4096, 512, 3, 3
 O = 16
+FO = C + O
 NH = 2
 OFF = 2064.0
 XCH = [0, 1280, 2560, 3584, 4096]
+FV, DV = (1,), (1,)
+GAT, HOP, SELF, LOOK, RATE = 1.8, 200, 100, 60, 300
 
 SCRATCH = {
-    "G": ("sbuf", [128, C + O], "bfloat16"), "U": ("sbuf", [128, C + O], "bfloat16"),
-    "XI": ("sbuf", [128, C + O], "int32"), "XF": ("sbuf", [128, C + O], "float32"),
+    "G": ("sbuf", [128, 2 * FO], "bfloat16"), "FP": ("sbuf", [128, C], "bfloat16"), "U": ("sbuf", [128, FO], "bfloat16"),
+    "P16": ("sbuf", [128, 256], "uint16"), "PM": ("sbuf", [128, 256], "int32"),
+    "XI": ("sbuf", [128, FO], "int32"), "XF": ("sbuf", [128, FO], "float32"),
     "WT": ("sbuf", [128, 2 * K + O], "bfloat16"), "B0": ("sbuf", [128, K], "bfloat16"),
     "M0": ("sbuf", [128, 32], "int32"), "PL": ("sbuf", [128, 256], "int32"),
     "PA": ("sbuf", [128, 256], "int32"), "PC": ("sbuf", [128, 256], "int32"),
@@ -24,25 +28,25 @@ SCRATCH = {
     "KI": ("sbuf", [128, 32], "int32"), "KK": ("sbuf", [128, 32], "float32"),
     "F": ("sbuf", [128, K], "bfloat16"), "F2": ("sbuf", [128, K], "bfloat16"), "X": ("sbuf", [128, K], "float32"),
     "R1": ("sbuf", [128, 2 * K], "bfloat16"), "D": ("sbuf", [128, K], "bfloat16"), "Y": ("sbuf", [128, K], "float16"),
-    "GA": ("sbuf", [128, 3 * K], "bfloat16"), "GB": ("sbuf", [128, 3 * K], "bfloat16"),
-    "BW": ("sbuf", [128, K], "bfloat16"), "EX": ("sbuf", [128, K], "bfloat16"),
+    "GA": ("sbuf", [128, 9 * K], "bfloat16"), "BW": ("sbuf", [128, K], "bfloat16"), "EX": ("sbuf", [128, K], "bfloat16"),
     "MT": ("sbuf", [128, 64], "int32"), "LS": ("sbuf", [128, 64], "uint16"),
-    "J1": ("sbuf", [128, 32], "uint16"), "J2": ("sbuf", [128, 32], "uint16"), "WL": ("sbuf", [128, 32], "uint16"),
+    "J1": ("sbuf", [128, 32], "uint16"), "WL": ("sbuf", [128, 32], "uint16"),
     "N": ("sbuf", [128, 32 * 16], "float32"), "CN": ("sbuf", [128, 96], "bfloat16"), "NI32": ("sbuf", [128, 96], "int32"),
     "H": ("sbuf", [128, 288], "bfloat16"), "P": ("sbuf", [128, 288], "float32"), "PR": ("sbuf", [128, 288], "float32"),
-    "SB0": ("sbuf", [128, K], "bfloat16"), "SB1": ("sbuf", [128, K], "bfloat16"),
-    "RB0": ("sbuf", [128, K], "bfloat16"), "RB1": ("sbuf", [128, K], "bfloat16"),
-    "SA0": ("sbuf", [128, 256], "float16"), "SA1": ("sbuf", [128, 160], "float16"),
-    "RA0": ("sbuf", [128, 256], "float16"), "RA1": ("sbuf", [128, 160], "float16"),
-    "SL0": ("sbuf", [128, 64], "float16"), "RL0": ("sbuf", [128, 64], "float16"),
-    "SL1": ("sbuf", [128, 192], "float16"), "RL1": ("sbuf", [128, 192], "float16"),
     "OB": ("sbuf", [128, K], "float32"), "OL": ("sbuf", [128, 288], "float32"), "OM": ("sbuf", [128, 32], "float32"),
     "OC": ("sbuf", [128, 32], "float32"),
 }
+for _v in range(V_ - 1):
+    for _n in ("SB", "RB", "RG"):
+        SCRATCH["%s%d" % (_n, _v)] = ("sbuf", [128, K], "bfloat16")
+    for _n in ("SA", "RA"):
+        SCRATCH["%s%d" % (_n, _v)] = ("sbuf", [128, 160], "float16")
+    for _n in ("SL", "RL"):
+        SCRATCH["%s%d" % (_n, _v)] = ("sbuf", [128, 96 * (_v + 1)], "float16")
 PSUM = ["PB0", "PB1", "Z0", "Z1", "T1", "TU", "T2", "LG"]
 for _n in PSUM:
     SCRATCH[_n] = ("psum", [128, 512], "float32")
-SEMAPHORES = ["eV", "eS", "eP", "eG", "sent", "a0", "a1", "b0", "b1", "l0", "l1"] + ["d%d" % i for i in range(24)]
+SEMAPHORES = ["eV", "eS", "eP", "eG", "sent", "a0", "a1", "b0", "b1", "l0", "l1", "g0", "g1"] + ["d%d" % i for i in range(24)]
 
 
 def rank_program(g, core, T, topo):
@@ -60,6 +64,7 @@ def rank_program(g, core, T, topo):
     acc = {}
     ndma = [0]
     ends = []
+    prog = []
 
     def ap(r):
         if r[0] == "ind":
@@ -111,17 +116,93 @@ def rank_program(g, core, T, topo):
                     lst[:] = [a for a in lst if not (r[1] <= a[0] and a[1] <= r[2] and len(r) == 3)]
                 lst.append([r[1], r[2], w, e, tok, clock])
 
-    def op(e, fn, out, ins):
-        order(e, ins, [out])
-        cnt["e" + e] += 1
-        fn().then_inc(T.sem["e" + e], 1)
-        note(e, ins, [out], ("e" + e, cnt["e" + e]))
+    def width(r):
+        if r[0] == "ind":
+            return 16 * (r[2][2] - r[2][1])
+        return -((r[1] - r[2]) // (r[3] if len(r) == 4 else 1))
+
+    def op(e, fn, out, ins, two=False):
+        def emit():
+            order(e, ins, [out])
+            cnt["e" + e] += 1
+            fn().then_inc(T.sem["e" + e], 1)
+            note(e, ins, [out], ("e" + e, cnt["e" + e]))
+        aps = [r for r in ins if isinstance(r, tuple) and r[0] in list(SCRATCH) + ["ind"]]
+        n = width(out)
+        if e == "P":
+            t = max(64, width(ins[1])) * 0.5
+        elif e == "G":
+            t = 130 + 2 * n
+        elif any(r[0] == "ind" for r in aps):
+            t = 60 + GAT * n
+        elif two:
+            t = max(64, n * (1 if any(r[0] in PSUM for r in aps) else 2))
+        elif e == "V" and all(SCRATCH[r[0]][2] in ("bfloat16", "float16", "uint16") for r in aps + [out] if width(r) > 1):
+            t = max(64, n * 0.5)
+        else:
+            t = max(64, n)
+        prog.append([e, emit, ins, [out], t, t])
+
+    def arrange():
+        seen, deps = {}, []
+        for k, (e, emit, reads, writes) in enumerate(a[:4] for a in prog):
+            d = set()
+            for rs, w in ((reads, False), (writes, True)):
+                for r in spans(rs):
+                    for lo, hi, pw, pe, j in seen.get(r[0], []):
+                        if ((w or pw) and lo < r[2] and r[1] < hi) or (r[0] in PSUM and (pe != e or e == "P")):
+                            d.add(j)
+            for rs, w in ((reads, False), (writes, True)):
+                for r in spans(rs):
+                    lst = seen.setdefault(r[0], [])
+                    if w and len(r) == 3:
+                        lst[:] = [a for a in lst if not (r[1] <= a[0] and a[1] <= r[2])]
+                    lst.append((r[1], r[2], w, e, k))
+            d.discard(k)
+            deps.append(sorted(d))
+
+        def gap(j, k):
+            if prog[j][0] == prog[k][0] and prog[j][4] == prog[j][5]:
+                return 0 if prog[k][0] == "P" else SELF
+            return HOP
+        n = len(prog)
+        way, users = [0.0] * n, [[] for _ in range(n)]
+        for k in range(n - 1, -1, -1):
+            way[k] += prog[k][5]
+            for j in deps[k]:
+                users[j].append(k)
+                way[j] = max(way[j], way[k] + gap(j, k))
+        left = [len(d) for d in deps]
+        ready = {e: [] for e in Q}
+        at = [0.0] * n
+        for k in range(n):
+            if not left[k]:
+                ready[prog[k][0]].append(k)
+        free = {e: 0.0 for e in Q}
+        wire = 0.0
+        for _ in range(n):
+            e = min((q for q in Q if ready[q]), key=lambda q: max(free[q], min(at[k] for k in ready[q])))
+            now = max(free[e], min(at[k] for k in ready[e]))
+            best = max((k for k in ready[e] if at[k] <= now + LOOK), key=lambda k: (1e9 if len(prog[k]) > 6 else way[k], -k))
+            ready[e].remove(best)
+            start = max(free[e], at[best])
+            free[e] = start + prog[best][4]
+            done = start + prog[best][5]
+            if len(prog[best]) > 6:
+                wire = max(wire, start + 1500) + prog[best][6]
+                done = wire + 500
+            prog[best][1]()
+            for k in users[best]:
+                at[k] = max(at[k], done + gap(best, k))
+                left[k] -= 1
+                if not left[k]:
+                    ready[prog[k][0]].append(k)
 
     def sc(x):
         return ap(x) if isinstance(x, tuple) else x
 
     def tt(out, a, b, o):
-        op("V", lambda: g.vector.tensor_tensor(ap(out), ap(a), ap(b), o), out, [a, b])
+        op("V", lambda: g.vector.tensor_tensor(ap(out), ap(a), ap(b), o), out, [a, b], True)
 
     def ts(out, a, s1, o0, s2=None, o1=None):
         if o1 is None:
@@ -135,35 +216,39 @@ def rank_program(g, core, T, topo):
     def ms(out, v):
         op("V", lambda: g.vector.memset(ap(out), v), out, [])
 
-    def act(out, a, func=AF.Copy, bias=None, scale=1.0):
+    def act(out, a, func=AF.Copy, bias=None, scale=1.0, after=()):
         if bias is None:
-            op("S", lambda: g.scalar.activation(ap(out), ap(a), func, scale=scale), out, [a])
+            op("S", lambda: g.scalar.activation(ap(out), ap(a), func, scale=scale), out, [a] + list(after))
         else:
             op("S", lambda: g.scalar.activation(ap(out), ap(a), func, bias=ap(bias), scale=scale), out, [a, bias])
 
     def mm(out, w, x, start, stop):
         op("P", lambda: g.tensor.matmul(ap(out), ap(w), ap(x), start, stop), out, [w, x])
 
-    def iota(out, pat, base, ch, small):
+    def iota(out, pat, base, ch, small, after=()):
         if small:
-            op("G", lambda: g.iota(ap(out), pat, base, ch, allow_small_or_imprecise_dtypes=True), out, [])
+            op("G", lambda: g.iota(ap(out), pat, base, ch, allow_small_or_imprecise_dtypes=True), out, list(after))
         else:
             op("G", lambda: g.iota(ap(out), pat, base, ch), out, [])
 
-    def dma(e, out_ap, in_ap, reads, writes):
-        order(e, reads, writes)
-        s = "d%d" % ndma[0]
-        ndma[0] += 1
-        Q[e].dma_start(out_ap, in_ap).then_inc(T.sem[s], 16)
-        note("dma", reads, writes, (s, 16))
-        ends.append((s, 16))
+    def dma(e, out_ap, in_ap, reads, writes, nbytes):
+        def emit():
+            order(e, reads, writes)
+            s = "d%d" % ndma[0]
+            ndma[0] += 1
+            Q[e].dma_start(out_ap, in_ap).then_inc(T.sem[s], 16)
+            note("dma", reads, writes, (s, 16))
+            ends.append((s, 16))
+        prog.append([e, emit, reads, writes, 60, 2000 + nbytes / RATE, nbytes / RATE])
 
     def send(dst, src, sem):
-        order("G", [src], [])
-        g.remote_dma(ap(dst), ap(src), T.sem[sem], T.sem["sent"], pid, rid, mask_out)
-        cnt["sent"] += n_out
-        acc.setdefault(dst[0], []).append([dst[1], dst[2], True, "rem", (sem, n_in), {}])
-        ends.append((sem, n_in))
+        def emit():
+            order("G", [src], [])
+            g.remote_dma(ap(dst), ap(src), T.sem[sem], T.sem["sent"], pid, rid, mask_out)
+            cnt["sent"] += n_out
+            acc.setdefault(dst[0], []).append([dst[1], dst[2], True, "rem", (sem, n_in), {}])
+            ends.append((sem, n_in))
+        prog.append(["G", emit, [src], [dst], 500, 2500 + 3.2 * width(src)])
 
     def ind(win, off):
         return ("ind", win, off)
@@ -179,31 +264,33 @@ def rank_program(g, core, T, topo):
 
     W = K // NH
     hs = [(h, h * W, (h + 1) * W) for h in range(NH)]
-    GW, UW, XW, XIW = ("G", 0, C + O), ("U", 0, C + O), ("XF", 0, C + O), ("XI", 0, C + O)
+    FW, GW, UW, XW, XIW = ("G", FO, 2 * FO), ("G", 0, 2 * FO), ("U", 0, FO), ("XF", 0, FO), ("XI", 0, FO)
     MU, TAU = ("MT", 0, 32), ("MT", 32, 64)
     C1, NN, SLOT = ("CN", 0, 32), ("CN", 32, 64), ("CN", 64, 96)
-    E0, E1, J2F, J1F, P1, NB, BK, BM, QQ, RR, VA, VB, HK, WX, P0 = [nn(i) for i in range(15)]
+    E0, E1, J2F, J1F, P1, NB, BK, BM, QQ, RR, VA, VB, HK, WX, P0, M4 = [nn(i) for i in range(16)]
     CNT, UP, TP, VP = ("T1", 0, 32), ("TU", 0, 32), ("TU", 32, 64), ("T2", 0, 32)
 
-    dma("Y", ap(("G", O, C + O)), T.fm[:, :], [], [("G", O, C + O)])
-    dma("S", T.M0[:, :], T.m0[:, :], [], [("M0", 0, 32)])
-    dma("S", T.B0[:, :], T.b0[:, :], [], [("B0", 0, K)])
-    dma("S", T.PL[:, :], T.nx[0:128:16, :], [], [("PL", 0, 256)])
+    for q in range(2):
+        dma("Y", T.PL[:, 128 * q:128 * q + 128], T.nx[0:128:16, 2048 * q:2048 * q + 2048], [], [("PL", 128 * q, 128 * q + 128)], 512 * 128)
+    dma("S", T.M0[:, :], T.m0[:, :], [], [("M0", 0, 32)], 512 * 32)
+    dma("Y", ap(("G", FO + O, 2 * FO)), T.fm[:, :], [], [("G", FO + O, 2 * FO)], 256 * C)
+    dma("Y", T.B0[:, :], T.b0[:, :], [], [("B0", 0, K)], 256 * K)
     for a, b in zip(XCH[:-1], XCH[1:]):
-        dma("Y", ap(("XI", O + a, O + b)), T.nx[:, a:b], [], [("XI", O + a, O + b)])
-    dma("Y", ap(("WT", O, O + 2 * K)), T.wl[:, :], [], [("WT", O, O + 2 * K)])
+        dma("Y", ap(("XI", O + a, O + b)), T.nx[:, a:b], [], [("XI", O + a, O + b)], 512 * (b - a))
+    dma("Y", ap(("WT", O, O + 2 * K)), T.wl[:, :], [], [("WT", O, O + 2 * K)], 512 * K)
 
     iota(("QI", 0, 1), [[0, 1]], 0, 1, False)
     iota(("J", 0, 144), [[1, 144]], 0, 0, True)
+    iota(("PM", 0, 256), [[2048, 2], [1, 128]], 0, 128, False)
     iota(("BI", 0, 18), [[0, 9], [16, 2]], 0, 0, False)
     iota(("KI", 0, 32), [[16, 32]], O, 0, False)
     iota(("SL", 0, 288), [[1, 9], [0, 32]], 1, 0, True)
-    ms(("U", 0, C + O), 0.0)
+    iota(UW, [[0, FO]], 0, 0, True, [("SL", 0, 288), ("PM", 0, 256), ("KI", 0, 32), ("BI", 0, 18), ("J", 0, 144), ("QI", 0, 1)])
     ms(("G", 0, O), 0.0)
+    ms(("G", FO, FO + O), 0.0)
     ms(("XI", 0, O), 0)
     ms(("XF", 0, O), 0.0)
     ms(("WT", 0, O), 0.0)
-    ms(("LG", 0, 96), -OFF)
     ms(col(9), -255.0)
     ms(col(10), 255.0)
     ts(("QI", 1, 2), ("QI", 0, 1), 15, A.bitwise_and)
@@ -241,13 +328,29 @@ def rank_program(g, core, T, topo):
     ts(("LS", 0, 32), ("M0", 0, 32), float(O), A.add)
     ts(MU, ("M0", 0, 32), float(O), A.add)
     ts(("EX", 0, K), ("B0", 0, K), -1.0, A.mult, 255.0, A.add)
-    ts(("PA", 0, 256), ("PL", 0, 256), float(O), A.add)
+    ts(("P16", 0, 256), ("PL", 0, 256), float(O), A.add)
+    ts(col(8), col(1), 128.0, A.mult)
+    tt(("PA", 0, 256), ("PL", 0, 256), ("PM", 0, 256), A.subtract)
+    ts(("PA", 0, 256), ("PA", 0, 256), col(8), A.add)
     ts(("PC", 0, 256), ("PA", 0, 256), 6, A.arith_shift_right)
     ts(("PA", 0, 256), ("PA", 0, 256), 63, A.bitwise_and)
     cp(("HI", 0, 256), ("PC", 0, 256))
     ts(("LO", 0, 256), ("PA", 0, 256), 1.0 / 128, A.mult)
-    dma("Y", T.U[0:128:16, O:C + O], T.HI[:, :], [("HI", 0, 256), UW], [("U0", 0, 1)])
-    dma("Y", T.U[1:128:16, O:C + O], T.LO[:, :], [("LO", 0, 256), UW], [("U1", 0, 1)])
+    for q in range(2):
+        a, b = O + 2048 * q, O + 2048 * q + 2048
+        dma("Y", T.U[0:128:16, a:b], T.HI[:, 128 * q:128 * q + 128], [("HI", 0, 256), UW], [("U0", q, q + 1)], 256 * 128)
+        dma("Y", T.U[1:128:16, a:b], T.LO[:, 128 * q:128 * q + 128], [("LO", 0, 256), UW], [("U1", q, q + 1)], 256 * 128)
+
+    def refunds():
+        for q in range(4):
+            (cp if q in FV else act)(("FP", 1024 * q, 1024 * q + 1024), ind(FW, ("P16", 64 * q, 64 * q + 64)))
+        for k in range(8):
+            bk, q = ("TU", "LG")[k % 2], k // 4
+            for r in range(4):
+                a = 512 * k + 128 * r
+                mm((bk, 128 * r, 128 * r + 128), M("NI"), ("G", FO + O + a, FO + O + a + 128), True, False)
+                mm((bk, 128 * r, 128 * r + 128), M("ID"), ("FP", 2048 * q + 4 * (k % 4) + r, 2048 * q + 2048, 16), False, True)
+            (cp if k in DV else act)(("G", O + 512 * k, O + 512 * k + 512), (bk, 0, K))
 
     def xconv(j):
         a, b = XCH[j], XCH[j + 1]
@@ -264,15 +367,10 @@ def rank_program(g, core, T, topo):
         return (name, lo // 16, hi // 16)
 
     bank = 0
-    later = []
     for v in range(V_):
         if v > 0:
             RB, RA = "RB%d" % (v - 1), "RA%d" % (v - 1)
-            if v == 1:
-                ms(("LG", 64, 192), -OFF)
-                cp(("LG", 0, 64), ("RL0", 0, 64))
-            else:
-                ms(("LG", 192, 288), -OFF)
+            ms(("LG", 96 * v, 96 * v + 96), -OFF)
             ts(("LS", 0, 64), (RA, 0, 64), OFF, A.add)
             if v == 1:
                 cp(("WL", 0, 32), (RA, 64, 96))
@@ -281,18 +379,13 @@ def rank_program(g, core, T, topo):
                 tt(WX, WX, (RA, 64, 96), A.mult)
                 cp(("WL", 0, 32), WX)
             cp(("BW", 0, K), ind(("WT", 0, O + 2 * K), ("WL", 0, 32)))
-            mm(("PB%d" % bank, 0, K), M("ID"), ("BW", 0, K), True, False)
-            mm(("PB%d" % bank, 0, K), M("NI"), (RB, 0, K), False, True)
+            mm(("PB%d" % bank, 0, K), M("NI"), (RB, 0, K), True, False)
+            mm(("PB%d" % bank, 0, K), M("NI"), ("RG%d" % (v - 1), 0, K), False, False)
+            mm(("PB%d" % bank, 0, K), M("ID"), ("BW", 0, K), False, True)
+            ts(M4, (RA, 0, 32), OFF + FO, A.add)
             ts(("MT", 0, 64), (RA, 0, 64), OFF, A.add)
-            if v == 1:
-                cp(("CN", 0, 96), (RA, 96, 192))
-                tt(VB, (RA, 224, 256), (RA, 192, 224), A.subtract)
-                tt(("H", 0, 96), bc(SLOT, 3), ("SL", 0, 96), A.is_equal)
-                tt(("P", 0, 96), bc(VB, 3), ("H", 0, 96), A.mult)
-                later.append(lambda: tt(("LG", 0, 96), ("P", 0, 96), ("LG", 0, 96), A.add))
-            else:
-                cp(("CN", 0, 64), (RA, 96, 160))
-                later.append(lambda: cp(("LG", 0, 192), ("RL1", 0, 192)))
+            cp(("CN", 0, 64), (RA, 96, 160))
+            cp(("LG", 0, 96 * v), ("RL%d" % (v - 1), 0, 96 * v))
         else:
             mm(("PB%d" % bank, 0, K), M("NI"), ("EX", 0, K), True, True)
         terms = [("NI", ("EX", 0, K))]
@@ -301,18 +394,17 @@ def rank_program(g, core, T, topo):
             i = S_ * v + st + 1
             last, fin = st == S_ - 1, i == S_ * V_
             PB, PN = "PB%d" % bank, ("PB%d" % (1 - bank), 0, K)
-            bank = 1 - bank
-            GA, GB = ("GA", K * st, K * st + K), ("GB", K * st, K * st + K)
+            if fin or not last:
+                bank = 1 - bank
+            GA = ("GA", K * (i - 1), K * i)
             fresh = st == 0 and v > 0
-            if not fresh:
+            if not fresh and (fin or not last):
                 for j, (w, x) in enumerate(terms):
                     mm(PN, M(w), x, j == 0, False)
             for h, lo, hi in hs:
-                act(("F", lo, hi), ind(GW, lst("LS", lo, hi)), AF.Identity, col(9))
+                act(("F", lo, hi), ind(FW, lst("LS", lo, hi)), AF.Identity, col(9))
             if i > 1:
-                if i == 2:
-                    order("S", [("U0", 0, 1), ("U1", 0, 1)], [])
-                act(("R1", K, 2 * K), ind(UW, ("LS", 32, 64)))
+                act(("R1", K, 2 * K), ind(UW, ("LS", 32, 64)), after=[("U0", 0, 2), ("U1", 0, 2)])
                 act(("X", 0, K), ind(XW, ("LS", 0, 32)))
             for h, lo, hi in hs:
                 tt(("R1", lo, hi), ("F", lo, hi), (PB, lo, hi), A.is_gt)
@@ -321,6 +413,9 @@ def rank_program(g, core, T, topo):
                 tt(("D", lo, hi), ("F2", lo, hi), (PB, lo, hi), A.is_gt)
             if fresh:
                 act(("EX", 0, K), (PB, 0, K), AF.Relu, None, -1.0)
+            if last and not fin:
+                act(("SB%d" % v, 0, K), (PB, 0, K), AF.Copy, None, -1.0)
+                send(("RB%d" % v, 0, K), ("SB%d" % v, 0, K), "b%d" % v)
             tolist(CNT, "R1", 0, K, True)
             for h, lo, hi in hs:
                 mm(("Z%d" % h, 0, W), M("ZS"), ("R1", lo, hi), True, False)
@@ -341,12 +436,11 @@ def rank_program(g, core, T, topo):
                 cp(C1, E0)
                 cp(("J1", 0, 32), P0)
                 cp(("LS", 32, 64), P0)
-                act(GA, ind(GW, ("J1", 0, 32)))
+                act(GA, ind(FW, ("J1", 0, 32)))
                 mm(PN, M("NI"), GA, False, True)
                 terms.append(("NI", GA))
                 cp(TAU, P0)
                 cp(NN, E0)
-                ts(("LG", 0, 32), P0, -OFF, A.add)
                 for j in range(1, len(XCH) - 2):
                     xconv(j)
                 for h, lo, hi in hs:
@@ -356,34 +450,34 @@ def rank_program(g, core, T, topo):
                 cp(("NI32", 0, 32), VP)
                 ts(MU, ("NI32", 0, 32), 8191, A.bitwise_and)
                 cp(("LS", 0, 32), MU)
+                ts(M4, MU, float(FO), A.add)
+                refunds()
+                ms(("LG", 32, 96), -OFF)
+                ts(("LG", 0, 32), P0, -OFF, A.add)
                 continue
 
             n0, n1 = 32 * (i - 1), 32 * i
             ts(E1, CNT, 64.0, A.is_equal)
             ts(E0, CNT, 0.0, A.is_equal)
             tt(J2F, E1, TAU, A.mult)
-            tt(P0, E0, MU, A.mult)
-            cp(("J2", 0, 32), J2F)
-            act(GB, ind(GW, ("J2", 0, 32)))
-            ycall()
-            tt(P1, E1, UP, A.mult)
-            tt(NN, NN, E0, A.add)
-            tt(J1F, P0, P1, A.add)
-            tt(QQ, NN, E0, A.mult)
+            tt(J1F, E0, M4, A.mult)
+            tt(J1F, J1F, J2F, A.add)
             cp(("J1", 0, 32), J1F)
             act(GA, ind(GW, ("J1", 0, 32)))
+            if last and not fin:
+                send(("RG%d" % v, 0, K), GA, "g%d" % v)
+            ycall()
+            tt(P0, E0, MU, A.mult)
+            tt(P1, E1, UP, A.mult)
+            tt(NN, NN, E0, A.add)
+            tt(QQ, NN, E0, A.mult)
             if fresh:
                 mm(PN, M("NI"), ("EX", 0, K), True, False)
-            mm(PN, M("ID"), GB, False, False)
             tt(SLOT, QQ, C1, A.max)
             ts(NB, J2F, 0.0, A.is_equal)
             tt(RR, C1, E1, A.subtract)
-            terms += [("ID", GB), ("NI", GA)]
-            if i != S_:
-                tt(VB, J1F, J2F, A.subtract)
-            for f in later:
-                f()
-            del later[:]
+            terms += [("NI", GA)]
+            tt(VB, P0, P1, A.add)
             tt(("H", 0, n1), bc(SLOT, i), ("SL", 0, n1), A.is_equal)
             if fin:
                 mm(PN, M("NI"), GA, False, True)
@@ -392,16 +486,16 @@ def rank_program(g, core, T, topo):
                 tt(("PR", 0, n1), ("P", 0, n1), ("LG", 0, n1), A.add)
                 tt(BM, BM, NB, A.mult)
                 ts(("OL", 0, 288), ("PR", 0, 288), OFF - O, A.add, -1.0, A.max)
-                dma("Y", T.yl[:, :], T.OL[:, :], [("OL", 0, 288)], [])
+                dma("Y", T.yl[:, :], T.OL[:, :], [("OL", 0, 288)], [], 512 * 288)
                 tt(("NI32", 0, 32), BM, MU, A.add)
                 tt(C1, QQ, RR, A.max)
                 ts(MU, ("NI32", 0, 32), 8191, A.bitwise_and)
                 ts(("OC", 0, 32), C1, -1.0, A.add)
                 ts(("OM", 0, 32), MU, -float(O), A.add)
-                dma("Y", T.yc[:, :], T.OC[:, :], [("OC", 0, 32)], [])
-                dma("Y", T.ym[:, :], T.OM[:, :], [("OM", 0, 32)], [])
+                dma("Y", T.yc[:, :], T.OC[:, :], [("OC", 0, 32)], [], 512 * 32)
+                dma("Y", T.ym[:, :], T.OM[:, :], [("OM", 0, 32)], [], 512 * 32)
                 act(("OB", 0, K), PN, AF.Identity, col(10))
-                dma("S", T.yb[:, :], T.OB[:, :], [("OB", 0, K)], [])
+                dma("S", T.yb[:, :], T.OB[:, :], [("OB", 0, K)], [], 512 * K)
                 continue
             if i > 2:
                 tt(("PQ", 0, n0 - 32), ("H", 32, n0), ("LG", 0, n0 - 32), A.mult)
@@ -409,9 +503,8 @@ def rank_program(g, core, T, topo):
                     mm(TP, M("KO"), ("H", 32 * j + 32, 32 * j + 64), j == 0, False)
                 for j in range(i - 2):
                     mm(TP, M("ID"), ("PQ", 32 * j, 32 * j + 32), False, j == i - 3)
-            mm(PN, M("NI"), GA, False, True)
-            if last:
-                act(("SB%d" % v, 0, K), PN, AF.Relu, None, -1.0)
+            if not last:
+                mm(PN, M("NI"), GA, False, True)
             tt(BM, VP, MU, A.subtract)
             ts(BK, CNT, 128.0, A.is_ge)
             tt(BM, BM, NB, A.mult)
@@ -422,11 +515,9 @@ def rank_program(g, core, T, topo):
             tt(BK, BK, P0, A.add)
             if not last:
                 cp(("LS", 0, 32), MU)
-            elif v == 0:
-                cp(("SA0", 96, 192), ("CN", 0, 96))
-                ts(("SA0", 192, 256), ("N", 64, 128), -OFF, A.add)
+                ts(M4, MU, float(FO), A.add)
             else:
-                cp(("SA1", 96, 160), ("CN", 0, 64))
+                cp(("SA%d" % v, 96, 160), ("CN", 0, 64))
             if i == 2:
                 cp(("LS", 32, 64), BK)
                 cp(TAU, BK)
@@ -440,9 +531,6 @@ def rank_program(g, core, T, topo):
                     cp(("LS", 32, 64), TAU)
                 tt(("P", 0, n1), bc(VB, i), ("H", 0, n1), A.mult)
                 tt(("LG", 0, n1), ("P", 0, n1), ("LG", 0, n1), A.add)
-                if i == 2:
-                    cp(("SL0", 0, 64), ("LG", 0, 64))
-                    send(("RL0", 0, 64), ("SL0", 0, 64), "l0")
             else:
                 SA = "SA%d" % v
                 tt(HK, HK, ("KK", 0, 32), A.mult)
@@ -450,14 +538,12 @@ def rank_program(g, core, T, topo):
                 ts((SA, 0, 64), ("MT", 0, 64), -OFF, A.add)
                 ts(WX, ("NI32", 64, 96), 512.0, A.mult)
                 tt((SA, 64, 96), WX, HK, A.add)
-                na = 256 if v == 0 else 160
-                send(("RA%d" % v, 0, na), (SA, 0, na), "a%d" % v)
-                send(("RB%d" % v, 0, K), ("SB%d" % v, 0, K), "b%d" % v)
-                if v == 1:
-                    tt(("P", 0, n1), bc(VB, i), ("H", 0, n1), A.mult)
-                    tt(("SL1", 0, n1), ("P", 0, n1), ("LG", 0, n1), A.add)
-                    send(("RL1", 0, n1), ("SL1", 0, n1), "l1")
+                send(("RA%d" % v, 0, 160), (SA, 0, 160), "a%d" % v)
+                tt(("P", 0, n1), bc(VB, i), ("H", 0, n1), A.mult)
+                tt(("SL%d" % v, 0, n1), ("P", 0, n1), ("LG", 0, n1), A.add)
+                send(("RL%d" % v, 0, n1), ("SL%d" % v, 0, n1), "l%d" % v)
 
+    arrange()
     for s in ("eV", "eS", "eP", "eG", "sent"):
         g.wait_ge(T.sem[s], cnt[s])
     for s, val in ends:

@@ -1,52 +1,58 @@
 from concourse.mybir import AluOpType as A, ActivationFunctionType as AF
+from concourse.bass import DstId, RemoteDMATransfer
 
 C, K, V_, S_ = 4096, 512, 3, 3
 O = 16
 FO = C + O
-NH = 2
-OFF = 2064.0
+W, L = K // 2, 16
 XCH = [0, 1280, 2560, 3584, 4096]
-FV, DV = (1,), (1,)
-GAT, HOP, SELF, LOOK, RATE = 1.8, 200, 100, 60, 300
+XAT = [9000, 10700, 17500, 18000]
+FAT = [("S", 6900), ("V", 5850), ("S", 8400), ("S", 10600)]
+DAT = [("S", 12100), ("S", 12200), ("S", 12600), ("S", 13100), ("S", 17600), ("S", 17700), ("S", 21500), ("S", 21600)]
+CYC, PE, GAT, HOP, LOOK, PART, RATE = 0.91, 0.46, 1.56, 100, 30, 0.5, 300
+TQ, NN, CU, WL, P0, PB_, QQ, MB, HH, U1, U0, P1, DL, J_, WP, WX, KK = 0, 1, 2, 3, 4, 6, 7, 8, 9, 10, 11, 12, 13, 14, 15, 16, 17
 
 SCRATCH = {
     "G": ("sbuf", [128, 2 * FO], "bfloat16"), "FP": ("sbuf", [128, C], "bfloat16"), "U": ("sbuf", [128, FO], "bfloat16"),
-    "P16": ("sbuf", [128, 256], "uint16"), "PM": ("sbuf", [128, 256], "int32"),
-    "XI": ("sbuf", [128, FO], "int32"), "XF": ("sbuf", [128, FO], "float32"),
-    "WT": ("sbuf", [128, 2 * K + O], "bfloat16"), "B0": ("sbuf", [128, K], "bfloat16"),
-    "M0": ("sbuf", [128, 32], "int32"), "PL": ("sbuf", [128, 256], "int32"),
+    "P16": ("sbuf", [128, 256], "uint16"), "PL": ("sbuf", [128, 256], "int32"), "PM": ("sbuf", [128, 256], "int32"),
     "PA": ("sbuf", [128, 256], "int32"), "PC": ("sbuf", [128, 256], "int32"),
     "HI": ("sbuf", [128, 256], "bfloat16"), "LO": ("sbuf", [128, 256], "bfloat16"),
+    "XI": ("sbuf", [128, C], "int32"), "XF": ("sbuf", [128, FO], "float32"),
+    "WT": ("sbuf", [128, 2 * K + O], "bfloat16"), "B0": ("sbuf", [128, K], "bfloat16"), "M0": ("sbuf", [128, 32], "int32"),
     "J": ("sbuf", [128, 144], "float32"), "QI": ("sbuf", [128, 8], "int32"), "COL": ("sbuf", [128, 16], "float32"),
     "TA": ("sbuf", [128, 128], "bfloat16"), "TC": ("sbuf", [128, 128], "bfloat16"),
     "TD": ("sbuf", [128, 128], "bfloat16"), "TE": ("sbuf", [128, 128], "bfloat16"), "TF": ("sbuf", [128, 128], "bfloat16"),
     "ZS": ("sbuf", [128, 128], "bfloat16"), "ZD": ("sbuf", [128, 128], "bfloat16"),
-    "ID": ("sbuf", [128, 128], "bfloat16"), "NI": ("sbuf", [128, 128], "bfloat16"),
-    "KO": ("sbuf", [128, 128], "bfloat16"), "PQ": ("sbuf", [128, 256], "float16"),
-    "WB": ("sbuf", [128, 144], "bfloat16"), "KC": ("sbuf", [128, 32], "float16"),
+    "ID": ("sbuf", [128, 128], "bfloat16"), "NI": ("sbuf", [128, 128], "bfloat16"), "KF": ("sbuf", [128, 128], "float16"),
+    "KB": ("sbuf", [128, 128], "bfloat16"), "KD": ("sbuf", [128, 128], "bfloat16"),
+    "IF": ("sbuf", [128, 128], "float32"), "NF": ("sbuf", [128, 128], "float32"),
+    "WB": ("sbuf", [128, 144], "bfloat16"), "WY": ("sbuf", [128, 144], "bfloat16"), "KC": ("sbuf", [128, 128], "float16"),
     "SL": ("sbuf", [128, 288], "bfloat16"), "BI": ("sbuf", [128, 18], "int32"), "BL": ("sbuf", [128, 18], "uint16"),
-    "KI": ("sbuf", [128, 32], "int32"), "KK": ("sbuf", [128, 32], "float32"),
-    "F": ("sbuf", [128, K], "bfloat16"), "F2": ("sbuf", [128, K], "bfloat16"), "X": ("sbuf", [128, K], "float32"),
-    "R1": ("sbuf", [128, 2 * K], "bfloat16"), "D": ("sbuf", [128, K], "bfloat16"), "Y": ("sbuf", [128, K], "float16"),
-    "GA": ("sbuf", [128, 9 * K], "bfloat16"), "BW": ("sbuf", [128, K], "bfloat16"), "EX": ("sbuf", [128, K], "bfloat16"),
-    "MT": ("sbuf", [128, 64], "int32"), "LS": ("sbuf", [128, 64], "uint16"),
-    "J1": ("sbuf", [128, 32], "uint16"), "WL": ("sbuf", [128, 32], "uint16"),
-    "N": ("sbuf", [128, 32 * 16], "float32"), "CN": ("sbuf", [128, 96], "bfloat16"), "NI32": ("sbuf", [128, 96], "int32"),
-    "H": ("sbuf", [128, 288], "bfloat16"), "P": ("sbuf", [128, 288], "float32"), "PR": ("sbuf", [128, 288], "float32"),
+    "KI": ("sbuf", [128, 32], "int32"), "L0I": ("sbuf", [128, 32], "uint16"),
+    "F": ("sbuf", [128, K], "bfloat16"), "F2": ("sbuf", [128, K], "bfloat16"), "D": ("sbuf", [128, K], "bfloat16"),
+    "X": ("sbuf", [128, K], "float32"), "Y": ("sbuf", [128, K], "float16"), "RU": ("sbuf", [128, 2, K], "bfloat16"),
+    "GA": ("sbuf", [128, 9 * K], "bfloat16"), "BW": ("sbuf", [128, K], "bfloat16"), "EX": ("sbuf", [128, 3 * K], "bfloat16"),
+    "ST": ("sbuf", [128, 18, 32], "float32"), "E": ("sbuf", [128, 4, 32], "bfloat16"), "SLOT": ("sbuf", [128, 32], "bfloat16"),
+    "LS": ("sbuf", [128, 32], "uint16"), "LT": ("sbuf", [128, 32], "uint16"), "LJ": ("sbuf", [128, 32], "uint16"),
+    "MI": ("sbuf", [128, 4, 32], "int32"),
+    "H0": ("sbuf", [128, 288], "bfloat16"), "H1": ("sbuf", [128, 288], "bfloat16"), "HC": ("sbuf", [128, 160], "bfloat16"),
+    "P": ("sbuf", [128, 288], "float32"), "PQ": ("sbuf", [128, 256], "float16"),
     "OB": ("sbuf", [128, K], "float32"), "OL": ("sbuf", [128, 288], "float32"), "OM": ("sbuf", [128, 32], "float32"),
     "OC": ("sbuf", [128, 32], "float32"),
 }
 for _v in range(V_ - 1):
-    for _n in ("SB", "RB", "RG"):
+    for _n in ("RB", "RG"):
         SCRATCH["%s%d" % (_n, _v)] = ("sbuf", [128, K], "bfloat16")
     for _n in ("SA", "RA"):
-        SCRATCH["%s%d" % (_n, _v)] = ("sbuf", [128, 160], "float16")
+        SCRATCH["%s%d" % (_n, _v)] = ("sbuf", [128, 5, 32], "uint16")
     for _n in ("SL", "RL"):
         SCRATCH["%s%d" % (_n, _v)] = ("sbuf", [128, 96 * (_v + 1)], "float16")
-PSUM = ["PB0", "PB1", "Z0", "Z1", "T1", "TU", "T2", "LG"]
+PSUM = ["PB0", "PB1", "Z0", "Z1", "L0", "L1", "TP", "LG"]
 for _n in PSUM:
     SCRATCH[_n] = ("psum", [128, 512], "float32")
-SEMAPHORES = ["eV", "eS", "eP", "eG", "sent", "a0", "a1", "b0", "b1", "l0", "l1", "g0", "g1"] + ["d%d" % i for i in range(24)]
+SCRATCH["TP"] = ("psum", [128, 16, 32], "float32")
+SEMAPHORES = (["eV", "eS", "eP", "eG", "sent"] + ["%s%d" % (n, v) for n in "abgl" for v in range(2)]
+              + ["d%d" % i for i in range(24)])
 
 
 def rank_program(g, core, T, topo):
@@ -60,28 +66,43 @@ def rank_program(g, core, T, topo):
     n_out, n_in = len(topo.engines(core, nxt)), len(topo.engines(prv, core))
     Q = {"V": g.vector, "S": g.scalar, "P": g.tensor, "G": g, "Y": g.sync}
     cnt = {"eV": 0, "eS": 0, "eP": 0, "eG": 0, "sent": 0}
-    known = {e: {} for e in list(Q) + ["dma"]}
+    known = {e: {} for e in Q}
     acc = {}
     ndma = [0]
     ends = []
     prog = []
+    sums, first = {}, {}
+    turn = [0, 0]
+
+    def t(x):
+        turn[1] = x
+
+    def put(e, emit, reads, writes, busy, line=0):
+        prog.append([e, emit, reads, writes, turn[0] + turn[1], busy, line])
+
+    def r2(name, lo, hi, step=1):
+        return (name, [(lo, hi)], -((lo - hi) // step), (slice(None), slice(lo, hi, step)), step == 1)
+
+    def r3(name, s0, s1, ss, c0, c1, cs=1):
+        wd = SCRATCH[name][1][2]
+        slots = list(range(s0, s1, ss))
+        ix = (slice(None), s0 if len(slots) == 1 else slice(s0, s1, ss), slice(c0, c1, cs))
+        return (name, [(s * wd + c0, s * wd + c1) for s in slots], len(slots) * -((c0 - c1) // cs), ix, cs == 1)
+
+    def ind(win, off):
+        return ("ind", win, 16 * off[2], off)
 
     def ap(r):
         if r[0] == "ind":
-            return ap(r[1]).indirect(ap(r[2]))
-        if len(r) == 4:
-            return T[r[0]][:, r[1]:r[2]:r[3]]
-        return T[r[0]][:, r[1]:r[2]]
+            return ap(r[1]).indirect(ap(r[3]))
+        return T[r[0]][r[3]]
 
     def spans(rs):
         out = []
         for r in rs:
-            if not isinstance(r, tuple):
-                continue
-            if r[0] == "ind":
-                out += [r[1], r[2]]
-            else:
-                out.append(r)
+            if isinstance(r, tuple):
+                for q in ([r[1], r[3]] if r[0] == "ind" else [r]):
+                    out += [(q[0], lo, hi, q[4]) for lo, hi in q[1]]
         return out
 
     def order(e, reads, writes):
@@ -107,102 +128,100 @@ def rank_program(g, core, T, topo):
                 if known[e].get(s2, 0) < v2:
                     known[e][s2] = v2
 
-    def note(e, reads, writes, tok):
+    def note(e, who, reads, writes, tok):
         clock = dict(known[e])
         for rs, w in ((reads, False), (writes, True)):
             for r in spans(rs):
                 lst = acc.setdefault(r[0], [])
-                if w:
-                    lst[:] = [a for a in lst if not (r[1] <= a[0] and a[1] <= r[2] and len(r) == 3)]
-                lst.append([r[1], r[2], w, e, tok, clock])
+                if w and r[3]:
+                    lst[:] = [a for a in lst if not (r[1] <= a[0] and a[1] <= r[2])]
+                lst.append([r[1], r[2], w, who, tok, clock])
 
-    def width(r):
-        if r[0] == "ind":
-            return 16 * (r[2][2] - r[2][1])
-        return -((r[1] - r[2]) // (r[3] if len(r) == 4 else 1))
-
-    def op(e, fn, out, ins, two=False):
+    def op(e, fn, out, ins):
         def emit():
             order(e, ins, [out])
             cnt["e" + e] += 1
             fn().then_inc(T.sem["e" + e], 1)
-            note(e, ins, [out], ("e" + e, cnt["e" + e]))
-        aps = [r for r in ins if isinstance(r, tuple) and r[0] in list(SCRATCH) + ["ind"]]
-        n = width(out)
+            note(e, e, ins, [out], ("e" + e, cnt["e" + e]))
+        aps = [r for r in ins if isinstance(r, tuple) and r[2] > 1]
+        n, two = out[2], e == "V" and len(aps) == 2
         if e == "P":
-            t = max(64, width(ins[1])) * 0.5
+            busy = max(64, ins[1][2]) * PE * (4 if SCRATCH[ins[1][0]][2] == "float32" else 1)
         elif e == "G":
-            t = 130 + 2 * n
+            busy = 130 + 2 * n * CYC
         elif any(r[0] == "ind" for r in aps):
-            t = 60 + GAT * n
+            busy = 85 + (2 if two else GAT) * n * CYC
         elif two:
-            t = max(64, n * (1 if any(r[0] in PSUM for r in aps) else 2))
-        elif e == "V" and all(SCRATCH[r[0]][2] in ("bfloat16", "float16", "uint16") for r in aps + [out] if width(r) > 1):
-            t = max(64, n * 0.5)
+            busy = 25 + max(64, n * (1 if any(r[0] in PSUM for r in aps) else 2)) * CYC
+        elif e == "V" and all(SCRATCH[r[0]][2] in ("bfloat16", "float16", "uint16") for r in aps + [out]):
+            busy = 25 + max(64, n * 0.5) * CYC
         else:
-            t = max(64, n)
-        prog.append([e, emit, ins, [out], t, t])
+            busy = 25 + max(64, n) * CYC
+        put(e, emit, ins, [out], busy)
 
     def arrange():
-        seen, deps = {}, []
+        seen, users, left, tail, deps = {}, [[] for _ in prog], [], {}, {}
         for k, (e, emit, reads, writes) in enumerate(a[:4] for a in prog):
             d = set()
+            if k in sums:
+                d.add(tail.get(sums[k][1], k))
+                tail[sums[k][1]] = k
             for rs, w in ((reads, False), (writes, True)):
                 for r in spans(rs):
                     for lo, hi, pw, pe, j in seen.get(r[0], []):
-                        if ((w or pw) and lo < r[2] and r[1] < hi) or (r[0] in PSUM and (pe != e or e == "P")):
+                        if (w or pw) and lo < r[2] and r[1] < hi:
                             d.add(j)
             for rs, w in ((reads, False), (writes, True)):
                 for r in spans(rs):
                     lst = seen.setdefault(r[0], [])
-                    if w and len(r) == 3:
+                    if w and r[3]:
                         lst[:] = [a for a in lst if not (r[1] <= a[0] and a[1] <= r[2])]
                     lst.append((r[1], r[2], w, e, k))
             d.discard(k)
-            deps.append(sorted(d))
-
-        def gap(j, k):
-            if prog[j][0] == prog[k][0] and prog[j][4] == prog[j][5]:
-                return 0 if prog[k][0] == "P" else SELF
-            return HOP
-        n = len(prog)
-        way, users = [0.0] * n, [[] for _ in range(n)]
-        for k in range(n - 1, -1, -1):
-            way[k] += prog[k][5]
+            if k in sums and sums[k][0] in ("TP", "L0"):
+                deps[sums[k][1]] = deps.get(sums[k][1], set()) | set(j for j in d if sums.get(j, (0, -1))[1] != sums[k][1])
+            deps[k] = deps.get(k, set()) | d
+        for k in range(len(prog)):
+            left.append(len(deps[k]))
             for j in deps[k]:
                 users[j].append(k)
-                way[j] = max(way[j], way[k] + gap(j, k))
-        left = [len(d) for d in deps]
-        ready = {e: [] for e in Q}
-        at = [0.0] * n
-        for k in range(n):
-            if not left[k]:
-                ready[prog[k][0]].append(k)
-        free = {e: 0.0 for e in Q}
-        wire = 0.0
-        for _ in range(n):
-            e = min((q for q in Q if ready[q]), key=lambda q: max(free[q], min(at[k] for k in ready[q])))
-            now = max(free[e], min(at[k] for k in ready[e]))
-            best = max((k for k in ready[e] if at[k] <= now + LOOK), key=lambda k: (1e9 if len(prog[k]) > 6 else way[k], -k))
-            ready[e].remove(best)
-            start = max(free[e], at[best])
-            free[e] = start + prog[best][4]
-            done = start + prog[best][5]
-            if len(prog[best]) > 6:
-                wire = max(wire, start + 1500) + prog[best][6]
-                done = wire + 500
+        ready = [k for k in range(len(prog)) if not left[k]]
+        banks = [set(r[0] for r in spans(a[2] + a[3]) if r[0] in PSUM) for a in prog]
+        held, used = {}, {}
+        at, free, wire = [0.0] * len(prog), {e: 0.0 for e in Q}, {"G": 0.0, "Y": 0.0}
+        while ready:
+            can = {}
+            for k in ready:
+                if all(held.get(b, -1) in (-1, sums.get(k, (0, -2))[1]) for b in banks[k]):
+                    since = max([at[k]] + [used[b][1] + HOP for b in banks[k] if b in used and used[b][0] != prog[k][0]])
+                    can.setdefault(prog[k][0], []).append((prog[k][4], k, since))
+            e = min(can, key=lambda q: max(free[q], min(c[2] for c in can[q])))
+            now = max(free[e], min(c[2] for c in can[e]))
+            pick = min(c for c in can[e] if c[2] <= now)
+            pick = min(c for c in can[e] if c[2] <= now + max(LOOK, PART * prog[pick[1]][5]))
+            best, start = pick[1], max(now, pick[2])
+            free[e] = done = start + prog[best][5]
+            if prog[best][6]:
+                line = "G" if e == "G" else "Y"
+                wire[line] = max(wire[line], start + 1500) + prog[best][6]
+                done = wire[line] + (800 if e == "G" else 500)
+            ready.remove(best)
+            for b in banks[best]:
+                used[b] = (e, done)
+            if best in sums:
+                held[sums[best][0]] = -1 if sums[best][2] else sums[best][1]
             prog[best][1]()
             for k in users[best]:
-                at[k] = max(at[k], done + gap(best, k))
+                at[k] = max(at[k], done + (0 if e == "P" == prog[k][0] else HOP))
                 left[k] -= 1
                 if not left[k]:
-                    ready[prog[k][0]].append(k)
+                    ready.append(k)
 
     def sc(x):
         return ap(x) if isinstance(x, tuple) else x
 
     def tt(out, a, b, o):
-        op("V", lambda: g.vector.tensor_tensor(ap(out), ap(a), ap(b), o), out, [a, b], True)
+        op("V", lambda: g.vector.tensor_tensor(ap(out), ap(a), ap(b), o), out, [a, b])
 
     def ts(out, a, s1, o0, s2=None, o1=None):
         if o1 is None:
@@ -223,325 +242,411 @@ def rank_program(g, core, T, topo):
             op("S", lambda: g.scalar.activation(ap(out), ap(a), func, bias=ap(bias), scale=scale), out, [a, bias])
 
     def mm(out, w, x, start, stop):
+        if start:
+            first[out[0]] = len(prog)
+        sums[len(prog)] = (out[0], first[out[0]], stop)
         op("P", lambda: g.tensor.matmul(ap(out), ap(w), ap(x), start, stop), out, [w, x])
 
-    def iota(out, pat, base, ch, small, after=()):
+    def iota(out, pat, base, ch, small):
         if small:
-            op("G", lambda: g.iota(ap(out), pat, base, ch, allow_small_or_imprecise_dtypes=True), out, list(after))
+            op("G", lambda: g.iota(ap(out), pat, base, ch, allow_small_or_imprecise_dtypes=True), out, [])
         else:
             op("G", lambda: g.iota(ap(out), pat, base, ch), out, [])
 
-    def dma(e, out_ap, in_ap, reads, writes, nbytes):
+    def dma(e, out_ap, in_ap, reads, writes):
         def emit():
             order(e, reads, writes)
             s = "d%d" % ndma[0]
             ndma[0] += 1
             Q[e].dma_start(out_ap, in_ap).then_inc(T.sem[s], 16)
-            note("dma", reads, writes, (s, 16))
+            note(e, "dma", reads, writes, (s, 16))
             ends.append((s, 16))
-        prog.append([e, emit, reads, writes, 60, 2000 + nbytes / RATE, nbytes / RATE])
+        r = (reads + writes)[0]
+        put(e, emit, reads, writes, 60, r[2] * (2 if SCRATCH[r[0]][2] == "bfloat16" else 4) * 128 / RATE)
 
-    def send(dst, src, sem):
+    def send(dst, srcs, sem):
         def emit():
-            order("G", [src], [])
-            g.remote_dma(ap(dst), ap(src), T.sem[sem], T.sem["sent"], pid, rid, mask_out)
+            order("G", srcs, [])
+            if len(srcs) == 1:
+                g.remote_dma(ap(dst), ap(srcs[0]), T.sem[sem], T.sem["sent"], pid, rid, mask_out)
+            else:
+                g.remote_dma_fused([RemoteDMATransfer(dst_ids=[DstId(rid=rid, pnc=pid)], dma_engine_mask=mask_out, remote_sem=T.sem[sem],
+                                                      srcs=[ap(r) for r in srcs], dsts=[ap(dst)], alu_op=1)], local_sem=T.sem["sent"])
             cnt["sent"] += n_out
-            acc.setdefault(dst[0], []).append([dst[1], dst[2], True, "rem", (sem, n_in), {}])
+            acc.setdefault(dst[0], []).append([dst[1][0][0], dst[1][-1][1], True, "rem", (sem, n_in), {}])
             ends.append((sem, n_in))
-        prog.append(["G", emit, [src], [dst], 500, 2500 + 3.2 * width(src)])
-
-    def ind(win, off):
-        return ("ind", win, off)
-
-    def nn(i):
-        return ("N", 32 * i, 32 * i + 32)
+        put("G", emit, srcs, [dst], 400, 2.0 * dst[2])
 
     def col(i):
-        return ("COL", i, i + 1)
+        return r2("COL", i, i + 1)
 
     def M(n):
-        return (n, 0, 128)
+        return r2(n, 0, 128)
 
-    W = K // NH
-    hs = [(h, h * W, (h + 1) * W) for h in range(NH)]
-    FW, GW, UW, XW, XIW = ("G", FO, 2 * FO), ("G", 0, 2 * FO), ("U", 0, FO), ("XF", 0, FO), ("XI", 0, FO)
-    MU, TAU = ("MT", 0, 32), ("MT", 32, 64)
-    C1, NN, SLOT = ("CN", 0, 32), ("CN", 32, 64), ("CN", 64, 96)
-    E0, E1, J2F, J1F, P1, NB, BK, BM, QQ, RR, VA, VB, HK, WX, P0, M4 = [nn(i) for i in range(16)]
-    CNT, UP, TP, VP = ("T1", 0, 32), ("TU", 0, 32), ("TU", 32, 64), ("T2", 0, 32)
+    def ls(name, s=0, n=1):
+        return r3(name, s, s + n, 1, 0, 32)
+
+    def st(s, n=1):
+        return ls("ST", s, n)
+
+    def fl(i, s=0, n=2):
+        return ls("E", 2 * (i % 2) + s, n)
+
+    def wide(name, h, at=0):
+        return r2(name, at + W * h, at + W * h + W)
+
+    def block(name, j):
+        return r2(name, K * j, K * j + K)
+
+    def logged(i):
+        return st(P0 + i % 2)
+
+    FW, GW, XW, UW = r2("G", 0, FO), r2("G", 0, 2 * FO), r2("XF", 0, FO), r2("U", 0, FO)
+    MU, SLOT = ls("MI"), r2("SLOT", 0, 32)
+    PB = [r2("PB%d" % h, 0, W) for h in range(2)]
+    CNT, UP = r2("L0", 0, 32), r2("L0", 32, 64)
+    BELOW, AT, LEN, CUR = [ls("TP", s) for s in range(4)]
 
     for q in range(2):
-        dma("Y", T.PL[:, 128 * q:128 * q + 128], T.nx[0:128:16, 2048 * q:2048 * q + 2048], [], [("PL", 128 * q, 128 * q + 128)], 512 * 128)
-    dma("S", T.M0[:, :], T.m0[:, :], [], [("M0", 0, 32)], 512 * 32)
-    dma("Y", ap(("G", FO + O, 2 * FO)), T.fm[:, :], [], [("G", FO + O, 2 * FO)], 256 * C)
-    dma("Y", T.B0[:, :], T.b0[:, :], [], [("B0", 0, K)], 256 * K)
+        dma("Y", T.PL[:, 128 * q:128 * q + 128], T.nx[0:128:16, 2048 * q:2048 * q + 2048], [], [r2("PL", 128 * q, 128 * q + 128)])
+    dma("S", T.M0[:, :], T.m0[:, :], [], [r2("M0", 0, 32)])
+    dma("Y", ap(r2("G", O, FO)), T.fm[:, :], [], [r2("G", O, FO)])
+    dma("Y", T.B0[:, :], T.b0[:, :], [], [r2("B0", 0, K)])
     for a, b in zip(XCH[:-1], XCH[1:]):
-        dma("Y", ap(("XI", O + a, O + b)), T.nx[:, a:b], [], [("XI", O + a, O + b)], 512 * (b - a))
-    dma("Y", ap(("WT", O, O + 2 * K)), T.wl[:, :], [], [("WT", O, O + 2 * K)], 512 * K)
+        dma("Y", ap(r2("XI", a, b)), T.nx[:, a:b], [], [r2("XI", a, b)])
+    dma("Y", ap(r2("WT", O, O + 2 * K)), T.wl[:, :], [], [r2("WT", O, O + 2 * K)])
 
-    iota(("QI", 0, 1), [[0, 1]], 0, 1, False)
-    iota(("J", 0, 144), [[1, 144]], 0, 0, True)
-    iota(("PM", 0, 256), [[2048, 2], [1, 128]], 0, 128, False)
-    iota(("BI", 0, 18), [[0, 9], [16, 2]], 0, 0, False)
-    iota(("KI", 0, 32), [[16, 32]], O, 0, False)
-    iota(("SL", 0, 288), [[1, 9], [0, 32]], 1, 0, True)
-    iota(UW, [[0, FO]], 0, 0, True, [("SL", 0, 288), ("PM", 0, 256), ("KI", 0, 32), ("BI", 0, 18), ("J", 0, 144), ("QI", 0, 1)])
-    ms(("G", 0, O), 0.0)
-    ms(("G", FO, FO + O), 0.0)
-    ms(("XI", 0, O), 0)
-    ms(("XF", 0, O), 0.0)
-    ms(("WT", 0, O), 0.0)
+    iota(r2("QI", 0, 1), [[0, 1]], 0, 1, False)
+    iota(r2("J", 0, 144), [[1, 144]], 0, 0, True)
+    iota(r2("PM", 0, 256), [[2048, 2], [1, 128]], 0, 128, False)
+    iota(r2("BI", 0, 18), [[0, 9], [16, 2]], 0, 0, False)
+    iota(r2("KI", 0, 32), [[16, 32]], 1, 0, False)
+    iota(r2("SL", 0, 288), [[1, 9], [0, 32]], 1, 0, True)
+    iota(UW, [[0, FO]], 0, 0, True)
+    ms(r2("G", 0, O), 0.0)
+    ms(r2("G", FO, FO + O), 0.0)
+    ms(r2("XF", 0, O), 0.0)
+    ms(r2("WT", 0, O), 0.0)
     ms(col(9), -255.0)
     ms(col(10), 255.0)
-    ts(("QI", 1, 2), ("QI", 0, 1), 15, A.bitwise_and)
-    cp(col(0), ("QI", 1, 2))
-    tt(col(1), ("QI", 0, 1), ("QI", 1, 2), A.subtract)
-    ts(col(3), col(0), 0.0, A.is_gt, 64.0, A.mult)
-    ts(col(4), col(0), 0.0, A.is_equal, 1.0 / 128, A.mult)
+    ms(col(11), 2047.0)
+    ms(ls("TP", 0, 4), 0.0)
+    ms(LEN, 1.0)
+    t(100)
+    ts(r2("QI", 1, 2), r2("QI", 0, 1), 15, A.bitwise_and)
+    for j, x in enumerate((0.5, 0.0, 481.0, 2048.0 + FO)):
+        ts(r2("KC", 32 * j, 32 * j + 32), r2("J", 0, 32), 0.0, A.mult, x, A.add)
+    tt(col(1), r2("QI", 0, 1), r2("QI", 1, 2), A.subtract)
+    cp(col(0), r2("QI", 1, 2))
+    ms(st(TQ), 0.0)
+    ts(M("TA"), M("J"), col(1), A.subtract)
+    ts(col(3), col(0), 0.0, A.is_gt, 0.5, A.mult)
     ts(col(6), col(0), 15.0, A.is_equal, 0.5, A.mult)
     ts(col(2), col(1), 15.0, A.add)
-    ts(col(3), col(3), 64.0, A.add)
-    ts(col(4), col(4), 1.0 / 128, A.add)
-    ts(col(7), col(6), 2048.0, A.mult, 255.0, A.add)
-    ts(col(5), col(4), -2048.0, A.mult)
-    ts(M("TA"), M("J"), col(1), A.subtract)
-    ts(("WB", 0, 144), ("J", 0, 144), col(2), A.is_equal, col(3), A.mult)
     ts(M("ID"), M("TA"), col(0), A.is_equal)
     ts(M("TC"), M("TA"), col(0), A.is_gt)
     ts(M("TD"), M("TA"), 0.0, A.is_ge, 64.0, A.mult)
-    ts(M("TE"), M("TA"), 0.0, A.is_equal, 64.0, A.mult)
     ts(M("TF"), M("TA"), 15.0, A.is_le)
-    tt(M("TD"), M("TD"), M("TE"), A.add)
-    ts(M("NI"), M("ID"), -1.0, A.mult)
-    ts(M("KO"), M("ID"), OFF, A.mult)
-    tt(M("TD"), M("TD"), M("TF"), A.mult)
-    ts(M("TE"), M("ID"), 16.0, A.mult, -1.0, A.add)
-    ts(M("TF"), M("TC"), -14.0, A.mult)
-    tt(M("TC"), M("ID"), M("TC"), A.subtract)
-    tt(M("TE"), M("TE"), M("TF"), A.add)
-    ts(M("TC"), M("TC"), col(6), A.subtract)
-    tt(M("ZS"), M("TE"), M("TD"), A.mult)
-    tt(M("ZD"), M("TC"), M("TD"), A.mult)
-    ts(("KC", 0, 32), ("J", 0, 32), 0.0, A.mult, 6160.0, A.add)
-    ts(("BL", 0, 18), ("BI", 0, 18), col(0), A.add)
-    ts(("KK", 0, 32), ("KI", 0, 32), col(0), A.add)
-    ts(("LS", 0, 32), ("M0", 0, 32), float(O), A.add)
-    ts(MU, ("M0", 0, 32), float(O), A.add)
-    ts(("EX", 0, K), ("B0", 0, K), -1.0, A.mult, 255.0, A.add)
-    ts(("P16", 0, 256), ("PL", 0, 256), float(O), A.add)
+    ts(col(3), col(3), 0.5, A.add)
+    ts(col(7), col(6), 2048.0, A.mult, 255.0, A.add)
+    ts(col(5), col(6), -1.0, A.mult)
+    ts(col(4), col(0), 0.0, A.mult, -1.0, A.add)
     ts(col(8), col(1), 128.0, A.mult)
-    tt(("PA", 0, 256), ("PL", 0, 256), ("PM", 0, 256), A.subtract)
-    ts(("PA", 0, 256), ("PA", 0, 256), col(8), A.add)
-    ts(("PC", 0, 256), ("PA", 0, 256), 6, A.arith_shift_right)
-    ts(("PA", 0, 256), ("PA", 0, 256), 63, A.bitwise_and)
-    cp(("HI", 0, 256), ("PC", 0, 256))
-    ts(("LO", 0, 256), ("PA", 0, 256), 1.0 / 128, A.mult)
+    for name, times in (("NI", -1.0), ("KB", -2.0 ** 24), ("KD", 30720.0), ("IF", 1.0), ("NF", -1.0)):
+        act(M(name), M("ID"), AF.Copy, None, times)
+    tt(M("TD"), M("TD"), M("TF"), A.mult)
+    act(M("TE"), M("ID"), AF.Identity, col(4), 16.0)
+    act(M("TF"), M("TC"), AF.Copy, None, -14.0)
+    tt(M("TC"), M("ID"), M("TC"), A.subtract)
+    ts(r2("WB", 0, 144), r2("J", 0, 144), col(2), A.is_equal, col(3), A.mult)
+    ts(r2("WY", 0, 144), r2("J", 0, 144), col(2), A.is_equal, 128.0, A.mult)
+    act(M("TC"), M("TC"), AF.Identity, col(5))
+    tt(M("TE"), M("TE"), M("TF"), A.add)
+    ts(M("KF"), M("ID"), float(FO), A.mult)
+    tt(M("ZD"), M("TC"), M("TD"), A.mult)
+    tt(M("ZS"), M("TE"), M("TD"), A.mult)
+    ts(r2("P16", 0, 256), r2("PL", 0, 256), float(O), A.add)
+    ts(r2("LS", 0, 32), r2("M0", 0, 32), float(O), A.add)
+    tt(r2("PA", 0, 256), r2("PL", 0, 256), r2("PM", 0, 256), A.subtract)
+    cp(r2("L0I", 0, 32), r2("M0", 0, 32))
+    ts(r2("PA", 0, 256), r2("PA", 0, 256), col(8), A.add)
+    ts(MU, r2("M0", 0, 32), 1.0, A.add)
+    ts(r2("PC", 0, 256), r2("PA", 0, 256), 6, A.arith_shift_right)
+    ts(r2("PA", 0, 256), r2("PA", 0, 256), 63, A.bitwise_and)
+    ms(st(NN), 1.0)
+    ms(st(HH), 0.0)
+    t(7350)
+    ts(block("EX", 0), r2("B0", 0, K), -1.0, A.mult, 255.0, A.add)
+    for h in range(2):
+        mm(PB[h], M("NI"), wide("EX", h), True, True)
+    t(10500)
+    ts(r2("HI", 0, 256), r2("PC", 0, 256), 128.0, A.mult)
+    cp(r2("LO", 0, 256), r2("PA", 0, 256))
+    ts(r2("BL", 0, 18), r2("BI", 0, 18), col(0), A.add)
+    ts(st(KK), r2("KI", 0, 32), col(0), A.add)
     for q in range(2):
         a, b = O + 2048 * q, O + 2048 * q + 2048
-        dma("Y", T.U[0:128:16, a:b], T.HI[:, 128 * q:128 * q + 128], [("HI", 0, 256), UW], [("U0", q, q + 1)], 256 * 128)
-        dma("Y", T.U[1:128:16, a:b], T.LO[:, 128 * q:128 * q + 128], [("LO", 0, 256), UW], [("U1", q, q + 1)], 256 * 128)
+        for row, name in enumerate(("HI", "LO")):
+            dma("Y", T.U[row:128:16, a:b], T[name][:, 128 * q:128 * q + 128], [r2(name, 0, 256), UW], [r2("PM", 2 * q + row, 2 * q + row + 1)])
+    for a, b, x in zip(XCH[:-1], XCH[1:], XAT):
+        t(x)
+        ts(r2("XF", O + a, O + b), r2("XI", a, b), 1.0 / 128, A.mult, -2047.0 / 128, A.add)
 
-    def refunds():
-        for q in range(4):
-            (cp if q in FV else act)(("FP", 1024 * q, 1024 * q + 1024), ind(FW, ("P16", 64 * q, 64 * q + 64)))
-        for k in range(8):
-            bk, q = ("TU", "LG")[k % 2], k // 4
-            for r in range(4):
-                a = 512 * k + 128 * r
-                mm((bk, 128 * r, 128 * r + 128), M("NI"), ("G", FO + O + a, FO + O + a + 128), True, False)
-                mm((bk, 128 * r, 128 * r + 128), M("ID"), ("FP", 2048 * q + 4 * (k % 4) + r, 2048 * q + 2048, 16), False, True)
-            (cp if k in DV else act)(("G", O + 512 * k, O + 512 * k + 512), (bk, 0, K))
-
-    def xconv(j):
-        a, b = XCH[j], XCH[j + 1]
-        ts(("XF", O + a, O + b), ("XI", O + a, O + b), col(4), A.mult, col(5), A.add)
-
-    def tolist(out, buf, lo, hi, first):
-        for r in range(16):
-            mm(out, ("WB", 15 - r, 143 - r), (buf, lo + r, hi, 16), first and r == 0, r == 15)
+    for q, (e, x) in enumerate(FAT):
+        t(x)
+        (cp if e == "V" else act)(r2("FP", 1024 * q, 1024 * q + 1024), ind(FW, r2("P16", 64 * q, 64 * q + 64)))
+    for k, (e, x) in enumerate(DAT):
+        bk, q = ("L1", "LG")[k % 2], k // 4
+        t(x - 600)
+        for r in range(4):
+            a = O + 512 * k + 128 * r
+            mm(r2(bk, 128 * r, 128 * r + 128), M("NI"), r2("G", a, a + 128), True, False)
+            mm(r2(bk, 128 * r, 128 * r + 128), M("ID"), r2("FP", 2048 * q + 4 * (k % 4) + r, 2048 * q + 2048, 16), False, True)
+        t(x)
+        (cp if e == "V" else act)(r2("G", FO + O + 512 * k, FO + O + 512 * k + 512), r2(bk, 0, K))
 
     def bc(win, n):
-        return win if n == 1 else ind(win, ("BL", 0, 2 * n))
+        return ind(win, r2("BL", 0, 2 * n))
 
-    def lst(name, lo, hi):
-        return (name, lo // 16, hi // 16)
+    def onehot(H, n, terms, at_p, at_v):
+        t(at_p)
+        a = min(W, K - 32 * n)
+        for j in range(n):
+            for k, (w, x) in enumerate(terms):
+                mm(r2("Z1", a + 32 * j, a + 32 + 32 * j), M(w), x, k == 0, k == len(terms) - 1)
+        t(at_v)
+        tt(r2(H, 0, 32 * n), r2("Z1", a, a + 32 * n), r2("SL", 0, 32 * n), A.is_equal)
 
-    bank = 0
-    for v in range(V_):
-        if v > 0:
-            RB, RA = "RB%d" % (v - 1), "RA%d" % (v - 1)
-            ms(("LG", 96 * v, 96 * v + 96), -OFF)
-            ts(("LS", 0, 64), (RA, 0, 64), OFF, A.add)
-            if v == 1:
-                cp(("WL", 0, 32), (RA, 64, 96))
-            else:
-                tt(WX, (RA, 64, 96), ("RA0", 64, 96), A.not_equal)
-                tt(WX, WX, (RA, 64, 96), A.mult)
-                cp(("WL", 0, 32), WX)
-            cp(("BW", 0, K), ind(("WT", 0, O + 2 * K), ("WL", 0, 32)))
-            mm(("PB%d" % bank, 0, K), M("NI"), (RB, 0, K), True, False)
-            mm(("PB%d" % bank, 0, K), M("NI"), ("RG%d" % (v - 1), 0, K), False, False)
-            mm(("PB%d" % bank, 0, K), M("ID"), ("BW", 0, K), False, True)
-            ts(M4, (RA, 0, 32), OFF + FO, A.add)
-            ts(("MT", 0, 64), (RA, 0, 64), OFF, A.add)
-            cp(("CN", 0, 64), (RA, 96, 160))
-            cp(("LG", 0, 96 * v), ("RL%d" % (v - 1), 0, 96 * v))
+    def look(H, n, at_v, at_p):
+        t(at_v)
+        tt(r2("PQ", 0, 32 * n), r2(H, 32, 32 * n + 32), r2("LG", 0, 32 * n), A.mult)
+        t(at_p)
+        mm(BELOW, M("ID"), r2("KC", 96, 128), True, False)
+        for j in range(n):
+            mm(BELOW, M("ID"), r2("PQ", 32 * j, 32 * j + 32), False, j == n - 1)
+
+    def tolist(s0, s1):
+        out = r2("L0", 32 * s0, 32 * s1)
+        if s0 == 0:
+            mm(out, M("ID"), r2("KC", 0, 32 * s1), True, False)
+        for r in range(16):
+            mm(out, r2("WB", 15 - r, 143 - r), r3("RU", s0, s1, 1, r, K, 16), s0 > 0 and r == 0, r == 15)
+
+    def write(i, at):
+        n, v = 32 * i, (i - 1) // S_
+        t(at[0])
+        tt(st(P1), UP, fl(i, 0, 1), A.mult)
+        t(at[1])
+        tt(st(DL), st(P1), logged(i), A.add)
+        t(at[2])
+        tt(r2("P", 0, n), bc(st(DL), i), r2("H%d" % (i % 2), 0, n), A.mult)
+        t(at[3])
+        if i == S_ * V_:
+            tt(r2("OL", 0, n), r2("P", 0, n), r2("LG", 0, n), A.add)
+            dma("Y", T.yl[:, :], T.OL[:, :], [r2("OL", 0, 288)], [])
+        elif i % S_:
+            tt(r2("LG", 0, n), r2("P", 0, n), r2("LG", 0, n), A.add)
         else:
-            mm(("PB%d" % bank, 0, K), M("NI"), ("EX", 0, K), True, True)
-        terms = [("NI", ("EX", 0, K))]
+            tt(r2("SL%d" % v, 0, n), r2("P", 0, n), r2("LG", 0, n), A.add)
+            send(r2("RL%d" % v, 0, n), [r2("SL%d" % v, 0, n)], "l%d" % v)
 
-        for st in range(S_):
-            i = S_ * v + st + 1
-            last, fin = st == S_ - 1, i == S_ * V_
-            PB, PN = "PB%d" % bank, ("PB%d" % (1 - bank), 0, K)
-            if fin or not last:
-                bank = 1 - bank
-            GA = ("GA", K * (i - 1), K * i)
-            fresh = st == 0 and v > 0
-            if not fresh and (fin or not last):
-                for j, (w, x) in enumerate(terms):
-                    mm(PN, M(w), x, j == 0, False)
-            for h, lo, hi in hs:
-                act(("F", lo, hi), ind(FW, lst("LS", lo, hi)), AF.Identity, col(9))
+    def step(i):
+        s, v = (i - 1) % S_, (i - 1) // S_
+        fresh, last, fin = i > 1 and s == 0, s == S_ - 1, i == S_ * V_
+        hand = last and not fin
+        owed = i > 2 and not fresh
+        RA, SA, EX = "RA%d" % (v - 1), "SA%d" % v, block("EX", v)
+        turn[0] = 5900 if i == 1 else 10000 * i
+        if fresh:
+            for h in range(2):
+                t(100 + 420 * h)
+                cp(wide("BW", h), ind(r2("WT", 0, O + 2 * K), r3(RA, 3, 4, 1, L * h, L * h + L)))
+            for h in range(2):
+                t(50)
+                mm(PB[h], M("NI"), wide("RB%d" % (v - 1), h), True, False)
+                mm(PB[h], M("NI"), wide("RG%d" % (v - 1), h), False, False)
+                t(550 + 420 * h)
+                mm(PB[h], M("ID"), wide("BW", h), False, True)
+            t(950)
+            ts(st(TQ, 3), ls(RA, 0, 3), 1.0 - O, A.add)
+            t(1300)
+            ts(MU, ls(RA, 4), 1.0 - O, A.add)
+            ts(r2("LT", 0, 32), ls(RA, 0), -float(FO), A.add)
+            t(1400)
+            act(st(HH), st(CU), AF.Sign)
+            t(1050)
+            mm(ls("TP", 1, 3), M("IF"), st(TQ, 3), True, True)
+            t(3300)
+            cp(r2("LG", 0, 96 * v), r2("RL%d" % (v - 1), 0, 96 * v))
+        if hand:
+            t(0)
+            send(r2("RB%d" % v, 0, K), [EX, block("GA", i - 3), block("GA", i - 2)], "b%d" % v)
+        lst = [r3(RA, 4, 5, 1, L * h, L * h + L) if fresh else r2("LS", L * h, L * h + L) for h in range(2)]
+        late = 7400 if i == 1 else 0
+        for h in range(2):
+            t(100 + 440 * h)
+            act(wide("F", h), ind(FW, lst[h]), AF.Identity, col(9))
+            t(980 + 430 * h + late)
             if i > 1:
-                act(("R1", K, 2 * K), ind(UW, ("LS", 32, 64)), after=[("U0", 0, 2), ("U1", 0, 2)])
-                act(("X", 0, K), ind(XW, ("LS", 0, 32)))
-            for h, lo, hi in hs:
-                tt(("R1", lo, hi), ("F", lo, hi), (PB, lo, hi), A.is_gt)
-            for h, lo, hi in hs:
-                ts(("F2", lo, hi), ("F", lo, hi), 2.0, A.mult, col(7), A.add)
-                tt(("D", lo, hi), ("F2", lo, hi), (PB, lo, hi), A.is_gt)
-            if fresh:
-                act(("EX", 0, K), (PB, 0, K), AF.Relu, None, -1.0)
-            if last and not fin:
-                act(("SB%d" % v, 0, K), (PB, 0, K), AF.Copy, None, -1.0)
-                send(("RB%d" % v, 0, K), ("SB%d" % v, 0, K), "b%d" % v)
-            tolist(CNT, "R1", 0, K, True)
-            for h, lo, hi in hs:
-                mm(("Z%d" % h, 0, W), M("ZS"), ("R1", lo, hi), True, False)
-                mm(("Z%d" % h, 0, W), M("ZD"), ("D", lo, hi), False, True)
-            if i > 1:
-                tolist(UP, "R1", K, 2 * K, True)
-            mm(VP, M("ID"), ("KC", 0, 32), True, False)
-
-            def ycall():
-                for h, lo, hi in hs:
-                    tt(("Y", lo, hi), ("X", lo, hi), ("Z%d" % h, 0, W), A.min)
-                tolist(VP, "Y", 0, K, False)
-
-            if i == 1:
-                xconv(0)
-                ts(E0, CNT, 0.0, A.is_equal)
-                tt(P0, E0, MU, A.mult)
-                cp(C1, E0)
-                cp(("J1", 0, 32), P0)
-                cp(("LS", 32, 64), P0)
-                act(GA, ind(FW, ("J1", 0, 32)))
-                mm(PN, M("NI"), GA, False, True)
-                terms.append(("NI", GA))
-                cp(TAU, P0)
-                cp(NN, E0)
-                for j in range(1, len(XCH) - 2):
-                    xconv(j)
-                for h, lo, hi in hs:
-                    ts(("X", lo, hi), ind(XIW, lst("LS", lo, hi)), col(4), A.mult, col(5), A.add)
-                ycall()
-                xconv(len(XCH) - 2)
-                cp(("NI32", 0, 32), VP)
-                ts(MU, ("NI32", 0, 32), 8191, A.bitwise_and)
-                cp(("LS", 0, 32), MU)
-                ts(M4, MU, float(FO), A.add)
-                refunds()
-                ms(("LG", 32, 96), -OFF)
-                ts(("LG", 0, 32), P0, -OFF, A.add)
-                continue
-
-            n0, n1 = 32 * (i - 1), 32 * i
-            ts(E1, CNT, 64.0, A.is_equal)
-            ts(E0, CNT, 0.0, A.is_equal)
-            tt(J2F, E1, TAU, A.mult)
-            tt(J1F, E0, M4, A.mult)
-            tt(J1F, J1F, J2F, A.add)
-            cp(("J1", 0, 32), J1F)
-            act(GA, ind(GW, ("J1", 0, 32)))
-            if last and not fin:
-                send(("RG%d" % v, 0, K), GA, "g%d" % v)
-            ycall()
-            tt(P0, E0, MU, A.mult)
-            tt(P1, E1, UP, A.mult)
-            tt(NN, NN, E0, A.add)
-            tt(QQ, NN, E0, A.mult)
-            if fresh:
-                mm(PN, M("NI"), ("EX", 0, K), True, False)
-            tt(SLOT, QQ, C1, A.max)
-            ts(NB, J2F, 0.0, A.is_equal)
-            tt(RR, C1, E1, A.subtract)
-            terms += [("NI", GA)]
-            tt(VB, P0, P1, A.add)
-            tt(("H", 0, n1), bc(SLOT, i), ("SL", 0, n1), A.is_equal)
-            if fin:
-                mm(PN, M("NI"), GA, False, True)
-                tt(("P", 0, n1), bc(VB, i), ("H", 0, n1), A.mult)
-                tt(BM, VP, MU, A.subtract)
-                tt(("PR", 0, n1), ("P", 0, n1), ("LG", 0, n1), A.add)
-                tt(BM, BM, NB, A.mult)
-                ts(("OL", 0, 288), ("PR", 0, 288), OFF - O, A.add, -1.0, A.max)
-                dma("Y", T.yl[:, :], T.OL[:, :], [("OL", 0, 288)], [], 512 * 288)
-                tt(("NI32", 0, 32), BM, MU, A.add)
-                tt(C1, QQ, RR, A.max)
-                ts(MU, ("NI32", 0, 32), 8191, A.bitwise_and)
-                ts(("OC", 0, 32), C1, -1.0, A.add)
-                ts(("OM", 0, 32), MU, -float(O), A.add)
-                dma("Y", T.yc[:, :], T.OC[:, :], [("OC", 0, 32)], [], 512 * 32)
-                dma("Y", T.ym[:, :], T.OM[:, :], [("OM", 0, 32)], [], 512 * 32)
-                act(("OB", 0, K), PN, AF.Identity, col(10))
-                dma("S", T.yb[:, :], T.OB[:, :], [("OB", 0, K)], [], 512 * K)
-                continue
-            if i > 2:
-                tt(("PQ", 0, n0 - 32), ("H", 32, n0), ("LG", 0, n0 - 32), A.mult)
-                for j in range(i - 2):
-                    mm(TP, M("KO"), ("H", 32 * j + 32, 32 * j + 64), j == 0, False)
-                for j in range(i - 2):
-                    mm(TP, M("ID"), ("PQ", 32 * j, 32 * j + 32), False, j == i - 3)
-            if not last:
-                mm(PN, M("NI"), GA, False, True)
-            tt(BM, VP, MU, A.subtract)
-            ts(BK, CNT, 128.0, A.is_ge)
-            tt(BM, BM, NB, A.mult)
-            tt(C1, QQ, RR, A.max)
-            tt(("NI32", 0, 32), BM, MU, A.add)
-            tt(BK, BK, TAU, A.mult)
-            ts(MU, ("NI32", 0, 32), 8191, A.bitwise_and)
-            tt(BK, BK, P0, A.add)
-            if not last:
-                cp(("LS", 0, 32), MU)
-                ts(M4, MU, float(FO), A.add)
+                act(wide("X", h), ind(XW, lst[h]))
             else:
-                cp(("SA%d" % v, 96, 160), ("CN", 0, 64))
-            if i == 2:
-                cp(("LS", 32, 64), BK)
-                cp(TAU, BK)
+                ts(wide("X", h), ind(r2("XI", 0, C), r2("L0I", L * h, L * h + L)), 1.0 / 128, A.mult, -2047.0 / 128, A.add)
+        for h in range(2):
+            Z, R1 = r2("Z%d" % h, 0, W), r3("RU", 0, 1, 1, W * h, W * h + W)
+            t((1000, 1075)[h] if fresh else (640, 1075)[h])
+            tt(R1, wide("F", h), PB[h], A.is_gt)
+            t((880, 1300)[h])
+            if h == 1 and i > 1:
+                t(976)
+                act(wide("F2", h), wide("F", h), AF.Identity, col(7), 2.0)
             else:
-                tt(VA, E1, TP, A.mult)
-                if last:
-                    ts(HK, C1, 0.0, A.is_gt)
-                tt(TAU, VA, BK, A.add)
-            if not last:
-                if i > 2:
-                    cp(("LS", 32, 64), TAU)
-                tt(("P", 0, n1), bc(VB, i), ("H", 0, n1), A.mult)
-                tt(("LG", 0, n1), ("P", 0, n1), ("LG", 0, n1), A.add)
-            else:
-                SA = "SA%d" % v
-                tt(HK, HK, ("KK", 0, 32), A.mult)
-                ts(("NI32", 64, 96), TAU, 1, A.bitwise_and)
-                ts((SA, 0, 64), ("MT", 0, 64), -OFF, A.add)
-                ts(WX, ("NI32", 64, 96), 512.0, A.mult)
-                tt((SA, 64, 96), WX, HK, A.add)
-                send(("RA%d" % v, 0, 160), (SA, 0, 160), "a%d" % v)
-                tt(("P", 0, n1), bc(VB, i), ("H", 0, n1), A.mult)
-                tt(("SL%d" % v, 0, n1), ("P", 0, n1), ("LG", 0, n1), A.add)
-                send(("RL%d" % v, 0, n1), ("SL%d" % v, 0, n1), "l%d" % v)
+                ts(wide("F2", h), wide("F", h), 2.0, A.mult, col(7), A.add)
+            t((1310, 1710)[h])
+            tt(wide("D", h), wide("F2", h), PB[h], A.is_gt)
+            t((1890, 2010)[h])
+            mm(Z, M("ZS"), R1, True, False)
+            t((1900, 2130)[h])
+            mm(Z, M("ZD"), wide("D", h), False, True)
+            t(((2750, 2800) if hand else (2100, 2400))[h] + late)
+            tt(wide("Y", h), wide("X", h), Z, A.min)
+        t(1840)
+        if fresh:
+            for h in range(2):
+                act(wide("EX", h, K * v), PB[h], AF.Relu, None, -1.0)
+        t(1410)
+        tolist(0, 2 if owed else 1)
+        if i > 1:
+            t(3500 if hand else 1850)
+            act(r3("RU", 1, 2, 1, 0, K), ind(UW, r2("LT", 0, 32)), after=[r2("PM", 0, 4)])
+        t(1990)
+        tt(fl(i, 0, 1), CNT, st(HH), A.is_equal)
+        ts(fl(i, 1, 1), CNT, 0.5, A.is_equal)
+        t(2300)
+        tt(st(PB_, 2), ls("TP", 1, 2), fl(i), A.mult)
+        tt(logged(i), fl(i, 1, 1), MU, A.mult)
+        t(2600)
+        tt(st(J_), st(PB_), logged(i), A.max)
+        t(2610 if hand else 2625)
+        tt(SLOT, CUR, st(QQ), A.max)
+        t(2620)
+        ts(r2("LJ", 0, 32), st(J_), O - 1.0, A.add)
+        t(3900 if i == 1 else 2650)
+        if fin:
+            for h in range(2):
+                act(wide("GA", h, K * (i - 1)), ind(GW, r2("LJ", L * h, L * h + L)))
+        else:
+            act(block("GA", i - 1), ind(GW if i > 1 else FW, r2("LJ", 0, 32)))
+        if hand:
+            send(r2("RG%d" % v, 0, K), [block("GA", i - 1)], "g%d" % v)
+        t(2850 if last else 2630)
+        tt(st(MB), fl(i, 0, 1), MU, A.mult)
+        if hand:
+            t(2640)
+            tt(st(U1, 2), ls("TP", 0, 2), fl(i), A.mult)
+        t(2640 if hand else 2800)
+        mm(CUR, M("ID"), SLOT, True, False)
+        mm(CUR, M("NI"), fl(i, 0, 1), False, True)
+        if fin:
+            t(2900)
+            ts(r2("OC", 0, 32), CUR, -1.0, A.add)
+            dma("Y", T.yc[:, :], T.OC[:, :], [r2("OC", 0, 32)], [])
+        else:
+            t(3460 if hand else 10975 if i > 1 else 4800)
+            act(st(HH), CUR, AF.Sign)
+        if i == 1:
+            t(16900)
+            ms(r2("LG", 32, 288), -2048.0)
+            ts(r2("LG", 0, 32), logged(i), -2048.0, A.add)
+        if owed:
+            write(i - 1, (4000, 4100, 4200, 4300) if hand else (2626, 2640, 3050, 3400))
+        if i > 1:
+            onehot("H%d" % (i % 2), i, [("ID", SLOT)], 3850 if hand else 3260, 4250 if hand else 3550)
+        if fin:
+            t(3480)
+            act(r2("LG", 0, 288), r2("LG", 0, 288), AF.Identity, col(11))
+        elif not last and i > 1:
+            look("H%d" % (i % 2), i - 1, 3700, 3900)
+        VP = r2("L1", 0, 32) if i > 1 else r2("L0", 64, 96)
+        t(300 + late)
+        mm(VP, M("KD"), r2("KC", 64, 96), True, False)
+        t((3350 if hand else 2750) + late)
+        for r in range(16):
+            mm(VP, r2("WY", 15 - r, 143 - r), r2("Y", r, K, 16), False, False)
+        mm(VP, M("KB"), fl(i, 0, 1), False, True)
+        t((3700 if hand else 3350) + late)
+        tt(ls("MI", 1), VP, st(MB), A.max)
+        t((3750 if hand else 3500) + late)
+        ts(MU, ls("MI", 1), 8191, A.bitwise_and)
+        t((3800 if hand else 3650) + late)
+        if fin:
+            ts(r2("OM", 0, 32), MU, -1.0, A.add)
+            dma("Y", T.ym[:, :], T.OM[:, :], [r2("OM", 0, 32)], [])
+        elif hand:
+            ts(ls(SA, 4), MU, O - 1.0, A.add)
+        else:
+            ts(r2("LS", 0, 32), MU, O - 1.0, A.add)
+        if not hand:
+            for h in range(2):
+                t(2320)
+                mm(PB[h], M("NI"), wide("EX", h, K * v), True, False)
+                for j in range(s + 1):
+                    t(3880 if j == s else 3270)
+                    mm(PB[h], M("NI"), wide("GA", h, K * (i - 1 - s + j)), False, j == s)
+        if fin:
+            for h in range(2):
+                t((3100, 3470)[h])
+                act(wide("OB", h), PB[h], AF.Identity, col(10))
+                dma("Y", T.yb[:, W * h:W * h + W], ap(wide("OB", h)), [wide("OB", h)], [])
+            t(2700)
+            tolist(1, 2)
+            write(i, (3600, 3700, 3800, 3900))
+            return
+        if not hand:
+            t(4000)
+            tt(st(U1, 2), ls("TP", 0, 2), fl(i), A.mult)
+        t(2700 if hand else 4100)
+        mm(ls("TP", 1, 2), M("IF"), st(TQ, 2), True, False)
+        mm(LEN, M("ID"), fl(i, 1, 1), False, False)
+        for w, x in (("KF", fl(i, 1, 1)), ("NF", st(PB_)), ("IF", logged(i)), ("IF", st(U1))):
+            mm(AT, M(w), x, False, False)
+        mm(AT, M("NF"), st(U0), False, True)
+        if not hand:
+            t(11305 if i > 1 else 4700)
+            ts(r2("LT", 0, 32), AT, O - 1.0 - FO, A.add)
+            t(11845 if i > 1 else 4810)
+            act(st(TQ, 2), ls("TP", 1, 2))
+            if s == S_ - 2 and v < V_ - 1:
+                onehot("HC", i, [("ID", SLOT), ("NI", fl(i, 0, 1))], 4050, 11320)
+                look("HC", i - 1, 11720, 11895)
+            return
+        t(3300)
+        ts(ls("MI", 2), AT, 1.0, A.add, float(K), A.mult)
+        ts(ls(SA, 0, 3), ls("TP", 1, 3), O - 1.0, A.add)
+        t(3400)
+        ts(ls("MI", 3), ls("MI", 2), K, A.bitwise_and)
+        t(3500)
+        tt(st(WX), ls("MI", 3), st(KK), A.add)
+        t(3600)
+        if v == 0:
+            tt(st(WL), st(WX), st(HH), A.mult)
+        else:
+            tt(st(WL), st(WX), st(WP), A.not_equal)
+            tt(st(WX), st(WX), st(HH), A.mult)
+            t(3710)
+            tt(st(WL), st(WL), st(WX), A.mult)
+        t(3760)
+        ts(ls(SA, 3), st(WL), O - 1.0, A.add)
+        t(3810)
+        send(ls("RA%d" % v, 0, 5), [ls(SA, 0, 5)], "a%d" % v)
+        if v == 0:
+            t(5000)
+            cp(st(WP), st(WL))
+        t(4400)
+        tolist(1, 2)
+        write(i, (4500, 4600, 4700, 4800))
+
+    for i in range(1, S_ * V_ + 1):
+        step(i)
 
     arrange()
     for s in ("eV", "eS", "eP", "eG", "sent"):

@@ -6,11 +6,14 @@ O = 16
 FO = C + O
 W, L = K // 2, 16
 XCH = [0, 1280, 2560, 3584, 4096]
-XAT = [9000, 10700, 17500, 18000]
+XAT = [("G", 0, 1280, 9000), ("G", 1280, 2560, 10700), ("G", 2560, 3584, 12000), ("V", 3584, 4096, 17000)]
+UG = 3072
 FAT = [("S", 6900), ("V", 5850), ("S", 8400), ("S", 10600)]
-DAT = [("S", 12100), ("S", 12200), ("S", 12600), ("S", 13100), ("S", 17600), ("S", 17700), ("S", 21500), ("S", 21600)]
+DAT = [("V", 9400), ("V", 9950), ("V", 11200), ("S", 11600), ("S", 12100), ("S", 12200), ("V", 16000), ("S", 21500)]
+UT, SAFE, PLOOK = 10530, 250, 80
+HT = (2635, 2636, 2640, 2637, 2638, 2585)
 CYC, PE, GAT, HOP, LOOK, PART, RATE = 0.91, 0.46, 1.56, 100, 30, 0.5, 300
-TQ, NN, CU, WL, P0, PB_, QQ, MB, HH, U1, U0, P1, DL, J_, WP, WX, KK = 0, 1, 2, 3, 4, 6, 7, 8, 9, 10, 11, 12, 13, 14, 15, 16, 17
+P0, TQ, NN, CU, WL, PB_, QQ, MB, HH, U1, U0, DL, J_, WP, WX, KK = 0, 2, 3, 4, 5, 6, 7, 8, 9, 10, 11, 18, 13, 15, 16, 17
 
 SCRATCH = {
     "G": ("sbuf", [128, 2 * FO], "bfloat16"), "FP": ("sbuf", [128, C], "bfloat16"), "U": ("sbuf", [128, FO], "bfloat16"),
@@ -25,18 +28,19 @@ SCRATCH = {
     "ZS": ("sbuf", [128, 128], "bfloat16"), "ZD": ("sbuf", [128, 128], "bfloat16"),
     "ID": ("sbuf", [128, 128], "bfloat16"), "NI": ("sbuf", [128, 128], "bfloat16"), "KF": ("sbuf", [128, 128], "float16"),
     "KB": ("sbuf", [128, 128], "bfloat16"), "KD": ("sbuf", [128, 128], "bfloat16"),
-    "IF": ("sbuf", [128, 128], "float32"), "NF": ("sbuf", [128, 128], "float32"),
-    "WB": ("sbuf", [128, 144], "bfloat16"), "WY": ("sbuf", [128, 144], "bfloat16"), "KC": ("sbuf", [128, 128], "float16"),
+    "IF": ("sbuf", [128, 128], "float32"), "KR": ("sbuf", [128, 128], "bfloat16"),
+    "WB": ("sbuf", [128, 144], "bfloat16"), "WY": ("sbuf", [128, 144], "bfloat16"), "KC": ("sbuf", [128, 224], "float16"),
+    "KP": ("sbuf", [128, 128], "bfloat16"),
     "SL": ("sbuf", [128, 288], "bfloat16"), "BI": ("sbuf", [128, 18], "int32"), "BL": ("sbuf", [128, 18], "uint16"),
     "KI": ("sbuf", [128, 32], "int32"), "L0I": ("sbuf", [128, 32], "uint16"),
     "F": ("sbuf", [128, K], "bfloat16"), "F2": ("sbuf", [128, K], "bfloat16"), "D": ("sbuf", [128, K], "bfloat16"),
     "X": ("sbuf", [128, K], "float32"), "Y": ("sbuf", [128, K], "float16"), "RU": ("sbuf", [128, 2, K], "bfloat16"),
     "GA": ("sbuf", [128, 9 * K], "bfloat16"), "BW": ("sbuf", [128, K], "bfloat16"), "EX": ("sbuf", [128, 3 * K], "bfloat16"),
-    "ST": ("sbuf", [128, 18, 32], "float32"), "E": ("sbuf", [128, 4, 32], "bfloat16"), "SLOT": ("sbuf", [128, 32], "bfloat16"),
+    "ST": ("sbuf", [128, 19, 32], "float32"), "E": ("sbuf", [128, 4, 32], "bfloat16"), "SLOT": ("sbuf", [128, 32], "bfloat16"),
     "LS": ("sbuf", [128, 32], "uint16"), "LT": ("sbuf", [128, 32], "uint16"), "LJ": ("sbuf", [128, 32], "uint16"),
-    "MI": ("sbuf", [128, 4, 32], "int32"),
+    "MI": ("sbuf", [128, 5, 32], "int32"),
     "H0": ("sbuf", [128, 288], "bfloat16"), "H1": ("sbuf", [128, 288], "bfloat16"), "HC": ("sbuf", [128, 160], "bfloat16"),
-    "P": ("sbuf", [128, 288], "float32"), "PQ": ("sbuf", [128, 256], "float16"),
+    "P": ("sbuf", [128, 288], "float32"), "PR": ("sbuf", [128, 288], "float32"), "PQ": ("sbuf", [128, 256], "float16"),
     "OB": ("sbuf", [128, K], "float32"), "OL": ("sbuf", [128, 288], "float32"), "OM": ("sbuf", [128, 32], "float32"),
     "OC": ("sbuf", [128, 32], "float32"),
 }
@@ -51,7 +55,7 @@ PSUM = ["PB0", "PB1", "Z0", "Z1", "L0", "L1", "TP", "LG"]
 for _n in PSUM:
     SCRATCH[_n] = ("psum", [128, 512], "float32")
 SCRATCH["TP"] = ("psum", [128, 16, 32], "float32")
-SEMAPHORES = (["eV", "eS", "eP", "eG", "sent"] + ["%s%d" % (n, v) for n in "abgl" for v in range(2)]
+SEMAPHORES = (["eV", "eS", "eP", "eG", "sent"] + ["%s%d" % (n, v) for n in "abghl" for v in range(2)]
               + ["d%d" % i for i in range(24)])
 
 
@@ -62,8 +66,6 @@ def rank_program(g, core, T, topo):
     n_ranks = len(T.cores)
     nxt, prv = T.cores[(rank + 1) % n_ranks], T.cores[(rank - 1) % n_ranks]
     rid, pid = topo.addr(nxt)[0], topo.addr(nxt)[1]
-    mask_out = topo.mask(core, nxt)
-    n_out, n_in = len(topo.engines(core, nxt)), len(topo.engines(prv, core))
     Q = {"V": g.vector, "S": g.scalar, "P": g.tensor, "G": g, "Y": g.sync}
     cnt = {"eV": 0, "eS": 0, "eP": 0, "eG": 0, "sent": 0}
     known = {e: {} for e in Q}
@@ -71,7 +73,9 @@ def rank_program(g, core, T, topo):
     ndma = [0]
     ends = []
     prog = []
-    sums, first = {}, {}
+    sums, first, whole, mark = {}, {}, set(), {}
+    behind, held_back = {}, []
+    made, moment = {e: [] for e in Q}, [0, 0]
     turn = [0, 0]
 
     def t(x):
@@ -117,11 +121,17 @@ def rank_program(g, core, T, topo):
                     if hit and need.get(tok[0], (0, None))[0] < tok[1]:
                         need[tok[0]] = (tok[1], clock)
         items = sorted(need.items())
-        for s, (v, clock) in items:
+        for s, (v, clock) in list(items):
             if known[e].get(s, 0) >= v:
                 continue
             if any(s2 != s and c2.get(s, 0) >= v for s2, (v2, c2) in items):
                 continue
+            if s in cnt and s != "sent":
+                past = made[s[1]]
+                while v < len(past) and past[v][0] + SAFE <= moment[0]:
+                    v += 1
+                items.append((s, (v, past[v - 1][1])))
+                known[e][s] = v
             Q[e].wait_ge(T.sem[s], v)
         for s, (v, clock) in items:
             for s2, v2 in list(clock.items()) + [(s, v)]:
@@ -143,6 +153,7 @@ def rank_program(g, core, T, topo):
             cnt["e" + e] += 1
             fn().then_inc(T.sem["e" + e], 1)
             note(e, e, ins, [out], ("e" + e, cnt["e" + e]))
+            made[e].append((moment[1], dict(known[e])))
         aps = [r for r in ins if isinstance(r, tuple) and r[2] > 1]
         n, two = out[2], e == "V" and len(aps) == 2
         if e == "P":
@@ -178,7 +189,9 @@ def rank_program(g, core, T, topo):
                         lst[:] = [a for a in lst if not (r[1] <= a[0] and a[1] <= r[2])]
                     lst.append((r[1], r[2], w, e, k))
             d.discard(k)
-            if k in sums and sums[k][0] in ("TP", "L0"):
+            if k in behind:
+                d.add(behind[k])
+            if k in sums and sums[k][1] in whole:
                 deps[sums[k][1]] = deps.get(sums[k][1], set()) | set(j for j in d if sums.get(j, (0, -1))[1] != sums[k][1])
             deps[k] = deps.get(k, set()) | d
         for k in range(len(prog)):
@@ -198,7 +211,7 @@ def rank_program(g, core, T, topo):
             e = min(can, key=lambda q: max(free[q], min(c[2] for c in can[q])))
             now = max(free[e], min(c[2] for c in can[e]))
             pick = min(c for c in can[e] if c[2] <= now)
-            pick = min(c for c in can[e] if c[2] <= now + max(LOOK, PART * prog[pick[1]][5]))
+            pick = min(c for c in can[e] if c[2] <= now + max(PLOOK if e == "P" else LOOK, PART * prog[pick[1]][5]))
             best, start = pick[1], max(now, pick[2])
             free[e] = done = start + prog[best][5]
             if prog[best][6]:
@@ -206,13 +219,14 @@ def rank_program(g, core, T, topo):
                 wire[line] = max(wire[line], start + 1500) + prog[best][6]
                 done = wire[line] + (800 if e == "G" else 500)
             ready.remove(best)
+            moment[:] = [start, done]
             for b in banks[best]:
                 used[b] = (e, done)
             if best in sums:
                 held[sums[best][0]] = -1 if sums[best][2] else sums[best][1]
             prog[best][1]()
             for k in users[best]:
-                at[k] = max(at[k], done + (0 if e == "P" == prog[k][0] else HOP))
+                at[k] = max(at[k], free[e] if behind.get(k) == best else done + (0 if e == "P" == prog[k][0] else HOP))
                 left[k] -= 1
                 if not left[k]:
                     ready.append(k)
@@ -241,17 +255,22 @@ def rank_program(g, core, T, topo):
         else:
             op("S", lambda: g.scalar.activation(ap(out), ap(a), func, bias=ap(bias), scale=scale), out, [a, bias])
 
-    def mm(out, w, x, start, stop):
+    def mm(out, w, x, start, stop, after=()):
         if start:
             first[out[0]] = len(prog)
+            if out[2] == 32 and out != CNT:
+                whole.add(len(prog))
         sums[len(prog)] = (out[0], first[out[0]], stop)
-        op("P", lambda: g.tensor.matmul(ap(out), ap(w), ap(x), start, stop), out, [w, x])
+        op("P", lambda: g.tensor.matmul(ap(out), ap(w), ap(x), start, stop), out, [w, x] + list(after))
 
     def iota(out, pat, base, ch, small):
         if small:
             op("G", lambda: g.iota(ap(out), pat, base, ch, allow_small_or_imprecise_dtypes=True), out, [])
         else:
             op("G", lambda: g.iota(ap(out), pat, base, ch), out, [])
+
+    def keep(out, a):
+        op("G", lambda: g.affine_select(ap(out), ap(a), [[0, out[2]]], A.is_ge, 0.0, 0, 0), out, [a])
 
     def dma(e, out_ap, in_ap, reads, writes):
         def emit():
@@ -264,7 +283,12 @@ def rank_program(g, core, T, topo):
         r = (reads + writes)[0]
         put(e, emit, reads, writes, 60, r[2] * (2 if SCRATCH[r[0]][2] == "bfloat16" else 4) * 128 / RATE)
 
-    def send(dst, srcs, sem):
+    def send(dst, srcs, sem, part=None):
+        outs, ins = topo.engines(core, nxt), topo.engines(prv, core)
+        if part is not None:
+            outs, ins = outs[part * len(outs) // 2:(part + 1) * len(outs) // 2], ins[:len(ins) // 2]
+        mask_out, n_out, n_in = sum(1 << e for e in outs), len(outs), len(ins)
+
         def emit():
             order("G", srcs, [])
             if len(srcs) == 1:
@@ -302,10 +326,11 @@ def rank_program(g, core, T, topo):
         return st(P0 + i % 2)
 
     FW, GW, XW, UW = r2("G", 0, FO), r2("G", 0, 2 * FO), r2("XF", 0, FO), r2("U", 0, FO)
-    MU, SLOT = ls("MI"), r2("SLOT", 0, 32)
+    MU, SLOT = ls("MI", 1), r2("SLOT", 0, 32)
     PB = [r2("PB%d" % h, 0, W) for h in range(2)]
     CNT, UP = r2("L0", 0, 32), r2("L0", 32, 64)
-    BELOW, AT, LEN, CUR = [ls("TP", s) for s in range(4)]
+    AT, LEN = ls("TP", 1), ls("TP", 2)
+    BELOW, KEEP, CUR = [r2("Z0", W + 32 * s, W + 32 * s + 32) for s in range(3)]
 
     for q in range(2):
         dma("Y", T.PL[:, 128 * q:128 * q + 128], T.nx[0:128:16, 2048 * q:2048 * q + 2048], [], [r2("PL", 128 * q, 128 * q + 128)])
@@ -322,7 +347,8 @@ def rank_program(g, core, T, topo):
     iota(r2("BI", 0, 18), [[0, 9], [16, 2]], 0, 0, False)
     iota(r2("KI", 0, 32), [[16, 32]], 1, 0, False)
     iota(r2("SL", 0, 288), [[1, 9], [0, 32]], 1, 0, True)
-    iota(UW, [[0, FO]], 0, 0, True)
+    iota(r2("U", 0, UG), [[0, UG]], 0, 0, True)
+    ms(col(12), -2047.0 / 128)
     ms(r2("G", 0, O), 0.0)
     ms(r2("G", FO, FO + O), 0.0)
     ms(r2("XF", 0, O), 0.0)
@@ -330,11 +356,12 @@ def rank_program(g, core, T, topo):
     ms(col(9), -255.0)
     ms(col(10), 255.0)
     ms(col(11), 2047.0)
-    ms(ls("TP", 0, 4), 0.0)
+    ms(AT, 0.0)
+    ms(r2("Z0", W, W + 96), 0.0)
     ms(LEN, 1.0)
     t(100)
     ts(r2("QI", 1, 2), r2("QI", 0, 1), 15, A.bitwise_and)
-    for j, x in enumerate((0.5, 0.0, 481.0, 2048.0 + FO)):
+    for j, x in enumerate((0.5, 16384.0, 481.0, 0.0, 2048.0 + FO - 16384, 2048.0 + FO - 32768, 0.0)):
         ts(r2("KC", 32 * j, 32 * j + 32), r2("J", 0, 32), 0.0, A.mult, x, A.add)
     tt(col(1), r2("QI", 0, 1), r2("QI", 1, 2), A.subtract)
     cp(col(0), r2("QI", 1, 2))
@@ -352,7 +379,7 @@ def rank_program(g, core, T, topo):
     ts(col(5), col(6), -1.0, A.mult)
     ts(col(4), col(0), 0.0, A.mult, -1.0, A.add)
     ts(col(8), col(1), 128.0, A.mult)
-    for name, times in (("NI", -1.0), ("KB", -2.0 ** 24), ("KD", 30720.0), ("IF", 1.0), ("NF", -1.0)):
+    for name, times in (("NI", -1.0), ("KB", -2.0 ** 24), ("KD", 30720.0), ("IF", 1.0), ("KR", -16384.0), ("KP", 16384.0)):
         act(M(name), M("ID"), AF.Copy, None, times)
     tt(M("TD"), M("TD"), M("TF"), A.mult)
     act(M("TE"), M("ID"), AF.Identity, col(4), 16.0)
@@ -380,6 +407,7 @@ def rank_program(g, core, T, topo):
     for h in range(2):
         mm(PB[h], M("NI"), wide("EX", h), True, True)
     t(10500)
+    ms(r2("U", UG, FO), 0.0)
     ts(r2("HI", 0, 256), r2("PC", 0, 256), 128.0, A.mult)
     cp(r2("LO", 0, 256), r2("PA", 0, 256))
     ts(r2("BL", 0, 18), r2("BI", 0, 18), col(0), A.add)
@@ -388,16 +416,20 @@ def rank_program(g, core, T, topo):
         a, b = O + 2048 * q, O + 2048 * q + 2048
         for row, name in enumerate(("HI", "LO")):
             dma("Y", T.U[row:128:16, a:b], T[name][:, 128 * q:128 * q + 128], [r2(name, 0, 256), UW], [r2("PM", 2 * q + row, 2 * q + row + 1)])
-    for a, b, x in zip(XCH[:-1], XCH[1:], XAT):
+    for e, a, b, x in XAT:
         t(x)
-        ts(r2("XF", O + a, O + b), r2("XI", a, b), 1.0 / 128, A.mult, -2047.0 / 128, A.add)
+        if e == "V":
+            held_back.append(len(prog))
+            cp(r2("XF", O + a, O + b), r2("XI", a, b))
+        else:
+            keep(r2("XF", O + a, O + b), r2("XI", a, b))
 
     for q, (e, x) in enumerate(FAT):
         t(x)
         (cp if e == "V" else act)(r2("FP", 1024 * q, 1024 * q + 1024), ind(FW, r2("P16", 64 * q, 64 * q + 64)))
     for k, (e, x) in enumerate(DAT):
         bk, q = ("L1", "LG")[k % 2], k // 4
-        t(x - 600)
+        t(min(x - 600, 16500))
         for r in range(4):
             a = O + 512 * k + 128 * r
             mm(r2(bk, 128 * r, 128 * r + 128), M("NI"), r2("G", a, a + 128), True, False)
@@ -415,36 +447,51 @@ def rank_program(g, core, T, topo):
             for k, (w, x) in enumerate(terms):
                 mm(r2("Z1", a + 32 * j, a + 32 + 32 * j), M(w), x, k == 0, k == len(terms) - 1)
         t(at_v)
+        if H != "HC":
+            held_back.append(len(prog))
         tt(r2(H, 0, 32 * n), r2("Z1", a, a + 32 * n), r2("SL", 0, 32 * n), A.is_equal)
 
-    def look(H, n, at_v, at_p):
+    def look(H, n, at_v, at_p, back=None):
         t(at_v)
         tt(r2("PQ", 0, 32 * n), r2(H, 32, 32 * n + 32), r2("LG", 0, 32 * n), A.mult)
         t(at_p)
-        mm(BELOW, M("ID"), r2("KC", 96, 128), True, False)
+        mm(BELOW, M("ID"), r2("KC", 128, 160) if back else r2("KC", 96, 128), True, False)
+        if back:
+            mm(BELOW, M("KP"), back, False, False)
         for j in range(n):
             mm(BELOW, M("ID"), r2("PQ", 32 * j, 32 * j + 32), False, j == n - 1)
 
-    def tolist(s0, s1):
+    def tolist(s0, s1, i):
         out = r2("L0", 32 * s0, 32 * s1)
-        if s0 == 0:
-            mm(out, M("ID"), r2("KC", 0, 32 * s1), True, False)
+        if "change" in mark:
+            behind[len(prog)] = mark["change"]
+        mm(out, M("ID"), r2("KC", 32 * s0, 32 * s1), True, False)
+        if s1 == 2:
+            mm(UP, M("KR"), fl(i, 0, 1), False, False)
         for r in range(16):
-            mm(out, r2("WB", 15 - r, 143 - r), r3("RU", s0, s1, 1, r, K, 16), s0 > 0 and r == 0, r == 15)
+            mm(out, r2("WB", 15 - r, 143 - r), r3("RU", s0, s1, 1, r, K, 16), False, r == 15)
 
     def write(i, at):
         n, v = 32 * i, (i - 1) // S_
-        t(at[0])
-        tt(st(P1), UP, fl(i, 0, 1), A.mult)
         t(at[1])
-        tt(st(DL), st(P1), logged(i), A.add)
+        mark["change"] = len(prog)
+        if at[0] == 4000:
+            held_back.append(len(prog))
+        tt(st(DL), UP, st(J_ + i % 2), A.min)
         t(at[2])
-        tt(r2("P", 0, n), bc(st(DL), i), r2("H%d" % (i % 2), 0, n), A.mult)
+        P = "PR" if i == S_ * V_ else "P"
+        tt(r2(P, 0, n), bc(st(DL), i), r2("H%d" % (i % 2), 0, n), A.mult)
         t(at[3])
         if i == S_ * V_:
-            tt(r2("OL", 0, n), r2("P", 0, n), r2("LG", 0, n), A.add)
+            tt(r2("OL", 0, n), r2(P, 0, n), r2("LG", 0, n), A.add)
             dma("Y", T.yl[:, :], T.OL[:, :], [r2("OL", 0, 288)], [])
+        elif i == S_ * V_ - 1:
+            t(1846)
+            act(r2("LG", 0, 288), r2("LG", 0, 288), AF.Identity, col(11))
+            t(3560)
+            tt(r2("LG", 0, n), r2("P", 0, n), r2("LG", 0, n), A.add)
         elif i % S_:
+            held_back.append(len(prog))
             tt(r2("LG", 0, n), r2("P", 0, n), r2("LG", 0, n), A.add)
         else:
             tt(r2("SL%d" % v, 0, n), r2("P", 0, n), r2("LG", 0, n), A.add)
@@ -464,8 +511,9 @@ def rank_program(g, core, T, topo):
             for h in range(2):
                 t(50)
                 mm(PB[h], M("NI"), wide("RB%d" % (v - 1), h), True, False)
+                t(50 + 350 * h)
                 mm(PB[h], M("NI"), wide("RG%d" % (v - 1), h), False, False)
-                t(550 + 420 * h)
+                t(60 + 420 * h)
                 mm(PB[h], M("ID"), wide("BW", h), False, True)
             t(950)
             ts(st(TQ, 3), ls(RA, 0, 3), 1.0 - O, A.add)
@@ -474,8 +522,9 @@ def rank_program(g, core, T, topo):
             ts(r2("LT", 0, 32), ls(RA, 0), -float(FO), A.add)
             t(1400)
             act(st(HH), st(CU), AF.Sign)
-            t(1050)
-            mm(ls("TP", 1, 3), M("IF"), st(TQ, 3), True, True)
+            t(1950)
+            mm(ls("TP", 1, 2), M("IF"), st(TQ, 2), True, True)
+            mm(CUR, M("IF"), st(CU), True, True)
             t(3300)
             cp(r2("LG", 0, 96 * v), r2("RL%d" % (v - 1), 0, 96 * v))
         if hand:
@@ -484,18 +533,20 @@ def rank_program(g, core, T, topo):
         lst = [r3(RA, 4, 5, 1, L * h, L * h + L) if fresh else r2("LS", L * h, L * h + L) for h in range(2)]
         late = 7400 if i == 1 else 0
         for h in range(2):
-            t(100 + 440 * h)
+            t(380 * h)
+            if h == 1 and "has" in mark:
+                behind[mark.pop("has")] = len(prog)
             act(wide("F", h), ind(FW, lst[h]), AF.Identity, col(9))
             t(980 + 430 * h + late)
             if i > 1:
-                act(wide("X", h), ind(XW, lst[h]))
-            else:
-                ts(wide("X", h), ind(r2("XI", 0, C), r2("L0I", L * h, L * h + L)), 1.0 / 128, A.mult, -2047.0 / 128, A.add)
+                act(wide("X", h), ind(XW, lst[h]), AF.Identity, col(12), 1.0 / 128)
+            elif h == 0:
+                ts(r2("X", 0, K), ind(r2("XI", 0, C), r2("L0I", 0, 32)), 1.0 / 128, A.mult, -2047.0 / 128, A.add)
         for h in range(2):
-            Z, R1 = r2("Z%d" % h, 0, W), r3("RU", 0, 1, 1, W * h, W * h + W)
-            t((1000, 1075)[h] if fresh else (640, 1075)[h])
+            Z, R1 = r2("L1", W, K) if h == 0 and i > 1 else r2("Z%d" % h, 0, W), r3("RU", 0, 1, 1, W * h, W * h + W)
+            t((640, 1075)[h])
             tt(R1, wide("F", h), PB[h], A.is_gt)
-            t((880, 1300)[h])
+            t((1180, 1300)[h])
             if h == 1 and i > 1:
                 t(976)
                 act(wide("F2", h), wide("F", h), AF.Identity, col(7), 2.0)
@@ -503,146 +554,190 @@ def rank_program(g, core, T, topo):
                 ts(wide("F2", h), wide("F", h), 2.0, A.mult, col(7), A.add)
             t((1310, 1710)[h])
             tt(wide("D", h), wide("F2", h), PB[h], A.is_gt)
-            t((1890, 2010)[h])
+            t((1000, 2010)[h])
             mm(Z, M("ZS"), R1, True, False)
             t((1900, 2130)[h])
             mm(Z, M("ZD"), wide("D", h), False, True)
-            t(((2750, 2800) if hand else (2100, 2400))[h] + late)
+            t((2100, 2628 if hand else 2400)[h] + late)
+            if h == 0:
+                mark["y0"] = len(prog)
             tt(wide("Y", h), wide("X", h), Z, A.min)
         t(1840)
         if fresh:
             for h in range(2):
                 act(wide("EX", h, K * v), PB[h], AF.Relu, None, -1.0)
         t(1410)
-        tolist(0, 2 if owed else 1)
+        tolist(0, 2 if owed else 1, i - 1)
         if i > 1:
             t(3500 if hand else 1850)
+            mark["partner"] = len(prog)
             act(r3("RU", 1, 2, 1, 0, K), ind(UW, r2("LT", 0, 32)), after=[r2("PM", 0, 4)])
         t(1990)
         tt(fl(i, 0, 1), CNT, st(HH), A.is_equal)
         ts(fl(i, 1, 1), CNT, 0.5, A.is_equal)
-        t(2300)
+        t(2600 if hand else 2300)
         tt(st(PB_, 2), ls("TP", 1, 2), fl(i), A.mult)
         tt(logged(i), fl(i, 1, 1), MU, A.mult)
         t(2600)
-        tt(st(J_), st(PB_), logged(i), A.max)
-        t(2610 if hand else 2625)
+        tt(st(J_ + i % 2), st(PB_), logged(i), A.max)
+        t(2625)
         tt(SLOT, CUR, st(QQ), A.max)
         t(2620)
-        ts(r2("LJ", 0, 32), st(J_), O - 1.0, A.add)
+        ts(r2("LJ", 0, 32), st(J_ + i % 2), O - 1.0, A.add)
         t(3900 if i == 1 else 2650)
-        if fin:
+        if last:
             for h in range(2):
                 act(wide("GA", h, K * (i - 1)), ind(GW, r2("LJ", L * h, L * h + L)))
+                if hand:
+                    mark["second"] = len(prog)
+                    behind[mark["partner"]] = len(prog) - 1
+                    send(wide("RG%d" % v, h), [wide("GA", h, K * (i - 1))], "gh"[h] + "%d" % v)
         else:
             act(block("GA", i - 1), ind(GW if i > 1 else FW, r2("LJ", 0, 32)))
-        if hand:
-            send(r2("RG%d" % v, 0, K), [block("GA", i - 1)], "g%d" % v)
-        t(2850 if last else 2630)
+        t(2690)
         tt(st(MB), fl(i, 0, 1), MU, A.mult)
         if hand:
-            t(2640)
-            tt(st(U1, 2), ls("TP", 0, 2), fl(i), A.mult)
+            one, two, same = [r2("LG", 320 + 32 * j, 352 + 32 * j) for j in range(3)]
+            terms = [(one, "KR", fl(i - 1, 0, 1)), (two, "KP", fl(i - 1, 0, 1))]
+            terms += [(one, "ID", r2("PQ", 32 * j, 32 * j + 32)) for j in range(i - 2)]
+            terms += [(two, "ID", r2("PQ", 128 + 32 * j, 160 + 32 * j)) for j in range(i - 3)]
+            t(600)
+            mm(r2("LG", 320, 416), M("ID"), r2("KC", 128, 224), True, False, [r2("PQ", 0, 256)])
+            for out, w, x in terms:
+                mm(out, M(w), x, False, False)
+            t(1905)
+            for out, w, x in ((same, "IF", st(TQ)), (one, "KP", fl(i, 0, 1)), (two, "KP", fl(i, 0, 1)), (same, "KR", fl(i, 0, 1))):
+                mm(out, M(w), x, False, False)
+            mm(same, M("KR"), fl(i, 1, 1), False, True)
+            t(2610)
+            ts(st(U1, 3), r2("LG", 320, 416), 0.0, A.max)
+        elif not fin:
+            t(2810)
+            mm(KEEP, M("IF"), st(TQ), True, False)
+            mm(KEEP, M("KR"), fl(i, 0, 1), False, False)
+            mm(KEEP, M("KR"), fl(i, 1, 1), False, True)
         t(2640 if hand else 2800)
         mm(CUR, M("ID"), SLOT, True, False)
         mm(CUR, M("NI"), fl(i, 0, 1), False, True)
         if fin:
-            t(2900)
+            t(4100)
             ts(r2("OC", 0, 32), CUR, -1.0, A.add)
             dma("Y", T.yc[:, :], T.OC[:, :], [r2("OC", 0, 32)], [])
-        else:
-            t(3460 if hand else 10975 if i > 1 else 4800)
+        elif not hand:
+            t(10975 if i > 1 else 4800)
+            if i > 1:
+                mark["has"] = len(prog)
             act(st(HH), CUR, AF.Sign)
         if i == 1:
             t(16900)
             ms(r2("LG", 32, 288), -2048.0)
             ts(r2("LG", 0, 32), logged(i), -2048.0, A.add)
-        if owed:
-            write(i - 1, (4000, 4100, 4200, 4300) if hand else (2626, 2640, 3050, 3400))
+        if owed and i != 8:
+            write(i - 1, (4000, 4100, 4200, 4300) if hand else (2626, 2490, 3050, 3400))
         if i > 1:
-            onehot("H%d" % (i % 2), i, [("ID", SLOT)], 3850 if hand else 3260, 4250 if hand else 3550)
-        if fin:
-            t(3480)
-            act(r2("LG", 0, 288), r2("LG", 0, 288), AF.Identity, col(11))
-        elif not last and i > 1:
-            look("H%d" % (i % 2), i - 1, 3700, 3900)
+            onehot("H%d" % (i % 2), i, [("ID", SLOT)], 3850 if hand else 2331 if fin else 3260, 4250 if hand else 3055 if fin else 3550)
+        if not last and i > 1:
+            look("H%d" % (i % 2), i - 1, 3700, 3900, fl(i, 0, 1))
+        if i == 8:
+            write(i - 1, (2626, 2490, 3050, 11696))
         VP = r2("L1", 0, 32) if i > 1 else r2("L0", 64, 96)
-        t(300 + late)
+        t(2200 + late)
         mm(VP, M("KD"), r2("KC", 64, 96), True, False)
-        t((3350 if hand else 2750) + late)
+        whole.discard(len(prog) - 1)
+        behind[len(prog) - 1] = mark["y0"]
+        mm(VP, M("KB"), fl(i, 0, 1), False, False)
+        t(2750 + late)
         for r in range(16):
-            mm(VP, r2("WY", 15 - r, 143 - r), r2("Y", r, K, 16), False, False)
-        mm(VP, M("KB"), fl(i, 0, 1), False, True)
-        t((3700 if hand else 3350) + late)
-        tt(ls("MI", 1), VP, st(MB), A.max)
-        t((3750 if hand else 3500) + late)
-        ts(MU, ls("MI", 1), 8191, A.bitwise_and)
-        t((3800 if hand else 3650) + late)
+            mark["named"] = len(prog)
+            mm(VP, r2("WY", 15 - r, 143 - r), r2("Y", r, K, 16), False, r == 15)
+        late += 700 if fin else 0
+        t((2632 if hand else 3410) + late)
+        if i == 1:
+            mark["change"] = len(prog)
+        tt(ls("MI", 4), VP, st(MB), A.max)
+        t((2633 if hand else 3500) + late)
+        ts(MU, ls("MI", 4), 8191, A.bitwise_and)
+        t((2634 if hand else 3650) + late)
+        while held_back:
+            k = held_back.pop()
+            if not fin:
+                behind[k] = len(prog)
         if fin:
             ts(r2("OM", 0, 32), MU, -1.0, A.add)
-            dma("Y", T.ym[:, :], T.OM[:, :], [r2("OM", 0, 32)], [])
-        elif hand:
-            ts(ls(SA, 4), MU, O - 1.0, A.add)
-        else:
+            dma("S", T.ym[:, :], T.OM[:, :], [r2("OM", 0, 32)], [])
+        elif not hand:
             ts(r2("LS", 0, 32), MU, O - 1.0, A.add)
         if not hand:
             for h in range(2):
                 t(2320)
                 mm(PB[h], M("NI"), wide("EX", h, K * v), True, False)
                 for j in range(s + 1):
-                    t(3880 if j == s else 3270)
+                    t((2690 if j == s else 2330) if fin else 4480 if j == s else 3270)
+                    if j < s and not fin:
+                        behind[len(prog)] = mark["named"]
                     mm(PB[h], M("NI"), wide("GA", h, K * (i - 1 - s + j)), False, j == s)
         if fin:
             for h in range(2):
                 t((3100, 3470)[h])
                 act(wide("OB", h), PB[h], AF.Identity, col(10))
-                dma("Y", T.yb[:, W * h:W * h + W], ap(wide("OB", h)), [wide("OB", h)], [])
-            t(2700)
-            tolist(1, 2)
-            write(i, (3600, 3700, 3800, 3900))
+                dma("S", T.yb[:, W * h:W * h + W], ap(wide("OB", h)), [wide("OB", h)], [])
+            t(2332)
+            tolist(1, 2, i)
+            write(i, (3060, 3070, 3800, 3900))
             return
         if not hand:
-            t(4000)
-            tt(st(U1, 2), ls("TP", 0, 2), fl(i), A.mult)
-        t(2700 if hand else 4100)
-        mm(ls("TP", 1, 2), M("IF"), st(TQ, 2), True, False)
+            t(UT if i > 1 else 4000)
+            act(st(U1, 2), r2("Z0", W, W + 64), AF.Relu)
+        t(2140 if hand else 3280)
+        if not hand and i > 1:
+            behind[len(prog)] = mark["named"]
+        mm(ls("TP", 1, 2), M("IF"), r3("ST", P0 + i % 2, NN + 1, NN - P0 - i % 2, 0, 32), True, False)
         mm(LEN, M("ID"), fl(i, 1, 1), False, False)
-        for w, x in (("KF", fl(i, 1, 1)), ("NF", st(PB_)), ("IF", logged(i)), ("IF", st(U1))):
-            mm(AT, M(w), x, False, False)
-        mm(AT, M("NF"), st(U0), False, True)
+        mm(AT, M("KF"), fl(i, 1, 1), False, False)
+        t(2150 if hand else 11300 if i > 1 else 4090)
+        if hand:
+            mm(AT, M("IF"), st(U0 + 1), False, False)
+        mm(AT, M("IF"), st(U0), False, False)
+        mm(AT, M("IF"), st(U1), False, True)
         if not hand:
             t(11305 if i > 1 else 4700)
             ts(r2("LT", 0, 32), AT, O - 1.0 - FO, A.add)
-            t(11845 if i > 1 else 4810)
+            ahead = s == S_ - 2 and v < V_ - 1
+            t(11400 if ahead else 11845 if i > 1 else 4810)
             act(st(TQ, 2), ls("TP", 1, 2))
-            if s == S_ - 2 and v < V_ - 1:
-                onehot("HC", i, [("ID", SLOT), ("NI", fl(i, 0, 1))], 4050, 11320)
-                look("HC", i - 1, 11720, 11895)
+            if ahead and i > 2:
+                t(3710)
+                tt(r2("PQ", 128, 128 + 32 * (i - 2)), r2("H%d" % (i % 2), 64, 32 * i), r2("LG", 0, 32 * (i - 2)), A.mult)
             return
-        t(3300)
-        ts(ls("MI", 2), AT, 1.0, A.add, float(K), A.mult)
-        ts(ls(SA, 0, 3), ls("TP", 1, 3), O - 1.0, A.add)
-        t(3400)
-        ts(ls("MI", 3), ls("MI", 2), K, A.bitwise_and)
-        t(3500)
-        tt(st(WX), ls("MI", 3), st(KK), A.add)
-        t(3600)
-        if v == 0:
-            tt(st(WL), st(WX), st(HH), A.mult)
-        else:
-            tt(st(WL), st(WX), st(WP), A.not_equal)
-            tt(st(WX), st(WX), st(HH), A.mult)
-            t(3710)
-            tt(st(WL), st(WL), st(WX), A.mult)
-        t(3760)
-        ts(ls(SA, 3), st(WL), O - 1.0, A.add)
+        t(HT[0])
+        ts(ls("MI", 2), AT, 1.0, A.add, float(K) if v == 0 else 1.0, A.mult)
+        t(HT[1])
+        ts(ls("MI", 3), ls("MI", 2), K if v == 0 else 1, A.bitwise_and)
+        t(HT[2])
+        ts(st(HH), CUR, 0.0, A.is_equal, -4096.0, A.mult)
+        tt(st(WX), st(HH), st(KK), A.add)
+        if v > 0:
+            t(HT[3])
+            tt(st(CU), ls("MI", 3), st(WP), A.mult)
+        t(HT[4])
+        tt(ls("MI"), st(WX), ls("MI", 3) if v == 0 else st(CU), A.add)
+        t(HT[5])
+        ts(ls(SA, 0, 2), ls("TP", 1, 2), O - 1.0, A.add)
+        ts(ls(SA, 2), CUR, O - 1.0, A.add)
+        ts(ls(SA, 3, 2), ls("MI", 0, 2), O - 1.0, A.add)
         t(3810)
+        behind[mark["second"]] = len(prog)
         send(ls("RA%d" % v, 0, 5), [ls(SA, 0, 5)], "a%d" % v)
         if v == 0:
             t(5000)
-            cp(st(WP), st(WL))
+            tt(st(WX), ls("MI"), st(KK), A.subtract)
+            ts(st(WL), st(WX), 0.0, A.is_equal, -4096.0, A.mult)
+            ts(st(WX), st(WX), float(K), A.is_equal, -4096.0, A.mult)
+            tt(st(KK), st(KK), st(WL), A.add)
+            tt(st(WX), st(WX), st(WL), A.subtract)
+            ts(st(WP), st(WX), float(K), A.add)
         t(4400)
-        tolist(1, 2)
+        tolist(1, 2, i)
         write(i, (4500, 4600, 4700, 4800))
 
     for i in range(1, S_ * V_ + 1):

from concourse.mybir import AluOpType as A, ActivationFunctionType as AF
from concourse.bass import DstId, RemoteDMATransfer

C, K, V_, S_ = 4096, 512, 3, 3
O = 16
FO = C + O
W, L = K // 2, 16
XCH = [0, 1280, 2560, 3584, 4096]
XAT = [("G", 0, 1280, 9000), ("G", 1280, 2560, 10700), ("G", 2560, 3584, 12000), ("V", 3584, 4096, 17000)]
UG = 3072
FAT = [("S", 6900), ("V", 5850), ("S", 8400), ("S", 10600)]
DAT = [("V", 9400), ("V", 9950), ("V", 11200), ("S", 11600), ("S", 12100), ("S", 12200), ("V", 16000), ("S", 21500)]
UT, SAFE, PLOOK = 10530, 250, 80
HT = (2635, 2636, 2640, 2637, 2638, 2585)
CYC, PE, GAT, HOP, LOOK, PART, RATE = 0.91, 0.46, 1.56, 100, 30, 0.5, 300
P0, TQ, NN, CU, WL, PB_, QQ, MB, HH, U1, U0, DL, J_, WP, WX, KK = 0, 2, 3, 4, 5, 6, 7, 8, 9, 10, 11, 18, 13, 15, 16, 17

SCRATCH = {
    "G": ("sbuf", [128, 2 * FO], "bfloat16"), "FP": ("sbuf", [128, C], "bfloat16"), "U": ("sbuf", [128, FO], "bfloat16"),
    "P16": ("sbuf", [128, 256], "uint16"), "PL": ("sbuf", [128, 256], "int32"), "PM": ("sbuf", [128, 256], "int32"),
    "PA": ("sbuf", [128, 256], "int32"), "PC": ("sbuf", [128, 256], "int32"),
    "HI": ("sbuf", [128, 256], "bfloat16"), "LO": ("sbuf", [128, 256], "bfloat16"),
    "XI": ("sbuf", [128, C], "int32"), "XF": ("sbuf", [128, FO], "float32"),
    "WT": ("sbuf", [128, 2 * K + O], "bfloat16"), "B0": ("sbuf", [128, K], "bfloat16"), "M0": ("sbuf", [128, 32], "int32"),
    "J": ("sbuf", [128, 144], "float32"), "QI": ("sbuf", [128, 8], "int32"), "COL": ("sbuf", [128, 16], "float32"),
    "TA": ("sbuf", [128, 128], "bfloat16"), "TC": ("sbuf", [128, 128], "bfloat16"),
    "TD": ("sbuf", [128, 128], "bfloat16"), "TE": ("sbuf", [128, 128], "bfloat16"), "TF": ("sbuf", [128, 128], "bfloat16"),
    "ZS": ("sbuf", [128, 128], "bfloat16"), "ZD": ("sbuf", [128, 128], "bfloat16"),
    "ID": ("sbuf", [128, 128], "bfloat16"), "NI": ("sbuf", [128, 128], "bfloat16"), "KF": ("sbuf", [128, 128], "float16"),
    "KB": ("sbuf", [128, 128], "bfloat16"), "KD": ("sbuf", [128, 128], "bfloat16"),
    "IF": ("sbuf", [128, 128], "float32"), "KR": ("sbuf", [128, 128], "bfloat16"),
    "WB": ("sbuf", [128, 144], "bfloat16"), "WY": ("sbuf", [128, 144], "bfloat16"), "KC": ("sbuf", [128, 224], "float16"),
    "KP": ("sbuf", [128, 128], "bfloat16"),
    "SL": ("sbuf", [128, 288], "bfloat16"), "BI": ("sbuf", [128, 18], "int32"), "BL": ("sbuf", [128, 18], "uint16"),
    "KI": ("sbuf", [128, 32], "int32"), "L0I": ("sbuf", [128, 32], "uint16"),
    "F": ("sbuf", [128, K], "bfloat16"), "F2": ("sbuf", [128, K], "bfloat16"), "D": ("sbuf", [128, K], "bfloat16"),
    "X": ("sbuf", [128, K], "float32"), "Y": ("sbuf", [128, K], "float16"), "RU": ("sbuf", [128, 2, K], "bfloat16"),
    "GA": ("sbuf", [128, 9 * K], "bfloat16"), "BW": ("sbuf", [128, K], "bfloat16"), "EX": ("sbuf", [128, 3 * K], "bfloat16"),
    "ST": ("sbuf", [128, 19, 32], "float32"), "E": ("sbuf", [128, 4, 32], "bfloat16"), "SLOT": ("sbuf", [128, 32], "bfloat16"),
    "LS": ("sbuf", [128, 32], "uint16"), "LT": ("sbuf", [128, 32], "uint16"), "LJ": ("sbuf", [128, 32], "uint16"),
    "MI": ("sbuf", [128, 5, 32], "int32"),
    "H0": ("sbuf", [128, 288], "bfloat16"), "H1": ("sbuf", [128, 288], "bfloat16"), "HC": ("sbuf", [128, 160], "bfloat16"),
    "P": ("sbuf", [128, 288], "float32"), "PR": ("sbuf", [128, 288], "float32"), "PQ": ("sbuf", [128, 256], "float16"),
    "OB": ("sbuf", [128, K], "float32"), "OL": ("sbuf", [128, 288], "float32"), "OM": ("sbuf", [128, 32], "float32"),
    "OC": ("sbuf", [128, 32], "float32"),
}
for _v in range(V_ - 1):
    for _n in ("RB", "RG"):
        SCRATCH["%s%d" % (_n, _v)] = ("sbuf", [128, K], "bfloat16")
    for _n in ("SA", "RA"):
        SCRATCH["%s%d" % (_n, _v)] = ("sbuf", [128, 5, 32], "uint16")
    for _n in ("SL", "RL"):
        SCRATCH["%s%d" % (_n, _v)] = ("sbuf", [128, 96 * (_v + 1)], "float16")
PSUM = ["PB0", "PB1", "Z0", "Z1", "L0", "L1", "TP", "LG"]
for _n in PSUM:
    SCRATCH[_n] = ("psum", [128, 512], "float32")
SCRATCH["TP"] = ("psum", [128, 16, 32], "float32")
SEMAPHORES = (["eV", "eS", "eP", "eG", "sent"] + ["%s%d" % (n, v) for n in "abghl" for v in range(2)]
              + ["d%d" % i for i in range(24)])


def rank_program(g, core, T, topo):
    rank = T.rank_of(core)
    if rank is None:
        return
    n_ranks = len(T.cores)
    nxt, prv = T.cores[(rank + 1) % n_ranks], T.cores[(rank - 1) % n_ranks]
    rid, pid = topo.addr(nxt)[0], topo.addr(nxt)[1]
    Q = {"V": g.vector, "S": g.scalar, "P": g.tensor, "G": g, "Y": g.sync}
    cnt = {"eV": 0, "eS": 0, "eP": 0, "eG": 0, "sent": 0}
    known = {e: {} for e in Q}
    acc = {}
    ndma = [0]
    ends = []
    prog = []
    sums, first, whole, mark = {}, {}, set(), {}
    behind, held_back = {}, []
    made, moment = {e: [] for e in Q}, [0, 0]
    turn = [0, 0]

    def t(x):
        turn[1] = x

    def put(e, emit, reads, writes, busy, line=0):
        prog.append([e, emit, reads, writes, turn[0] + turn[1], busy, line])

    def r2(name, lo, hi, step=1):
        return (name, [(lo, hi)], -((lo - hi) // step), (slice(None), slice(lo, hi, step)), step == 1)

    def r3(name, s0, s1, ss, c0, c1, cs=1):
        wd = SCRATCH[name][1][2]
        slots = list(range(s0, s1, ss))
        ix = (slice(None), s0 if len(slots) == 1 else slice(s0, s1, ss), slice(c0, c1, cs))
        return (name, [(s * wd + c0, s * wd + c1) for s in slots], len(slots) * -((c0 - c1) // cs), ix, cs == 1)

    def ind(win, off):
        return ("ind", win, 16 * off[2], off)

    def ap(r):
        if r[0] == "ind":
            return ap(r[1]).indirect(ap(r[3]))
        return T[r[0]][r[3]]

    def spans(rs):
        out = []
        for r in rs:
            if isinstance(r, tuple):
                for q in ([r[1], r[3]] if r[0] == "ind" else [r]):
                    out += [(q[0], lo, hi, q[4]) for lo, hi in q[1]]
        return out

    def order(e, reads, writes):
        need = {}
        for rs, w in ((reads, False), (writes, True)):
            for r in spans(rs):
                for lo, hi, pw, pe, tok, clock in acc.get(r[0], []):
                    if r[0] in PSUM:
                        hit = pe != e or (e != "P" and (w or pw) and lo < r[2] and r[1] < hi)
                    else:
                        hit = (w or pw) and lo < r[2] and r[1] < hi
                    if hit and need.get(tok[0], (0, None))[0] < tok[1]:
                        need[tok[0]] = (tok[1], clock)
        items = sorted(need.items())
        for s, (v, clock) in list(items):
            if known[e].get(s, 0) >= v:
                continue
            if any(s2 != s and c2.get(s, 0) >= v for s2, (v2, c2) in items):
                continue
            if s in cnt and s != "sent":
                past = made[s[1]]
                while v < len(past) and past[v][0] + SAFE <= moment[0]:
                    v += 1
                items.append((s, (v, past[v - 1][1])))
                known[e][s] = v
            Q[e].wait_ge(T.sem[s], v)
        for s, (v, clock) in items:
            for s2, v2 in list(clock.items()) + [(s, v)]:
                if known[e].get(s2, 0) < v2:
                    known[e][s2] = v2

    def note(e, who, reads, writes, tok):
        clock = dict(known[e])
        for rs, w in ((reads, False), (writes, True)):
            for r in spans(rs):
                lst = acc.setdefault(r[0], [])
                if w and r[3]:
                    lst[:] = [a for a in lst if not (r[1] <= a[0] and a[1] <= r[2])]
                lst.append([r[1], r[2], w, who, tok, clock])

    def op(e, fn, out, ins):
        def emit():
            order(e, ins, [out])
            cnt["e" + e] += 1
            fn().then_inc(T.sem["e" + e], 1)
            note(e, e, ins, [out], ("e" + e, cnt["e" + e]))
            made[e].append((moment[1], dict(known[e])))
        aps = [r for r in ins if isinstance(r, tuple) and r[2] > 1]
        n, two = out[2], e == "V" and len(aps) == 2
        if e == "P":
            busy = max(64, ins[1][2]) * PE * (4 if SCRATCH[ins[1][0]][2] == "float32" else 1)
        elif e == "G":
            busy = 130 + 2 * n * CYC
        elif any(r[0] == "ind" for r in aps):
            busy = 85 + (2 if two else GAT) * n * CYC
        elif two:
            busy = 25 + max(64, n * (1 if any(r[0] in PSUM for r in aps) else 2)) * CYC
        elif e == "V" and all(SCRATCH[r[0]][2] in ("bfloat16", "float16", "uint16") for r in aps + [out]):
            busy = 25 + max(64, n * 0.5) * CYC
        else:
            busy = 25 + max(64, n) * CYC
        put(e, emit, ins, [out], busy)

    def arrange():
        seen, users, left, tail, deps = {}, [[] for _ in prog], [], {}, {}
        for k, (e, emit, reads, writes) in enumerate(a[:4] for a in prog):
            d = set()
            if k in sums:
                d.add(tail.get(sums[k][1], k))
                tail[sums[k][1]] = k
            for rs, w in ((reads, False), (writes, True)):
                for r in spans(rs):
                    for lo, hi, pw, pe, j in seen.get(r[0], []):
                        if (w or pw) and lo < r[2] and r[1] < hi:
                            d.add(j)
            for rs, w in ((reads, False), (writes, True)):
                for r in spans(rs):
                    lst = seen.setdefault(r[0], [])
                    if w and r[3]:
                        lst[:] = [a for a in lst if not (r[1] <= a[0] and a[1] <= r[2])]
                    lst.append((r[1], r[2], w, e, k))
            d.discard(k)
            if k in behind:
                d.add(behind[k])
            if k in sums and sums[k][1] in whole:
                deps[sums[k][1]] = deps.get(sums[k][1], set()) | set(j for j in d if sums.get(j, (0, -1))[1] != sums[k][1])
            deps[k] = deps.get(k, set()) | d
        for k in range(len(prog)):
            left.append(len(deps[k]))
            for j in deps[k]:
                users[j].append(k)
        ready = [k for k in range(len(prog)) if not left[k]]
        banks = [set(r[0] for r in spans(a[2] + a[3]) if r[0] in PSUM) for a in prog]
        held, used = {}, {}
        at, free, wire = [0.0] * len(prog), {e: 0.0 for e in Q}, {"G": 0.0, "Y": 0.0}
        while ready:
            can = {}
            for k in ready:
                if all(held.get(b, -1) in (-1, sums.get(k, (0, -2))[1]) for b in banks[k]):
                    since = max([at[k]] + [used[b][1] + HOP for b in banks[k] if b in used and used[b][0] != prog[k][0]])
                    can.setdefault(prog[k][0], []).append((prog[k][4], k, since))
            e = min(can, key=lambda q: max(free[q], min(c[2] for c in can[q])))
            now = max(free[e], min(c[2] for c in can[e]))
            pick = min(c for c in can[e] if c[2] <= now)
            pick = min(c for c in can[e] if c[2] <= now + max(PLOOK if e == "P" else LOOK, PART * prog[pick[1]][5]))
            best, start = pick[1], max(now, pick[2])
            free[e] = done = start + prog[best][5]
            if prog[best][6]:
                line = "G" if e == "G" else "Y"
                wire[line] = max(wire[line], start + 1500) + prog[best][6]
                done = wire[line] + (800 if e == "G" else 500)
            ready.remove(best)
            moment[:] = [start, done]
            for b in banks[best]:
                used[b] = (e, done)
            if best in sums:
                held[sums[best][0]] = -1 if sums[best][2] else sums[best][1]
            prog[best][1]()
            for k in users[best]:
                at[k] = max(at[k], free[e] if behind.get(k) == best else done + (0 if e == "P" == prog[k][0] else HOP))
                left[k] -= 1
                if not left[k]:
                    ready.append(k)

    def sc(x):
        return ap(x) if isinstance(x, tuple) else x

    def tt(out, a, b, o):
        op("V", lambda: g.vector.tensor_tensor(ap(out), ap(a), ap(b), o), out, [a, b])

    def ts(out, a, s1, o0, s2=None, o1=None):
        if o1 is None:
            op("V", lambda: g.vector.tensor_scalar(ap(out), ap(a), sc(s1), None, o0), out, [a, s1])
        else:
            op("V", lambda: g.vector.tensor_scalar(ap(out), ap(a), sc(s1), sc(s2), o0, o1), out, [a, s1, s2])

    def cp(out, a):
        op("V", lambda: g.vector.tensor_copy(ap(out), ap(a)), out, [a])

    def ms(out, v):
        op("V", lambda: g.vector.memset(ap(out), v), out, [])

    def act(out, a, func=AF.Copy, bias=None, scale=1.0, after=()):
        if bias is None:
            op("S", lambda: g.scalar.activation(ap(out), ap(a), func, scale=scale), out, [a] + list(after))
        else:
            op("S", lambda: g.scalar.activation(ap(out), ap(a), func, bias=ap(bias), scale=scale), out, [a, bias])

    def mm(out, w, x, start, stop, after=()):
        if start:
            first[out[0]] = len(prog)
            if out[2] == 32 and out != CNT:
                whole.add(len(prog))
        sums[len(prog)] = (out[0], first[out[0]], stop)
        op("P", lambda: g.tensor.matmul(ap(out), ap(w), ap(x), start, stop), out, [w, x] + list(after))

    def iota(out, pat, base, ch, small):
        if small:
            op("G", lambda: g.iota(ap(out), pat, base, ch, allow_small_or_imprecise_dtypes=True), out, [])
        else:
            op("G", lambda: g.iota(ap(out), pat, base, ch), out, [])

    def keep(out, a):
        op("G", lambda: g.affine_select(ap(out), ap(a), [[0, out[2]]], A.is_ge, 0.0, 0, 0), out, [a])

    def dma(e, out_ap, in_ap, reads, writes):
        def emit():
            order(e, reads, writes)
            s = "d%d" % ndma[0]
            ndma[0] += 1
            Q[e].dma_start(out_ap, in_ap).then_inc(T.sem[s], 16)
            note(e, "dma", reads, writes, (s, 16))
            ends.append((s, 16))
        r = (reads + writes)[0]
        put(e, emit, reads, writes, 60, r[2] * (2 if SCRATCH[r[0]][2] == "bfloat16" else 4) * 128 / RATE)

    def send(dst, srcs, sem, part=None):
        outs, ins = topo.engines(core, nxt), topo.engines(prv, core)
        if part is not None:
            outs, ins = outs[part * len(outs) // 2:(part + 1) * len(outs) // 2], ins[:len(ins) // 2]
        mask_out, n_out, n_in = sum(1 << e for e in outs), len(outs), len(ins)

        def emit():
            order("G", srcs, [])
            if len(srcs) == 1:
                g.remote_dma(ap(dst), ap(srcs[0]), T.sem[sem], T.sem["sent"], pid, rid, mask_out)
            else:
                g.remote_dma_fused([RemoteDMATransfer(dst_ids=[DstId(rid=rid, pnc=pid)], dma_engine_mask=mask_out, remote_sem=T.sem[sem],
                                                      srcs=[ap(r) for r in srcs], dsts=[ap(dst)], alu_op=1)], local_sem=T.sem["sent"])
            cnt["sent"] += n_out
            acc.setdefault(dst[0], []).append([dst[1][0][0], dst[1][-1][1], True, "rem", (sem, n_in), {}])
            ends.append((sem, n_in))
        put("G", emit, srcs, [dst], 400, 2.0 * dst[2])

    def col(i):
        return r2("COL", i, i + 1)

    def M(n):
        return r2(n, 0, 128)

    def ls(name, s=0, n=1):
        return r3(name, s, s + n, 1, 0, 32)

    def st(s, n=1):
        return ls("ST", s, n)

    def fl(i, s=0, n=2):
        return ls("E", 2 * (i % 2) + s, n)

    def wide(name, h, at=0):
        return r2(name, at + W * h, at + W * h + W)

    def block(name, j):
        return r2(name, K * j, K * j + K)

    def logged(i):
        return st(P0 + i % 2)

    FW, GW, XW, UW = r2("G", 0, FO), r2("G", 0, 2 * FO), r2("XF", 0, FO), r2("U", 0, FO)
    MU, SLOT = ls("MI", 1), r2("SLOT", 0, 32)
    PB = [r2("PB%d" % h, 0, W) for h in range(2)]
    CNT, UP = r2("L0", 0, 32), r2("L0", 32, 64)
    AT, LEN = ls("TP", 1), ls("TP", 2)
    BELOW, KEEP, CUR = [r2("Z0", W + 32 * s, W + 32 * s + 32) for s in range(3)]

    for q in range(2):
        dma("Y", T.PL[:, 128 * q:128 * q + 128], T.nx[0:128:16, 2048 * q:2048 * q + 2048], [], [r2("PL", 128 * q, 128 * q + 128)])
    dma("S", T.M0[:, :], T.m0[:, :], [], [r2("M0", 0, 32)])
    dma("Y", ap(r2("G", O, FO)), T.fm[:, :], [], [r2("G", O, FO)])
    dma("Y", T.B0[:, :], T.b0[:, :], [], [r2("B0", 0, K)])
    for a, b in zip(XCH[:-1], XCH[1:]):
        dma("Y", ap(r2("XI", a, b)), T.nx[:, a:b], [], [r2("XI", a, b)])
    dma("Y", ap(r2("WT", O, O + 2 * K)), T.wl[:, :], [], [r2("WT", O, O + 2 * K)])

    iota(r2("QI", 0, 1), [[0, 1]], 0, 1, False)
    iota(r2("J", 0, 144), [[1, 144]], 0, 0, True)
    iota(r2("PM", 0, 256), [[2048, 2], [1, 128]], 0, 128, False)
    iota(r2("BI", 0, 18), [[0, 9], [16, 2]], 0, 0, False)
    iota(r2("KI", 0, 32), [[16, 32]], 1, 0, False)
    iota(r2("SL", 0, 288), [[1, 9], [0, 32]], 1, 0, True)
    iota(r2("U", 0, UG), [[0, UG]], 0, 0, True)
    ms(col(12), -2047.0 / 128)
    ms(r2("G", 0, O), 0.0)
    ms(r2("G", FO, FO + O), 0.0)
    ms(r2("XF", 0, O), 0.0)
    ms(r2("WT", 0, O), 0.0)
    ms(col(9), -255.0)
    ms(col(10), 255.0)
    ms(col(11), 2047.0)
    ms(AT, 0.0)
    ms(r2("Z0", W, W + 96), 0.0)
    ms(LEN, 1.0)
    t(100)
    ts(r2("QI", 1, 2), r2("QI", 0, 1), 15, A.bitwise_and)
    for j, x in enumerate((0.5, 16384.0, 481.0, 0.0, 2048.0 + FO - 16384, 2048.0 + FO - 32768, 0.0)):
        ts(r2("KC", 32 * j, 32 * j + 32), r2("J", 0, 32), 0.0, A.mult, x, A.add)
    tt(col(1), r2("QI", 0, 1), r2("QI", 1, 2), A.subtract)
    cp(col(0), r2("QI", 1, 2))
    ms(st(TQ), 0.0)
    ts(M("TA"), M("J"), col(1), A.subtract)
    ts(col(3), col(0), 0.0, A.is_gt, 0.5, A.mult)
    ts(col(6), col(0), 15.0, A.is_equal, 0.5, A.mult)
    ts(col(2), col(1), 15.0, A.add)
    ts(M("ID"), M("TA"), col(0), A.is_equal)
    ts(M("TC"), M("TA"), col(0), A.is_gt)
    ts(M("TD"), M("TA"), 0.0, A.is_ge, 64.0, A.mult)
    ts(M("TF"), M("TA"), 15.0, A.is_le)
    ts(col(3), col(3), 0.5, A.add)
    ts(col(7), col(6), 2048.0, A.mult, 255.0, A.add)
    ts(col(5), col(6), -1.0, A.mult)
    ts(col(4), col(0), 0.0, A.mult, -1.0, A.add)
    ts(col(8), col(1), 128.0, A.mult)
    for name, times in (("NI", -1.0), ("KB", -2.0 ** 24), ("KD", 30720.0), ("IF", 1.0), ("KR", -16384.0), ("KP", 16384.0)):
        act(M(name), M("ID"), AF.Copy, None, times)
    tt(M("TD"), M("TD"), M("TF"), A.mult)
    act(M("TE"), M("ID"), AF.Identity, col(4), 16.0)
    act(M("TF"), M("TC"), AF.Copy, None, -14.0)
    tt(M("TC"), M("ID"), M("TC"), A.subtract)
    ts(r2("WB", 0, 144), r2("J", 0, 144), col(2), A.is_equal, col(3), A.mult)
    ts(r2("WY", 0, 144), r2("J", 0, 144), col(2), A.is_equal, 128.0, A.mult)
    act(M("TC"), M("TC"), AF.Identity, col(5))
    tt(M("TE"), M("TE"), M("TF"), A.add)
    ts(M("KF"), M("ID"), float(FO), A.mult)
    tt(M("ZD"), M("TC"), M("TD"), A.mult)
    tt(M("ZS"), M("TE"), M("TD"), A.mult)
    ts(r2("P16", 0, 256), r2("PL", 0, 256), float(O), A.add)
    ts(r2("LS", 0, 32), r2("M0", 0, 32), float(O), A.add)
    tt(r2("PA", 0, 256), r2("PL", 0, 256), r2("PM", 0, 256), A.subtract)
    cp(r2("L0I", 0, 32), r2("M0", 0, 32))
    ts(r2("PA", 0, 256), r2("PA", 0, 256), col(8), A.add)
    ts(MU, r2("M0", 0, 32), 1.0, A.add)
    ts(r2("PC", 0, 256), r2("PA", 0, 256), 6, A.arith_shift_right)
    ts(r2("PA", 0, 256), r2("PA", 0, 256), 63, A.bitwise_and)
    ms(st(NN), 1.0)
    ms(st(HH), 0.0)
    t(7350)
    ts(block("EX", 0), r2("B0", 0, K), -1.0, A.mult, 255.0, A.add)
    for h in range(2):
        mm(PB[h], M("NI"), wide("EX", h), True, True)
    t(10500)
    ms(r2("U", UG, FO), 0.0)
    ts(r2("HI", 0, 256), r2("PC", 0, 256), 128.0, A.mult)
    cp(r2("LO", 0, 256), r2("PA", 0, 256))
    ts(r2("BL", 0, 18), r2("BI", 0, 18), col(0), A.add)
    ts(st(KK), r2("KI", 0, 32), col(0), A.add)
    for q in range(2):
        a, b = O + 2048 * q, O + 2048 * q + 2048
        for row, name in enumerate(("HI", "LO")):
            dma("Y", T.U[row:128:16, a:b], T[name][:, 128 * q:128 * q + 128], [r2(name, 0, 256), UW], [r2("PM", 2 * q + row, 2 * q + row + 1)])
    for e, a, b, x in XAT:
        t(x)
        if e == "V":
            held_back.append(len(prog))
            cp(r2("XF", O + a, O + b), r2("XI", a, b))
        else:
            keep(r2("XF", O + a, O + b), r2("XI", a, b))

    for q, (e, x) in enumerate(FAT):
        t(x)
        (cp if e == "V" else act)(r2("FP", 1024 * q, 1024 * q + 1024), ind(FW, r2("P16", 64 * q, 64 * q + 64)))
    for k, (e, x) in enumerate(DAT):
        bk, q = ("L1", "LG")[k % 2], k // 4
        t(min(x - 600, 16500))
        for r in range(4):
            a = O + 512 * k + 128 * r
            mm(r2(bk, 128 * r, 128 * r + 128), M("NI"), r2("G", a, a + 128), True, False)
            mm(r2(bk, 128 * r, 128 * r + 128), M("ID"), r2("FP", 2048 * q + 4 * (k % 4) + r, 2048 * q + 2048, 16), False, True)
        t(x)
        (cp if e == "V" else act)(r2("G", FO + O + 512 * k, FO + O + 512 * k + 512), r2(bk, 0, K))

    def bc(win, n):
        return ind(win, r2("BL", 0, 2 * n))

    def onehot(H, n, terms, at_p, at_v):
        t(at_p)
        a = min(W, K - 32 * n)
        for j in range(n):
            for k, (w, x) in enumerate(terms):
                mm(r2("Z1", a + 32 * j, a + 32 + 32 * j), M(w), x, k == 0, k == len(terms) - 1)
        t(at_v)
        if H != "HC":
            held_back.append(len(prog))
        tt(r2(H, 0, 32 * n), r2("Z1", a, a + 32 * n), r2("SL", 0, 32 * n), A.is_equal)

    def look(H, n, at_v, at_p, back=None):
        t(at_v)
        tt(r2("PQ", 0, 32 * n), r2(H, 32, 32 * n + 32), r2("LG", 0, 32 * n), A.mult)
        t(at_p)
        mm(BELOW, M("ID"), r2("KC", 128, 160) if back else r2("KC", 96, 128), True, False)
        if back:
            mm(BELOW, M("KP"), back, False, False)
        for j in range(n):
            mm(BELOW, M("ID"), r2("PQ", 32 * j, 32 * j + 32), False, j == n - 1)

    def tolist(s0, s1, i):
        out = r2("L0", 32 * s0, 32 * s1)
        if "change" in mark:
            behind[len(prog)] = mark["change"]
        mm(out, M("ID"), r2("KC", 32 * s0, 32 * s1), True, False)
        if s1 == 2:
            mm(UP, M("KR"), fl(i, 0, 1), False, False)
        for r in range(16):
            mm(out, r2("WB", 15 - r, 143 - r), r3("RU", s0, s1, 1, r, K, 16), False, r == 15)

    def write(i, at):
        n, v = 32 * i, (i - 1) // S_
        t(at[1])
        mark["change"] = len(prog)
        if at[0] == 4000:
            held_back.append(len(prog))
        tt(st(DL), UP, st(J_ + i % 2), A.min)
        t(at[2])
        P = "PR" if i == S_ * V_ else "P"
        tt(r2(P, 0, n), bc(st(DL), i), r2("H%d" % (i % 2), 0, n), A.mult)
        t(at[3])
        if i == S_ * V_:
            tt(r2("OL", 0, n), r2(P, 0, n), r2("LG", 0, n), A.add)
            dma("Y", T.yl[:, :], T.OL[:, :], [r2("OL", 0, 288)], [])
        elif i == S_ * V_ - 1:
            t(1846)
            act(r2("LG", 0, 288), r2("LG", 0, 288), AF.Identity, col(11))
            t(3560)
            tt(r2("LG", 0, n), r2("P", 0, n), r2("LG", 0, n), A.add)
        elif i % S_:
            held_back.append(len(prog))
            tt(r2("LG", 0, n), r2("P", 0, n), r2("LG", 0, n), A.add)
        else:
            tt(r2("SL%d" % v, 0, n), r2("P", 0, n), r2("LG", 0, n), A.add)
            send(r2("RL%d" % v, 0, n), [r2("SL%d" % v, 0, n)], "l%d" % v)

    def step(i):
        s, v = (i - 1) % S_, (i - 1) // S_
        fresh, last, fin = i > 1 and s == 0, s == S_ - 1, i == S_ * V_
        hand = last and not fin
        owed = i > 2 and not fresh
        RA, SA, EX = "RA%d" % (v - 1), "SA%d" % v, block("EX", v)
        turn[0] = 5900 if i == 1 else 10000 * i
        if fresh:
            for h in range(2):
                t(100 + 420 * h)
                cp(wide("BW", h), ind(r2("WT", 0, O + 2 * K), r3(RA, 3, 4, 1, L * h, L * h + L)))
            for h in range(2):
                t(50)
                mm(PB[h], M("NI"), wide("RB%d" % (v - 1), h), True, False)
                t(50 + 350 * h)
                mm(PB[h], M("NI"), wide("RG%d" % (v - 1), h), False, False)
                t(60 + 420 * h)
                mm(PB[h], M("ID"), wide("BW", h), False, True)
            t(950)
            ts(st(TQ, 3), ls(RA, 0, 3), 1.0 - O, A.add)
            t(1300)
            ts(MU, ls(RA, 4), 1.0 - O, A.add)
            ts(r2("LT", 0, 32), ls(RA, 0), -float(FO), A.add)
            t(1400)
            act(st(HH), st(CU), AF.Sign)
            t(1950)
            mm(ls("TP", 1, 2), M("IF"), st(TQ, 2), True, True)
            mm(CUR, M("IF"), st(CU), True, True)
            t(3300)
            cp(r2("LG", 0, 96 * v), r2("RL%d" % (v - 1), 0, 96 * v))
        if hand:
            t(0)
            send(r2("RB%d" % v, 0, K), [EX, block("GA", i - 3), block("GA", i - 2)], "b%d" % v)
        lst = [r3(RA, 4, 5, 1, L * h, L * h + L) if fresh else r2("LS", L * h, L * h + L) for h in range(2)]
        late = 7400 if i == 1 else 0
        for h in range(2):
            t(380 * h)
            if h == 1 and "has" in mark:
                behind[mark.pop("has")] = len(prog)
            act(wide("F", h), ind(FW, lst[h]), AF.Identity, col(9))
            t(980 + 430 * h + late)
            if i > 1:
                act(wide("X", h), ind(XW, lst[h]), AF.Identity, col(12), 1.0 / 128)
            elif h == 0:
                ts(r2("X", 0, K), ind(r2("XI", 0, C), r2("L0I", 0, 32)), 1.0 / 128, A.mult, -2047.0 / 128, A.add)
        for h in range(2):
            Z, R1 = r2("L1", W, K) if h == 0 and i > 1 else r2("Z%d" % h, 0, W), r3("RU", 0, 1, 1, W * h, W * h + W)
            t((640, 1075)[h])
            tt(R1, wide("F", h), PB[h], A.is_gt)
            t((1180, 1300)[h])
            if h == 1 and i > 1:
                t(976)
                act(wide("F2", h), wide("F", h), AF.Identity, col(7), 2.0)
            else:
                ts(wide("F2", h), wide("F", h), 2.0, A.mult, col(7), A.add)
            t((1310, 1710)[h])
            tt(wide("D", h), wide("F2", h), PB[h], A.is_gt)
            t((1000, 2010)[h])
            mm(Z, M("ZS"), R1, True, False)
            t((1900, 2130)[h])
            mm(Z, M("ZD"), wide("D", h), False, True)
            t((2100, 2628 if hand else 2400)[h] + late)
            if h == 0:
                mark["y0"] = len(prog)
            tt(wide("Y", h), wide("X", h), Z, A.min)
        t(1840)
        if fresh:
            for h in range(2):
                act(wide("EX", h, K * v), PB[h], AF.Relu, None, -1.0)
        t(1410)
        tolist(0, 2 if owed else 1, i - 1)
        if i > 1:
            t(3500 if hand else 1850)
            mark["partner"] = len(prog)
            act(r3("RU", 1, 2, 1, 0, K), ind(UW, r2("LT", 0, 32)), after=[r2("PM", 0, 4)])
        t(1990)
        tt(fl(i, 0, 1), CNT, st(HH), A.is_equal)
        ts(fl(i, 1, 1), CNT, 0.5, A.is_equal)
        t(2600 if hand else 2300)
        tt(st(PB_, 2), ls("TP", 1, 2), fl(i), A.mult)
        tt(logged(i), fl(i, 1, 1), MU, A.mult)
        t(2600)
        tt(st(J_ + i % 2), st(PB_), logged(i), A.max)
        t(2625)
        tt(SLOT, CUR, st(QQ), A.max)
        t(2620)
        ts(r2("LJ", 0, 32), st(J_ + i % 2), O - 1.0, A.add)
        t(3900 if i == 1 else 2650)
        if last:
            for h in range(2):
                act(wide("GA", h, K * (i - 1)), ind(GW, r2("LJ", L * h, L * h + L)))
                if hand:
                    mark["second"] = len(prog)
                    behind[mark["partner"]] = len(prog) - 1
                    send(wide("RG%d" % v, h), [wide("GA", h, K * (i - 1))], "gh"[h] + "%d" % v)
        else:
            act(block("GA", i - 1), ind(GW if i > 1 else FW, r2("LJ", 0, 32)))
        t(2690)
        tt(st(MB), fl(i, 0, 1), MU, A.mult)
        if hand:
            one, two, same = [r2("LG", 320 + 32 * j, 352 + 32 * j) for j in range(3)]
            terms = [(one, "KR", fl(i - 1, 0, 1)), (two, "KP", fl(i - 1, 0, 1))]
            terms += [(one, "ID", r2("PQ", 32 * j, 32 * j + 32)) for j in range(i - 2)]
            terms += [(two, "ID", r2("PQ", 128 + 32 * j, 160 + 32 * j)) for j in range(i - 3)]
            t(600)
            mm(r2("LG", 320, 416), M("ID"), r2("KC", 128, 224), True, False, [r2("PQ", 0, 256)])
            for out, w, x in terms:
                mm(out, M(w), x, False, False)
            t(1905)
            for out, w, x in ((same, "IF", st(TQ)), (one, "KP", fl(i, 0, 1)), (two, "KP", fl(i, 0, 1)), (same, "KR", fl(i, 0, 1))):
                mm(out, M(w), x, False, False)
            mm(same, M("KR"), fl(i, 1, 1), False, True)
            t(2610)
            ts(st(U1, 3), r2("LG", 320, 416), 0.0, A.max)
        elif not fin:
            t(2810)
            mm(KEEP, M("IF"), st(TQ), True, False)
            mm(KEEP, M("KR"), fl(i, 0, 1), False, False)
            mm(KEEP, M("KR"), fl(i, 1, 1), False, True)
        t(2640 if hand else 2800)
        mm(CUR, M("ID"), SLOT, True, False)
        mm(CUR, M("NI"), fl(i, 0, 1), False, True)
        if fin:
            t(4100)
            ts(r2("OC", 0, 32), CUR, -1.0, A.add)
            dma("Y", T.yc[:, :], T.OC[:, :], [r2("OC", 0, 32)], [])
        elif not hand:
            t(10975 if i > 1 else 4800)
            if i > 1:
                mark["has"] = len(prog)
            act(st(HH), CUR, AF.Sign)
        if i == 1:
            t(16900)
            ms(r2("LG", 32, 288), -2048.0)
            ts(r2("LG", 0, 32), logged(i), -2048.0, A.add)
        if owed and i != 8:
            write(i - 1, (4000, 4100, 4200, 4300) if hand else (2626, 2490, 3050, 3400))
        if i > 1:
            onehot("H%d" % (i % 2), i, [("ID", SLOT)], 3850 if hand else 2331 if fin else 3260, 4250 if hand else 3055 if fin else 3550)
        if not last and i > 1:
            look("H%d" % (i % 2), i - 1, 3700, 3900, fl(i, 0, 1))
        if i == 8:
            write(i - 1, (2626, 2490, 3050, 11696))
        VP = r2("L1", 0, 32) if i > 1 else r2("L0", 64, 96)
        t(2200 + late)
        mm(VP, M("KD"), r2("KC", 64, 96), True, False)
        whole.discard(len(prog) - 1)
        behind[len(prog) - 1] = mark["y0"]
        mm(VP, M("KB"), fl(i, 0, 1), False, False)
        t(2750 + late)
        for r in range(16):
            mark["named"] = len(prog)
            mm(VP, r2("WY", 15 - r, 143 - r), r2("Y", r, K, 16), False, r == 15)
        late += 700 if fin else 0
        t((2632 if hand else 3410) + late)
        if i == 1:
            mark["change"] = len(prog)
        tt(ls("MI", 4), VP, st(MB), A.max)
        t((2633 if hand else 3500) + late)
        ts(MU, ls("MI", 4), 8191, A.bitwise_and)
        t((2634 if hand else 3650) + late)
        while held_back:
            k = held_back.pop()
            if not fin:
                behind[k] = len(prog)
        if fin:
            ts(r2("OM", 0, 32), MU, -1.0, A.add)
            dma("S", T.ym[:, :], T.OM[:, :], [r2("OM", 0, 32)], [])
        elif not hand:
            ts(r2("LS", 0, 32), MU, O - 1.0, A.add)
        if not hand:
            for h in range(2):
                t(2320)
                mm(PB[h], M("NI"), wide("EX", h, K * v), True, False)
                for j in range(s + 1):
                    t((2690 if j == s else 2330) if fin else 4480 if j == s else 3270)
                    if j < s and not fin:
                        behind[len(prog)] = mark["named"]
                    mm(PB[h], M("NI"), wide("GA", h, K * (i - 1 - s + j)), False, j == s)
        if fin:
            for h in range(2):
                t((3100, 3470)[h])
                act(wide("OB", h), PB[h], AF.Identity, col(10))
                dma("S", T.yb[:, W * h:W * h + W], ap(wide("OB", h)), [wide("OB", h)], [])
            t(2332)
            tolist(1, 2, i)
            write(i, (3060, 3070, 3800, 3900))
            return
        if not hand:
            t(UT if i > 1 else 4000)
            act(st(U1, 2), r2("Z0", W, W + 64), AF.Relu)
        t(2140 if hand else 3280)
        if not hand and i > 1:
            behind[len(prog)] = mark["named"]
        mm(ls("TP", 1, 2), M("IF"), r3("ST", P0 + i % 2, NN + 1, NN - P0 - i % 2, 0, 32), True, False)
        mm(LEN, M("ID"), fl(i, 1, 1), False, False)
        mm(AT, M("KF"), fl(i, 1, 1), False, False)
        t(2150 if hand else 11300 if i > 1 else 4090)
        if hand:
            mm(AT, M("IF"), st(U0 + 1), False, False)
        mm(AT, M("IF"), st(U0), False, False)
        mm(AT, M("IF"), st(U1), False, True)
        if not hand:
            t(11305 if i > 1 else 4700)
            ts(r2("LT", 0, 32), AT, O - 1.0 - FO, A.add)
            ahead = s == S_ - 2 and v < V_ - 1
            t(11400 if ahead else 11845 if i > 1 else 4810)
            act(st(TQ, 2), ls("TP", 1, 2))
            if ahead and i > 2:
                t(3710)
                tt(r2("PQ", 128, 128 + 32 * (i - 2)), r2("H%d" % (i % 2), 64, 32 * i), r2("LG", 0, 32 * (i - 2)), A.mult)
            return
        t(HT[0])
        ts(ls("MI", 2), AT, 1.0, A.add, float(K) if v == 0 else 1.0, A.mult)
        t(HT[1])
        ts(ls("MI", 3), ls("MI", 2), K if v == 0 else 1, A.bitwise_and)
        t(HT[2])
        ts(st(HH), CUR, 0.0, A.is_equal, -4096.0, A.mult)
        tt(st(WX), st(HH), st(KK), A.add)
        if v > 0:
            t(HT[3])
            tt(st(CU), ls("MI", 3), st(WP), A.mult)
        t(HT[4])
        tt(ls("MI"), st(WX), ls("MI", 3) if v == 0 else st(CU), A.add)
        t(HT[5])
        ts(ls(SA, 0, 2), ls("TP", 1, 2), O - 1.0, A.add)
        ts(ls(SA, 2), CUR, O - 1.0, A.add)
        ts(ls(SA, 3, 2), ls("MI", 0, 2), O - 1.0, A.add)
        t(3810)
        behind[mark["second"]] = len(prog)
        send(ls("RA%d" % v, 0, 5), [ls(SA, 0, 5)], "a%d" % v)
        if v == 0:
            t(5000)
            tt(st(WX), ls("MI"), st(KK), A.subtract)
            ts(st(WL), st(WX), 0.0, A.is_equal, -4096.0, A.mult)
            ts(st(WX), st(WX), float(K), A.is_equal, -4096.0, A.mult)
            tt(st(KK), st(KK), st(WL), A.add)
            tt(st(WX), st(WX), st(WL), A.subtract)
            ts(st(WP), st(WX), float(K), A.add)
        t(4400)
        tolist(1, 2, i)
        write(i, (4500, 4600, 4700, 4800))

    for i in range(1, S_ * V_ + 1):
        step(i)

    arrange()
    for s in ("eV", "eS", "eP", "eG", "sent"):
        g.wait_ge(T.sem[s], cnt[s])
    for s, val in ends:
        g.wait_ge(T.sem[s], val)
